import numpy as np, ml_dtypes
CORES = [16,18,20,22]
N = 4
import mx_ref
BF = ml_dtypes.bfloat16
def gentries(a):
    return np.ascontiguousarray(a.reshape(8, 16, -1).transpose(0, 2, 1)).reshape(8, -1)
def gtable(e):
    e = np.asarray(e); return np.ascontiguousarray(e.reshape(8, -1, 16).transpose(0, 2, 1)).reshape(128, -1).astype(np.int32)
def cols(t, e):
    v = np.concatenate([t.reshape(128, -1, 4), np.zeros((128, 1, 4), BF)], axis=1)
    return np.ascontiguousarray(v[:, e]).reshape(128, -1)
def gcols(t, e):
    v = np.concatenate([t.reshape(8, 16, -1, 4), np.zeros((8, 16, 1, 4), BF)], axis=2)
    return np.ascontiguousarray(np.stack([v[g][:, e[g]] for g in range(8)])).reshape(128, -1)
def tile(rs):
    return np.stack(rs, axis=2).reshape(128, -1).astype(BF)
def cut(t, i, w=512):
    return t[:, w * i:w * i + w]
def pick(q, e):
    c = np.concatenate([q[0].reshape(128, -1, 4), np.zeros((128, 1, 4), np.uint8)], axis=1); s = np.concatenate([q[1], np.ones((16, 1), np.uint8)], axis=1)
    return (np.ascontiguousarray(c[:, e].reshape(128, -1)), np.ascontiguousarray(s[:, e]))
def join(*qs):
    return (np.concatenate([q[0] for q in qs], axis=1), np.concatenate([q[1] for q in qs], axis=1))
def put(q, e, v):
    c, s = q[0].reshape(128, -1, 4).copy(), q[1].copy(); c[:, e] = v[0].reshape(128, -1, 4); s[:, e] = v[1]
    return (c.reshape(128, -1), s)
def pk(c, s):
    return (np.ascontiguousarray(c), mx_ref.live(s))
def emit(q):
    return q[0], q[1]
def packed(v, rng):
    q = [mx_ref.quantize(np.ascontiguousarray(v[r])) for r in range(N)]
    return np.stack([a for a, b in q]), np.stack([mx_ref.plane(b, rng) for a, b in q])
def values_of_codes():
    e, c = np.zeros((128, 128, 4), np.float32), np.zeros((128, 2, 4), np.uint8)
    e[np.arange(128), np.arange(128), 0] = 1
    c[:127, :, 0] = np.arange(256).reshape(2, 128).T[:127]
    return mx_ref.matmul(mx_ref.quantize(e.reshape(128, 512).astype(BF)), (c.reshape(128, 8), np.full((16, 2), 127, np.uint8))).T.reshape(-1).astype(np.float64)
CODE_VALUE, SCALE_VALUE = values_of_codes(), 2.0 ** (np.arange(256) - 127.0)
def decode(q):
    return (CODE_VALUE[q[0]].reshape(16, 8, -1, 4) * SCALE_VALUE[q[1]][:, None, :, None] + 0.0).reshape(128, -1).astype(np.float32)
def f(rng, *shape):
    return mx_ref.flush((rng.standard_normal(shape, dtype=np.float32) * np.exp2(rng.integers(-2, 3, shape[:-1] + (1,)))).astype(BF))
def wide(rng, *shape, cols=0):
    v = rng.standard_normal(shape, dtype=np.float32) * np.exp2(rng.integers(-12, 13, shape)).astype(np.float32)
    if cols: v *= np.repeat(np.exp2(rng.integers(-cols, cols + 1, shape[:-2] + (1, shape[-1] // 4))) * (rng.random(shape[:-2] + (1, shape[-1] // 4)) > 0.0625), 4, axis=-1).astype(np.float32)
    return mx_ref.flush(v.astype(BF))
MC, P, A, K, R = 896, 384, 224, 32, 3
def numbers_of(rng):
    return {"m": np.array(f(rng, N, 128, 4 * MC)), "x": np.array(f(rng, N, 128, 4 * P)), "u": np.array(f(rng, N, 128, 512)), "v": np.array(f(rng, N, 128, 512))}
def weights(rng, w):
    c, p = packed(w, rng)
    return {"wc": c, "ws": p}
def still(rng):
    w = np.zeros((N, 128, 4, 128, 4), np.float32)
    i = np.arange(128)
    for b in range(4): w[:, i, b, i, b] = 32
    return weights(rng, w.reshape(N, 128, 2048).astype(BF))
def signs(rng):
    return np.stack([rng.permutation(8) % 2 * 2.0 - 1.0 for r in range(N)])
def mixed(rng, t):
    n = rng.integers(0, 2 * K + 1, (R, 8))
    n[0] = rng.permutation(np.concatenate([[0, K - 1, K, K + 1, 2 * K], n[0, :3]]))
    o = []
    for g in range(8):
        known = t[g]
        for i in range(R):
            new = np.setdiff1d(np.arange(MC), known)
            e = rng.permutation(np.concatenate([rng.choice(known, A - n[i, g], replace=False), rng.choice(new, n[i, g], replace=False)]))
            o.append(e)
            known = np.union1d(known, e)
    return np.stack(o).reshape(8, R * A)
def exact(rng, t, n):
    o, sure, out = [], t, np.setdiff1d(np.arange(MC), t)
    for i in range(R):
        e = rng.permutation(np.concatenate([rng.choice(sure, A - n, replace=False), rng.choice(out, n, replace=False)]))
        miss = np.isin(e, out)
        served = e[miss][:K]
        sure = np.concatenate([e[~miss], served])
        out = np.setdiff1d(out, served)
        o.append(e)
    return np.concatenate(o)
def draw_tags(rng):
    return np.stack([np.stack([rng.permutation(MC)[:P] for g in range(8)]) for r in range(N)])
def lists_of(rng):
    t = draw_tags(rng)
    return {"tg": np.stack([gtable(t[r]) for r in range(N)]), "ad": np.stack([gtable(mixed(rng, t[r])) for r in range(N)])}
def held(l, r):
    t, a = gentries(l["tg"][r]), gentries(l["ad"][r])[:, :A]
    return np.stack([np.isin(t[g], a[g]) for g in range(8)])
def fine(rng, v, s):
    v = v.astype(np.float32).reshape(N, 8, 16, -1, 4)
    g = ((s[..., None] >> np.arange(8)) & 1) * np.exp2(np.arange(8) - 23.0)
    v[:, :, 0] = 0
    v[:, :, 0, :, 0] = 1
    v[:, :, 8] = g[..., :4]
    v[:, :, 9] = g[..., 4:]
    a = v[:, :, 10:].shape
    v[:, :, 10:] = rng.integers(4, 8, a) * rng.choice([-1.0, 1.0], a) * 2.0 ** -20
    return v.reshape(N, 128, -1).astype(BF)
def setup_inputs(rng):
    return {**numbers_of(rng), **weights(rng, f(rng, N, 128, 2048)), **lists_of(rng)}
def setup_inputs_full(rng):
    d = {**numbers_of(rng), **weights(rng, f(rng, N, 128, 2048))}
    t = draw_tags(rng)
    e = rng.permutation(N)
    ad = []
    for r in range(N):
        kind = rng.permutation(8)
        o = []
        for g in range(8):
            if r == e[0]: o.append(exact(rng, t[r, g], A))
            elif r == e[1]: o.append(exact(rng, t[r, g], 0))
            elif kind[g] < 6: o.append(exact(rng, t[r, g], [0, 1, K - 1, K, K + 1, A][kind[g]]))
            elif kind[g] == 6: o.append(rng.permutation(MC)[:R * A])
            else: o.append(np.concatenate([rng.choice(np.setdiff1d(np.arange(MC), t[r, g]), A, replace=False)] + [rng.choice(t[r, g], A, replace=False) for i in range(R - 1)]))
        ad.append(gtable(np.stack(o)))
    return {**d, "tg": np.stack([gtable(t[r]) for r in range(N)]), "ad": np.stack(ad)}
def setup_inputs_ties(rng):
    d = setup_inputs(rng)
    e = rng.permutation(N)
    for r in range(N):
        k = np.zeros(P, int) if r == e[0] else rng.permutation(P) % 3
        d["x"][r] = cols(d["x"][r], np.where(k == 2, -1, k))
    o = (e[0] + 1) % N
    d["m"][o] = cols(d["m"][o], np.zeros(MC, int))
    d["x"][e[1]] = 0
    return d
def setup_inputs_near(rng):
    d = numbers_of(rng)
    l = lists_of(rng)
    g = signs(rng)
    down = (P - 1 - np.arange(P)) // 2
    s = np.tile(down, (N, 8, 1))
    r = int(rng.integers(N))
    hit = held(l, r)
    for i in range(8): s[r, i, np.argsort(hit[i], kind="stable")] = down
    u = d["u"].reshape(N, 128, 128, 4)
    u[:, :, ::16] = 0
    for h in range(0, 128, 16):
        u[:, h, h, 0] = g[:, h // 16].astype(BF)
        u[:, h + 8:h + 10, h] = 1
    return {"m": fine(rng, d["m"], rng.integers(0, P // 2, (N, 8, MC))), "x": fine(rng, d["x"], s), "u": u.reshape(N, 128, 512), "v": d["v"], **still(rng), **l}
def setup_inputs_huge(rng):
    d = numbers_of(rng)
    l = lists_of(rng)
    g = signs(rng)
    m = 2.0 ** 30 * (0.6 + 0.4 * rng.random((N, 128, 4 * MC), dtype=np.float32))
    x = 2.0 ** 30 * (0.6 + 0.4 * rng.random((N, 128, 4 * P), dtype=np.float32))
    a = 2.0 ** 30 * (1 - 0.25 * rng.random((N, 128, 8, 4)))
    c = np.stack([rng.permutation(P) % 2 * 2.0 - 1.0 for r in range(N)])
    e = rng.permutation(N)
    c[e[:N // 2]] = 1
    r = e[-1]
    hit = held(l, r)
    k = int(np.argmax(np.sum(hit, axis=1) == A - K))
    c[r] = np.where(hit[k], -g[r, k], g[r, k])
    x[r] = 2.0 ** 30
    a[r] = 2.0 ** 30
    x = x * np.repeat(c, 4, axis=1)[:, None, :]
    u = d["u"].reshape(N, 128, 128, 4)
    a = a * g[:, None, :, None]
    u[:, :, ::16] = a.astype(np.float32).astype(BF)
    return {"m": m.astype(np.float32).astype(BF), "x": x.astype(np.float32).astype(BF), "u": u.reshape(N, 128, 512), "v": d["v"], **still(rng), **l}
def setup_inputs_spread(rng):
    d = setup_inputs(rng)
    d["m"] = np.array(wide(rng, N, 128, 4 * MC, cols=6))
    d["x"] = np.array(wide(rng, N, 128, 4 * P, cols=6))
    r = int(rng.integers(N))
    t, a = gentries(d["tg"][r]), gentries(d["ad"][r])[:, :A]
    g = int(np.argmax([np.sum(~np.isin(a[i], t[i])) for i in range(8)]))
    size = np.full(P, 2.0 ** -24)
    size[rng.choice(np.flatnonzero(~np.isin(t[g], a[g])), 16, replace=False)] = 2.0 ** 20
    v = f(rng, 128, 4 * P).astype(np.float32) * np.repeat(size, 4).astype(np.float32)
    d["x"][r] = mx_ref.flush(v.astype(BF))
    return d
def check_inputs(d):
    b = []
    for k in ("m", "x", "u", "v"):
        a = np.abs(d[k].astype(np.float32))
        if not (np.isfinite(a).all() and ((a == 0) | (a >= 2.0 ** -30) & (a <= 2.0 ** 30)).all()): b.append("a value of " + k)
    t = np.stack([gentries(a) for a in d["tg"]])
    if (t < 0).any() or (t >= MC).any(): b.append("a tag out of range")
    if (np.diff(np.sort(t, axis=-1), axis=-1) == 0).any(): b.append("a tag twice in a cache")
    a = np.stack([gentries(a) for a in d["ad"]]).reshape(N, 8, R, A)
    if (a < 0).any() or (a >= MC).any(): b.append("an address out of range")
    if (np.diff(np.sort(a, axis=-1), axis=-1) == 0).any(): b.append("an address twice in a round of a cache")
    return b
def reference(m, x, u, v, wc, ws, tg, ad):
    qu = [mx_ref.quantize(u[r]) for r in range(N)]
    lay = [pk(wc[r], ws[r]) for r in range(N)]
    now = [x[r] for r in range(N)]
    tags = [np.array(gentries(tg[r])) for r in range(N)]
    acc = [gentries(ad[r]).reshape(8, R, A) for r in range(N)]
    for t in range(R):
        source, target, fetched = [], [], []
        for r in range(N):
            marks = mx_ref.matmul(qu[r], mx_ref.quantize(now[r]))[::16] + np.float32(0.0)
            ask = np.full((8, K), -1)
            src = np.full((8, A), -1)
            dst = np.full((8, A), -1)
            for g in range(8):
                want = acc[r][g, t]
                at = np.full(MC, -1)
                at[tags[r][g]] = np.arange(P)
                place = at[want]
                miss = np.flatnonzero(place < 0)[:K]
                n = len(miss)
                order = np.argsort(marks[g], kind="stable")
                victims = order[~np.isin(order, place)][:n]
                ask[g, :n] = want[miss]
                src[g] = place
                src[g, miss] = P + np.arange(n)
                dst[g] = place
                dst[g, miss] = victims
                tags[r][g, victims] = want[miss]
            source.append(src)
            target.append(dst)
            fetched.append(mx_ref.quantize(gcols(m[(r + 1) % N], ask)))
        came = decode(join(*fetched)).astype(BF)
        for r in range(N):
            z = mx_ref.quantize(gcols(np.concatenate([now[r], cut(came, r, 4 * K)], axis=1), source[r]))
            h = tile([np.maximum(mx_ref.matmul(pick(lay[r], np.arange(128 * b, 128 * b + 128)), z), np.float32(0.0)) * np.float32(0.03125) for b in range(4)])
            e = np.tile(np.arange(P), (8, 1))
            g, j = np.nonzero(target[r] >= 0)
            e[g, target[r][g, j]] = P + j
            now[r] = gcols(np.concatenate([now[r], h], axis=1), e)
    y, ot = np.zeros((N, 128, P), np.float32), np.zeros((N, 8, P), np.float32)
    oc, osc = np.zeros((N, 128, 4 * P), np.uint8), np.zeros((N, 16, P), np.uint8)
    for r in range(N):
        q = mx_ref.quantize(now[r])
        y[r] = mx_ref.matmul(mx_ref.quantize(v[r]), q)
        ot[r] = tags[r]
        oc[r], osc[r] = emit(q)
    return {"y": y, "ot": ot, "oc": oc, "osc": osc}

@@ -1,0 +1,597 @@
+from concourse.mybir import dt, AluOpType as Op, AxisListType, ActivationFunctionType as Fn
+
+MC, P, A, K = 896, 384, 224, 32
+OFF = 1920
+THR = 1916.0
+MISS = 73728
+HB = (480, 480, 644)
+ZC = (448, 448, 640)
+NS = (2, 2, 2)
+N2 = (0, 0, 0)
+RD = RL = WR = ("SSSS", "SSSS", "SSSS")
+MISS_ON = "VSV"
+f32, bf, i32, u16, u8, x4 = "float32", "bfloat16", "int32", "uint16", "uint8", "float8_e4m3fn_x4"
+
+
+def _s(n, d):
+    return ("sbuf", [128, n], d)
+
+
+SCRATCH = {
+    "tgi": _s(24, i32), "adi": _s(42, i32), "tgu": _s(24, u16), "adu": _s(42, u16),
+    "ms": _s(4 * (MC + 2 * K), bf), "us": _s(512, bf), "vs": _s(512, bf),
+    "wq": _s(512, x4), "wp": _s(512, u8),
+    "w0": _s(4 * 704, bf), "w1": _s(4 * 704, bf), "w2": _s(4 * 868, bf), "w3": _s(4 * 416, bf),
+    "uq": _s(128, x4), "up": _s(128, u8), "uq2": _s(128, x4), "up2": _s(128, u8),
+    "vq": _s(128, x4), "vp": _s(128, u8),
+    "xq": _s(P, x4), "xp": _s(P, u8), "zt": _s(3 * 4 * A, bf), "zq": _s(3 * A, x4), "zp": _s(3 * A, u8),
+    "eq": _s(512, x4), "ep": _s(512, u8), "ey": _s(516, bf), "ones": _s(516, bf),
+    "ft": _s(4 * A, bf), "fq2": _s(A, x4), "fp2": _s(A, u8), "fq0": _s(160, x4), "fp0": _s(160, u8),
+    "fq1": _s(160, x4), "fp1": _s(160, u8), "lc": _s(A, x4), "lp": _s(A, u8),
+    "rq2": _s(14, i32), "rq0": _s(8, u16), "rq1": _s(8, u16), "f2l": _s(56, u16),
+    "sa0": _s(16, u16), "sa1": _s(16, u16),
+    "iot": _s(MC, f32), "tb": _s(MC, f32), "at": _s(OFF + MC, f32), "sl": _s(416, f32),
+    "jc0": _s(A, f32), "jc2": _s(A, f32), "j2": _s(A, f32), "val": _s(3 * A, f32),
+    "e0": _s(640, f32), "e1": _s(640, f32), "e2": _s(640, f32),
+    "tags": _s(416, f32), "otb": _s(P, f32), "yb": _s(P, f32),
+    "ci": _s(16, i32), "cf": _s(40, f32), "ir": _s(96, f32), "pk": _s(40, u16), "pkp": _s(24, u16),
+    "uu": _s(96, f32), "ut": _s(96, f32), "g3": _s(128, f32), "seg1": _s(1024, bf), "seg2": _s(612, bf),
+    "ta": _s(480, f32), "tp": _s(288, f32), "t1": _s(288, f32), "t2": _s(224, f32), "tk": _s(96, f32), "tv": _s(96, f32), "te": _s(96, f32),
+    "mis": _s(A, f32), "qq": _s(A, f32), "alt": _s(A, f32), "src": _s(256, f32),
+    "lz": _s(240, u16), "lk": _s(96, u16), "le": _s(288, u16), "lv": _s(48, u16),
+    "pen": _s(3 * 416, bf), "kk": _s(P, f32), "m1": _s(128, f32), "mb": _s(160, f32), "ky": _s(16, f32),
+    "c1": _s(612, bf), "s1": _s(612, bf), "cn": _s(8, f32), "lt": _s(8, u16), "rw": _s(8 * 128, bf),
+    "jn1": _s(1024, bf), "jn2": _s(1024, bf),
+    "sm": _s(8, f32), "o6": _s(8, u16), "cb": _s(128, f32), "dl": _s(96, f32), "dk": _s(8, f32), "gb": _s(120, f32),
+    "cp": _s(96, f32), "rk": _s(8, u16), "sv": _s(96, f32), "dr": _s(96, f32), "vb": _s(80, f32), "eb": _s(64, f32),
+    "hs": _s(3 * 128, bf),
+    "ps": ("psum", [128, 4096], f32),
+}
+DMAS = ["tg", "ad", "x", "u", "m", "wc", "ws", "v", "oy", "oz", "oc", "os", "ot", "p0", "p1", "p2"]
+SEMAPHORES = ["cV", "cS", "cT", "cG", "sent", "a_rq2", "a_rq0", "a_rq1", "a_f2", "a_f0", "a_f1"] + ["d_" + n for n in DMAS]
+CYC, FIX, GAT, SCA, SAME, CROSS, FLY, BW = 1.04e-3, 0.06, 1.56, 3.8, 0.05, 0.15, 2.0, 190e3
+SEED, ITER, TEMP = 11, 11000, 0.5
+PLAN = {}
+
+
+def overlap(a, b):
+    if a[0] != b[0] or a[2] <= b[1] or b[2] <= a[1]:
+        return False
+    return not (a[3] == b[3] > 1 and (a[1] - b[1]) % a[3])
+
+
+def schedule(nodes):
+    every = range(len(nodes))
+    cost = [nd["cost"] for nd in nodes]
+    queue = [nd["q"] for nd in nodes]
+    group = [nd["st"] + nd["q"] for nd in nodes]
+
+    def gap(d, k):
+        if nodes[k]["soft"] == d:
+            return 0.0
+        return nodes[d]["lat"] + (SAME if queue[d] == queue[k] else 0.0 if queue[k] == "R" else CROSS)
+
+    pre = [[(d, gap(d, k)) for d in sorted(nodes[k]["deps"])] for k in every]
+    post = [[] for _ in every]
+    for k in every:
+        for d, w in pre[k]:
+            post[d].append((k, w))
+
+    def plan(bias):
+        way = [0.0] * len(nodes)
+        for k in reversed(every):
+            way[k] = cost[k] + 1e-6 + bias.get(group[k], 0.0) + max([way[u] + w for u, w in post[k]] + [nodes[k]["lat"]])
+        start, slots, span = [0.0] * len(nodes), {}, 0.0
+        for k in sorted(every, key=lambda j: (-way[j], j)):
+            t0 = max([start[d] + cost[d] + w for d, w in pre[k]] + [0.0])
+            sl = slots.setdefault(queue[k], [])
+            i = 0
+            for a, b in sl:
+                if b > t0:
+                    if t0 + cost[k] <= a:
+                        break
+                    t0 = b
+                i += 1
+            sl.insert(i, (t0, t0 + cost[k]))
+            start[k] = t0
+            span = max(span, t0 + cost[k] + nodes[k]["lat"])
+        return span, sorted(every, key=lambda j: (start[j], j))
+
+    seed = [SEED]
+
+    def rnd(n):
+        seed[0] = (seed[0] * 1103515245 + 12345) % 2147483648
+        return (seed[0] >> 9) % n
+
+    names = sorted(set(group))
+    best = {}
+    span, order = top = plan(best)
+    for it in range(ITER):
+        b = dict(best)
+        for _ in range(1 + rnd(3)):
+            nm = names[rnd(len(names))]
+            b[nm] = max(0.0, b.get(nm, 0.0) + (rnd(2001) / 1000.0 - 1.0) * (0.1, 0.5, 2.0, 6.0)[rnd(4)])
+        sp, od = plan(b)
+        if sp <= span + TEMP * (1 - it / ITER) * rnd(1000) / 1000.0:
+            best, span = b, sp
+            if sp < top[0]:
+                top = (sp, od)
+    return top
+
+
+def rank_program(g, core, T, topo):
+    rank = T.rank_of(core)
+    if rank is None:
+        return
+    n = len(T.cores)
+    owner, asker = T.cores[(rank + 1) % n], T.cores[(rank - 1) % n]
+    Q = {"V": g.vector, "S": g.scalar, "T": g.tensor, "G": g, "Y": g.sync}
+    nodes, hist, stage, busy, chain = [], {}, [""], [0.5], []
+
+    def v(name, lo=0, hi=None, step=1):
+        hi = SCRATCH[name][1][1] if hi is None else hi
+        ap = T[name][:, lo:hi] if step == 1 else T[name][:, lo:hi:step]
+        cnt = (hi - lo + step - 1) // step
+        wide = 2 if SCRATCH[name][2] in (bf, u16) else 4
+        if name == "ps":
+            return (ap, [(name, lo // 512 * 512, (hi + 511) // 512 * 512, 1)], cnt, wide, 0)
+        return (ap, [(name, lo, hi, step)], cnt, wide, 0)
+
+    def ind(win, off):
+        return (win[0].indirect(off[0]), win[1] + off[1], 16 * off[2], win[3], 1)
+
+    def w32(x):
+        return (x[0].bitcast(dt.uint32),) + x[1:]
+
+    def b8(x):
+        return (x[0].bitcast(dt.uint8),) + x[1:]
+
+    def node(q, kind, run, wr, rd, cost, lat=0.0, after=(), tag=0, soft=None):
+        deps = set(after)
+        for regs, w in ((wr, True), (rd, False)):
+            for r in regs:
+                for r2, w2, k in hist.get(r[0], []):
+                    if (w or w2 or r[0] == "ps") and overlap(r, r2):
+                        deps.add(k)
+        me = len(nodes)
+        nodes.append(dict(st=stage[0], q=q, kind=kind, run=run, deps=deps, cost=cost, lat=lat, tag=tag, soft=soft))
+        for regs, w in ((wr, True), (rd, False)):
+            for r in regs:
+                h = hist.setdefault(r[0], [])
+                if (w or r[0] == "ps") and r[3] == 1:
+                    h[:] = [e for e in h if not (r[1] <= e[0][1] and e[0][2] <= r[2])]
+                h.append((r, w, me))
+        return me
+
+    def op(q, call, outs, ins, cyc=None, more=()):
+        views = [i for i in ins if isinstance(i, tuple)]
+        if cyc is None:
+            big = views[0] if views else outs[0]
+            two = q == "V" and all(x[3] == 2 for x in outs + views if x[2] > 1)
+            cyc = big[2] * (GAT if big[4] else 0.5 if two else 1.0) + (30 if q == "S" else 0)
+        wr, rd = [r for o in outs for r in o[1]], list(more) + [r for i in views for r in i[1]]
+        args = [o[0] for o in outs] + [i[0] if isinstance(i, tuple) else i for i in ins]
+        return node(q, "op", lambda tag=stage[0]: call(*args), wr, rd, FIX + cyc * CYC)
+
+    def dma(q, name, out, in_, size, wr=(), rd=()):
+        node(q, "d_" + name, lambda tag=stage[0]: Q[q].dma_start(out, in_), list(wr), list(rd), 0.1, FLY + size / BW)
+
+    def load(q, name, dst, src, size):
+        busy[0] += size / BW
+        prev = chain[-1:] if q == "Y" else []
+        me = node(q, "d_" + name, lambda tag=stage[0]: Q[q].dma_start(dst[0], src), dst[1], [], 0.1, busy[0] + FLY - 0.7,
+                  after=prev, soft=prev[0] if prev else None)
+        if q == "Y":
+            chain.append(me)
+
+    def send(to, sem, dst, src, size, extra=0.0, after=None):
+        rid, pid = topo.addr(to)[:2]
+        return node("G", "send", lambda tag=stage[0]: g.remote_dma(dst[0], src[0], T.sem[sem], T.sem.sent, pid, rid, topo.mask(core, to)),
+                    [], src[1], 0.3 + extra, FLY - 0.3 + size / BW, tag=len(topo.engines(core, to)),
+                    after=[] if after is None else [after], soft=after)
+
+    def arrives(frm, sem, views, mine):
+        node("R", sem, None, [r for x in views for r in x[1]], [], 0.0, 0.0, after=mine, tag=len(views) * len(topo.engines(frm, core)))
+
+    V = g.vector
+
+    def ts(out, a, s1, o0, s2=None, o1=None):
+        if o1 is None:
+            op("V", lambda o, x, p: V.tensor_scalar(o, x, p, None, o0), [out], [a, s1])
+        else:
+            op("V", lambda o, x, p, q_: V.tensor_scalar(o, x, p, q_, o0, o1), [out], [a, s1, s2])
+
+    def tt(out, a, b, o):
+        op("V", lambda y, x, z: V.tensor_tensor(y, x, z, o), [out], [a, b], a[2] * (1 if a[1][0][0] == "ps" else 2))
+
+    def cp(out, a):
+        op("V", V.tensor_copy, [out], [a])
+
+    def scat(win, off, a):
+        op("V", V.tensor_copy, [(win[0].indirect(off[0]),) + win[1:]], [a], a[2] * SCA, off[1])
+
+    def scan(out, d0, d1, init, o0, o1):
+        op("V", lambda o, a, b, i: V.tensor_tensor_scan(o, a, b, i, o0, o1), [out], [d0, d1, init])
+
+    def act(out, a, f, scale=1.0, bias=None, acc=None):
+        if acc is not None:
+            op("S", lambda o, ac, x, s, b: g.scalar.activation(o, x, f, bias=b, scale=s, accum_out=ac), [out, acc], [a, scale, bias], a[2] + 50)
+        elif bias is None:
+            op("S", lambda o, x, s: g.scalar.activation(o, x, f, scale=s), [out], [a, scale])
+        else:
+            op("S", lambda o, x, s, b: g.scalar.activation(o, x, f, bias=b, scale=s), [out], [a, scale, bias])
+
+    def move(q, out, a):
+        if q == "V":
+            cp(out, a)
+        else:
+            op("S", lambda o, x: g.scalar.activation(o, x, Fn.Copy), [out], [a])
+
+    def quant(c, s, a):
+        op("V", V.quantize_mx, [c, s], [a], a[2] * 0.265)
+
+    def mm(out, lq, ls, rq, rs):
+        op("T", lambda o, a, b, c, d: g.tensor.matmul_mx(o, a, b, c, d, True, True), [out], [lq, ls, rq, rs], (rq[2] + 16) * 0.8)
+
+    def iota(out, pattern, base=0, cm=0):
+        if SCRATCH[out[1][0][0]][2] == i32:
+            op("G", lambda o: g.iota(o, pattern, base, cm), [out], [], 80 + 2 * out[2])
+        else:
+            op("G", lambda o: g.iota(o, pattern, base, cm, allow_small_or_imprecise_dtypes=True), [out], [], 80 + 2 * out[2])
+
+    def fill(out, c):
+        iota(out, [[0, out[2]]], c)
+
+    def keep(out, a, pattern, cmp, base, cm):
+        op("G", lambda o, x: g.affine_select(o, x, pattern, cmp, 0.0, base, cm), [out], [a], 130 + 2 * out[2])
+
+    def turn(to, name, lo, width):
+        op("V", V.transpose, [v(to, 0, width)], [v(name, lo, lo + width)])
+        op("V", V.transpose, [v(to, width, 2 * width + 32)], [v(name, lo - 16, lo + width + 16)])
+
+    def below(n, ns, width, row, key, cmp, sums, seg, out, cap):
+        nv = n - ns
+        cut = lambda name, c: v(name, width * c, width * c + width)
+        for c in range(nv, n):
+            act(cut(cmp, c), row(c), Fn.Sign, -1.0, key(c))
+            act(cut(sums, c), cut(cmp, c), Fn.Relu, 1.0, 0.0, v("cn", c, c + 1))
+        for c in range(nv):
+            ts(cut(cmp, c), row(c), key(c), Op.is_lt)
+        scan(v(sums, 0, width * nv), v(seg, 0, width * nv), v(cmp, 0, width * nv), 0.0, Op.mult, Op.add)
+        ts(v(out, 0, nv), v(sums, width - 1, width * nv, width), cap, Op.min)
+        if ns:
+            ts(v(out, nv, n), v("cn", nv, n), cap, Op.min)
+
+    ci = lambda k: v("ci", k, k + 1)
+    cf = lambda k: v("cf", k, k + 1)
+    pk = lambda a, b: v("pk", a, b)
+    (M0, CA, CB_, G16, GOF, GOF4, NGOF, QI, M8, AA, BB, C0, C2, TH, SP, JB, K0, K1, R16, B2, HF, RF, TMP, TM2,
+     B14, R24, B8, B6, P16, MS, MB, M47, A1) = [cf(k) for k in range(33)]
+    PK14, PK6, PKA, PKB, PKE, PKU, PK8 = pk(0, 5), pk(14, 15), pk(16, 17), pk(18, 19), pk(20, 21), pk(22, 30), pk(30, 31)
+    W = ["w0", "w1", "w2", "w3"]
+    E = ["e0", "e1", "e2"]
+    AT = v("at", OFF, OFF + MC)
+
+    def constants():
+        iota(ci(0), [[0, 1]], 0, 1)
+        iota(v("iot", 0, 416), [[1, 416]])
+        fill(v("at", OFF, OFF + 320), MISS)
+        op("V", lambda o: V.memset(o, float(MISS)), [v("at", OFF + 320, OFF + MC)], [])
+        iota(v("iot", 416, MC), [[1, MC - 416]], 416)
+        ts(ci(1), ci(0), 15, Op.bitwise_and)
+        ts(ci(2), ci(0), 112, Op.bitwise_and)
+        ts(ci(3), ci(0), 4, Op.logical_shift_right)
+        ts(ci(6), ci(0), 1, Op.bitwise_and)
+        ts(ci(7), ci(0), 1, Op.logical_shift_right, 7, Op.bitwise_and)
+        ts(M0, ci(1), 4.0, Op.is_lt)
+        ts(M8, ci(1), 8.0, Op.is_lt)
+        tt(ci(4), ci(0), ci(3), Op.add)
+        ts(G16, ci(2), 0.0, Op.add)
+        ts(GOF, ci(2), float(OFF), Op.add)
+        ts(CA, M0, 3.0, Op.mult, 1.0, Op.add)
+        ts(CB_, ci(1), M0, Op.mult)
+        ts(BB, M0, 4.0, Op.mult)
+        ts(TMP, M8, 3.0, Op.mult, 1.0, Op.add)
+        ts(ci(5), ci(4), 1, Op.bitwise_and)
+        ts(C0, ci(1), M8, Op.mult, GOF, Op.add)
+        ts(QI, CA, 415.0, Op.mult, CB_, Op.add)
+        ts(AA, TMP, BB, Op.subtract)
+        ts(GOF4, ci(2), float(OFF + 4), Op.add)
+        ts(MS, CA, 2.0 ** -16, Op.mult)
+        ts(MB, CA, -0.125, Op.mult)
+        ts(R16, ci(1), 16.0, Op.mult)
+        ts(P16, ci(6), 16.0, Op.mult)
+        ts(B14, ci(5), 240.0, Op.mult, R16, Op.add)
+        ts(B8, ci(5), 144.0, Op.mult, R16, Op.add)
+        ts(B6, ci(5), 112.0, Op.mult, R16, Op.add)
+        ts(B2, ci(5), 48.0, Op.mult, P16, Op.add)
+        ts(TM2, ci(7), 4.0, Op.is_ge, 8.0, Op.mult)
+        ts(HF, ci(7), TM2, Op.max)
+        ts(RF, ci(1), 0.0, Op.add)
+        ts(K0, ci(1), -2.0, Op.mult, 31.5, Op.add)
+        ts(K1, ci(1), -2.0, Op.mult, 30.5, Op.add)
+        ts(C2, M0, float(4 * HB[2] - OFF), Op.mult, C0, Op.add)
+        ts(TH, M0, 1788.0, Op.mult, CB_, Op.add)
+        ts(SP, M0, 16383.0, Op.mult, 1.0, Op.add)
+        ts(JB, M0, 1664.0, Op.mult, CB_, Op.add)
+        ts(NGOF, GOF, -1.0, Op.mult)
+        iota(v("ir"), [[0, 6], [1, 16]])
+        iota(v("ci", 8, 16), [[16, 8]])
+        ts(PK14, v("iot", 0, 5), B14, Op.add, 479.0, Op.min)
+        ts(PK8, B8, 287.0, Op.min)
+        ts(PK6, B6, -160.0, Op.add)
+        ts(PKA, ci(7), B2, Op.add, 4.0, Op.add)
+        ts(PKB, HF, B2, Op.add)
+        ts(PKE, B2, 9.0, Op.add)
+        cp(PKU, v("ci", 8, 16))
+        for t in range(3):
+            iota(v(E[t], 32, 416), [[4, 16], [64, 24]], 128, 1)
+            iota(v(E[t], 416, 448), [[4, 32]], 1664, 1)
+            fill(v(E[t], 448, 464), 0)
+            fill(v(W[t], 4 * ZC[t], 4 * HB[t]), 0)
+        for t in range(4):
+            fill(v(W[t], 0, 128), 0)
+        iota(v("otb"), [[1, 24], [24, 16]], 32)
+        tt(M47, M8, M0, Op.subtract)
+        tt(A1, CA, M47, Op.subtract)
+        act(v("sl", 0, 32), v("iot", 0, 32), Fn.Identity, CA, CB_)
+        act(v("yb"), v("iot", 32, 416), Fn.Identity, A1, CB_)
+        act(v("kk"), v("otb"), Fn.Identity, M47)
+        tt(v("sl", 32, 416), v("yb"), v("kk"), Op.add)
+        ts(R24, ci(1), 24.0, Op.mult)
+        ts(v("pkp"), v("iot", 0, 24), R24, Op.add)
+        act(v("tb"), v("iot"), Fn.Identity, AA)
+        act(v("jc0"), v("iot", 0, A), Fn.Identity, BB, C0)
+        act(v("jc2"), v("iot", 0, A), Fn.Identity, BB, C2)
+        act(v("j2"), v("iot", 0, A), Fn.Identity, BB, JB)
+        for name, lo, hi in (("src", 0, 16), ("src", 240, 256), ("mb", 0, 16), ("mb", 144, 160), ("cb", 0, 16), ("cb", 112, 128),
+                             ("vb", 0, 16), ("eb", 0, 16), ("eb", 48, 64)):
+            fill(v(name, lo, hi), 0)
+        fill(v("vb", 48, 80), MISS)
+        fill(v("ones"), 1)
+        keep(v("ey"), v("ones"), [[1, 516]], Op.is_equal, -3, -4)
+        for b in range(4):
+            quant(v("eq", 128 * b, 128 * b + 128), v("ep", 128 * b, 128 * b + 128), v("ey", 3 - b, 515 - b))
+        iota(v("g3", 0, 32), [[1, 32]])
+        fill(v("g3", 32, 128), -1)
+        for name, nv, width in (("seg1", 8 - min(NS), 128), ("seg2", 6 - min(N2), 102)):
+            fill(v(name, 0, width * nv), 1)
+            keep(v(name, 0, width * nv), v(name, 0, width * nv), [[0, nv], [1, width]], Op.is_gt, 0, 0)
+        ts(v("uu"), v("ir"), RF, Op.is_lt, 2.0 ** 90, Op.mult)
+        ts(v("ut"), v("ir"), RF, Op.is_equal, 2.0 ** 95, Op.mult)
+        tt(v("uu"), v("uu"), v("ut"), Op.subtract)
+
+    def sides():
+        quant(v("uq"), v("up"), v("us"))
+        op("V", V.tensor_copy, [w32(v("uq2"))], [ind(w32(v("uq")), PKU)])
+        move("S", v("up2"), ind(v("up"), PKU))
+
+    def tables():
+        cp(v("tgu"), v("tgi"))
+        cp(v("adu"), v("adi"))
+        scat(AT, v("tgu"), v("sl", 32, 416))
+        act(v("tags", 32, 416), ind(v("iot"), v("tgu")), Fn.Identity, 1.0, GOF)
+        iota(v("tags", 0, 32), [[4, 32]], 0, 1)
+
+    def lookup(t):
+        look = ind(AT, v("adu", 14 * t, 14 * t + 14))
+        if MISS_ON[t] == "S":
+            act(v("mis"), look, Fn.Relu, MS, MB)
+        else:
+            ts(v("mis"), look, 8192.0, Op.is_ge, CA, Op.mult)
+        scan(v("qq"), v("mis"), v("mis"), QI, Op.add, Op.max)
+        if t == 2:
+            ts(v("mis"), v("qq"), TH, Op.subtract, SP, Op.mult)
+            tt(v("alt"), v("mis"), v("j2"), Op.max)
+            tt(v("src", 16, 240), look, v("alt"), Op.min)
+        else:
+            tt(v("src", 16, 240), look, v("qq"), Op.min)
+        turn("ta", "src", 16, A)
+        ts(v("lz", 80 * t, 80 * t + 80), ind(v("ta"), PK14), float(4 * ZC[t]), Op.min)
+
+    def table(t):
+        val = v("val", A * t, A * t + A)
+        tt(val, ind(v("tb"), v("adu", 14 * t, 14 * t + 14)), v("jc2" if t == 2 else "jc0"), Op.add)
+        scat(v(E[t]), v("lz", 80 * t + 64, 80 * t + 78), val)
+
+    def served(t):
+        turn("tk", E[t], 416, 32)
+        if t < 2:
+            ts(v("sa%d" % t), ind(v("tk"), PKA), GOF4, Op.subtract)
+            mine = send(owner, "a_rq%d" % t, v("rq%d" % t), v("sa%d" % t, 0, 8), 2048, after=opened)
+            arrives(asker, "a_rq%d" % t, [v("rq%d" % t)], [mine])
+        ts(v("lk", 32 * t, 32 * t + 16), ind(v("tk"), PKB), G16, Op.subtract)
+        act(v("pen", 416 * t, 416 * t + P), ind(v(E[t], 32, 416), v("pkp")), Fn.Relu, 2.0 ** 70, -THR * 2.0 ** 70)
+        act(v("pen", 416 * t + P, 416 * t + 416), v(E[t], 416, 448), Fn.Relu, 2.0 ** 70, -THR * 2.0 ** 70)
+        tt(v("dr", 32 * t, 32 * t + 32), v("pen", 416 * t + P, 416 * t + 416), v("sl", 0, 32), Op.add)
+
+    def places(t):
+        for b in range(4):
+            to = v("tp", 96 * t + 24 * b, 96 * t + 24 * b + 24)
+            dma("Y", "p%d" % t, to[0], T[E[t]][b:128:16, 32:416], 12288, wr=to[1], rd=v(E[t], 32, 416)[1])
+        ts(v("le", 96 * t, 96 * t + 96), v("tp", 96 * t, 96 * t + 96), G16, Op.subtract)
+
+    def answer(t):
+        mem = v("ms", 0, 4 * MC)
+        c, s = "fq%d" % t, "fp%d" % t
+        if t == 2:
+            for b in range(4):
+                ts(v("f2l", 14 * b, 14 * b + 14), v("rq2"), 4.0, Op.mult, float(b), Op.add)
+                move("S", v("ft", b, 4 * A, 4), ind(mem, v("f2l", 14 * b, 14 * b + 14)))
+            quant(v(c), v(s), v("ft"))
+            lc, lp, w, wq = v("lc"), v("lp"), A, A
+            mine = [send(asker, "a_f2", b8(lc), b8(v(c)), 512 * A), send(asker, "a_f2", lp, v(s), 128 * A)]
+            arrives(owner, "a_f2", [lc, lp], mine)
+        else:
+            lo = 4 * (MC + K * t)
+            for b in range(4):
+                move("S", v("ms", lo + b, lo + 4 * K, 4), ind(mem, v("rq%d" % t, 2 * b, 2 * b + 2)))
+            quant(v(c, 0, 128), v(s, 0, 128), v("ms", lo + 4 * K - 512, lo + 4 * K))
+            mine = [send(asker, "a_f%d" % t, b8(v(c, 128, 160)), b8(v(c, 96, 128)), 512 * K),
+                    send(asker, "a_f%d" % t, v(s, 128, 160), v(s, 96, 128), 128 * K)]
+            arrives(owner, "a_f%d" % t, [v(c, 128, 160), v(s, 128, 160)], mine)
+            lc, lp, w, wq = v(c, 32, 160), v(s, 32, 160), K, 128
+        for b in range(4):
+            bank = 512 * (4 + b % 3)
+            mm(v("ps", bank, bank + wq), v("eq", 128 * b, 128 * b + 128), v("ep", 128 * b, 128 * b + 128), lc, lp)
+            move("S", v(W[t], 4 * 416 + b, 4 * (416 + w), 4), v("ps", bank + wq - w, bank + wq))
+
+    def layer(t):
+        z0 = 4 * A * t
+        for b in range(4):
+            move(RD[t][b], v("zt", z0 + b, z0 + 4 * A, 4), ind(v(W[t], 0, 4 * ZC[t] + 16), v("lz", 80 * t + 16 * b, 80 * t + 16 * b + 14)))
+        zq, zp = v("zq", A * t, A * t + A), v("zp", A * t, A * t + A)
+        quant(zq, zp, v("zt", z0, z0 + 4 * A))
+        for b in range(4):
+            mm(v("ps", 512 * b, 512 * b + A), v("wq", 128 * b, 128 * b + 128), v("wp", 128 * b, 128 * b + 128), zq, zp)
+        for b in range(4):
+            o, r = v(W[t], 4 * HB[t] + b, 4 * (HB[t] + A), 4), v("ps", 512 * b, 512 * b + A)
+            if RL[t][b] == "V":
+                ts(o, r, 0.0, Op.max, 0.03125, Op.mult)
+            else:
+                act(o, r, Fn.Relu, 0.03125)
+
+    def write(t):
+        hs = v("hs", 128 * t, 128 * t + 128)
+        move("S", hs, ind(v(W[t]), v("lk", 32 * t, 32 * t + 8)))
+        for b in range(4):
+            move(WR[t][b], v(W[t + 1], 128 + b, 1664, 4), ind(v(W[t]), v("le", 96 * t + 24 * b, 96 * t + 24 * b + 24)))
+        scat(v(W[t + 1], 0, 1664), v("lv", 16 * t, 16 * t + 8), hs)
+
+    def marks(t):
+        quant(v("xq"), v("xp"), v(W[t], 128, 1664))
+        mm(v("ps", 3584, 3584 + P), v("uq2"), v("up2"), v("xq"), v("xp"))
+
+    rw = lambda k: v("rw", 128 * k, 128 * k + 128)
+    sm = lambda k: v("sm", k, k + 1)
+
+    def blocks(t):
+        mins = v("mb", 16, 144)
+        tt(v("kk"), v("ps", 3584, 3584 + P), v("pen", 416 * t, 416 * t + P), Op.add)
+        tt(v("m1"), v("kk", 0, P, 3), v("kk", 1, P, 3), Op.min)
+        tt(mins, v("m1"), v("kk", 2, P, 3), Op.min)
+        turn("t1", "mb", 16, 128)
+        cp(v("ky"), ind(v("t1"), PK8))
+        below(8, NS[t], 128, lambda c: mins, lambda c: v("ky", c, c + 1), "jn1", "jn2", "seg1", "lt", 127.0)
+        act(rw(2), ind(v("iot", 0, 128), v("lt")), Fn.Identity, -1.0)
+        cp(rw(0), ind(v("g3"), v("lt")))
+        op("V", lambda y, x: V.tensor_reduce(y, x, AxisListType.X, Op.max, negate=True), [sm(0)], [rw(0)], 128)
+        ts(rw(3), rw(0), 0.0, Op.is_ge)
+        ts(rw(4), rw(2), sm(0), Op.is_gt)
+        scan(rw(5), rw(4), v("ones", 0, 128), sm(0), Op.add, Op.mult)
+        scan(rw(1), rw(3), rw(5), -32.0, Op.add, Op.min)
+        act(rw(6), rw(1), Fn.Sign, 1.0, K0, sm(2))
+        act(rw(7), rw(1), Fn.Sign, 1.0, K1, sm(3))
+
+    def victims(t):
+        for u in range(3):
+            ts(v("o6", u, 6, 3), v("sm", 2, 4), -1.5, Op.mult, 192.0 + u, Op.add)
+        ts(v("cb", 16, 112), ind(v("kk"), v("o6", 0, 6)), 2.0 ** 71, Op.min)
+        act(v("dl"), v("cb", 16, 112), Fn.Abs, 1.25 * 2.0 ** -24, 2.0 ** -124)
+        turn("t2", "cb", 16, 96)
+        cp(v("gb", 0, 16), ind(v("t2"), PK6))
+        act(v("dk", 0, 6), v("gb", 10, 16), Fn.Abs, 1.25 * 2.0 ** -24, 2.0 ** -124)
+        move("S", v("cp"), ind(v("sl", 32, 416), v("o6", 0, 6)))
+        tt(v("dl"), v("dl"), v("uu"), Op.min)
+        tt(v("gb", 16, 112), v("cb", 16, 112), v("dl"), Op.subtract)
+        tt(v("gb", 112, 118), v("gb", 10, 16), v("dk", 0, 6), Op.subtract)
+        below(6, N2[t], 102, lambda c: v("gb", 10 + c, 112 + c), lambda c: v("gb", 10 + c, 11 + c), "c1", "s1", "seg2", "rk", 95.0)
+        scat(v("sv"), v("rk", 0, 6), v("cp"))
+        tt(v("vb", 16, 48), v("sv", 0, 32), v("dr", 32 * t, 32 * t + 32), Op.min)
+        turn("tv", "vb", 16, 32)
+        cp(v("lv", 16 * t, 16 * t + 16), ind(v("tv"), PKB))
+
+    def retag(t):
+        lv = v("lv", 16 * t + 8, 16 * t + 10)
+        if t < 2:
+            move("S", v("eb", 16, 48), ind(v("tags"), lv))
+            turn("te", "eb", 16, 32)
+            ts(v("lk", 32 * t + 10, 32 * t + 26), ind(v("te"), PKE), G16, Op.subtract)
+            scat(v("at"), v("lk", 32 * t + 8, 32 * t + 12), v("vb", 16, 80))
+        scat(v("tags"), lv, v(E[t], 416, 448))
+
+    def last():
+        for lo in (0, 192):
+            q_, p_, bank, yb = v("xq", lo, lo + 192), v("xp", lo, lo + 192), 3584 - 512 * (lo > 0), v("yb", lo, lo + 192)
+            quant(q_, p_, v(W[3], 128 + 4 * lo, 896 + 4 * lo))
+            mm(v("ps", bank, bank + 192), v("vq"), v("vp"), q_, p_)
+            move("V" if lo else "S", yb, v("ps", bank, bank + 192))
+            dma("Y" if lo else "S", "oz" if lo else "oy", T.y[:, lo:lo + 192], yb[0], 512 * 192, rd=yb[1])
+
+    def store():
+        dma("Y", "oc", T.oc[:], b8(v("xq"))[0], 512 * P, rd=v("xq")[1])
+        act(v("otb"), v("tags", 32, 416), Fn.Identity, 1.0, NGOF)
+        for k in range(4):
+            dma("Y", "os", T.osc[4 * k:4 * k + 4, :], T.xp[32 * k:32 * k + 4, :], 4 * P, rd=v("xp")[1])
+        dma("Y", "ot", T.ot[:], T.otb[8:128:16, :], 32 * P, rd=v("otb")[1])
+
+    def late(t):
+        if t == 0:
+            dma("Y", "wc", b8(v("wq"))[0], T.wc[:], 262144, wr=v("wq")[1], rd=v("rq0")[1])
+            dma("Y", "ws", v("wp")[0], T.ws[:], 65536, wr=v("wp")[1], rd=v("rq0")[1])
+        if t == 1:
+            dma("Y", "v", v("vs")[0], T.v[:], 131072, wr=v("vs")[1], rd=v("fq0")[1])
+            quant(v("vq"), v("vp"), v("vs"))
+
+    def do(name, f, *a):
+        stage[0] = name + "".join(str(x) for x in a)
+        f(*a)
+
+    load("Y", "tg", v("tgi"), T.tg[:], 12288)
+    load("S", "ad", v("adi"), T.ad[:], 21504)
+    load("Y", "x", v("w0", 128, 1664), T.x[:], 1024 * P)
+    load("Y", "u", v("us"), T.u[:], 131072)
+    load("Y", "m", v("ms", 0, 4 * MC), T.m[:], 1024 * MC)
+    do("con", constants)
+    stage[0] = "rq2"
+    opened = send(owner, "a_rq2", v("rq2"), v("adi", 28, 42), 7168, 1.5)
+    arrives(asker, "a_rq2", [v("rq2")], [opened])
+    do("sid", sides)
+    do("tbl", tables)
+    for t in range(3):
+        for name, f in (("loo", lookup), ("tab", table), ("ser", served), ("lat", late), ("pla", places), ("ans", answer), ("mar", marks),
+                        ("blo", blocks), ("vic", victims), ("lay", layer), ("wri", write), ("ret", retag)):
+            do(name, f, t)
+    do("mar3", last)
+    do("sto", store)
+
+    if "order" not in PLAN:
+        PLAN["span"], PLAN["order"] = schedule(nodes)
+
+    waited, count, mark, total = {}, {}, {}, {}
+    for nd in nodes:
+        if nd["kind"].startswith("d_"):
+            total[nd["kind"]] = total.get(nd["kind"], 0) + 16
+
+    def wait(q, sem, val):
+        if waited.get((q, sem), 0) < val:
+            Q[q].wait_ge(T.sem[sem], val)
+            waited[(q, sem)] = val
+
+    for k in PLAN["order"]:
+        nd = nodes[k]
+        q, kind = nd["q"], nd["kind"]
+        if q == "R":
+            count[kind] = nd["tag"]
+            mark[k] = (kind, nd["tag"])
+            continue
+        need = {}
+        for d in nd["deps"]:
+            if d != nd["soft"]:
+                sem, val = mark[d]
+                need[sem] = max(need.get(sem, 0), val)
+        for sem in sorted(need):
+            wait(q, sem, need[sem])
+        call = nd["run"]()
+        if kind == "send":
+            count["sent"] = count.get("sent", 0) + nd["tag"]
+        elif kind == "op":
+            count["c" + q] = count.get("c" + q, 0) + 1
+            call.then_inc(T.sem["c" + q], 1)
+            mark[k] = ("c" + q, count["c" + q])
+        else:
+            count[kind] = total[kind]
+            call.then_inc(T.sem[kind], 16)
+            mark[k] = (kind, total[kind])
+    for sem in sorted(count):
+        wait("G", sem, count[sem])

@@ -6,10 +6,11 @@ THR = 1916.0
 MISS = 73728
 HB = (480, 480, 644)
 ZC = (448, 448, 640)
-NS = (2, 2, 2)
+NS = (3, 3, 3)
 N2 = (0, 0, 0)
 RD = RL = WR = ("SSSS", "SSSS", "SSSS")
-MISS_ON = "VSV"
+LIN = "V" * 6 + "S" * 40
+ATG = 320
 f32, bf, i32, u16, u8, x4 = "float32", "bfloat16", "int32", "uint16", "uint8", "float8_e4m3fn_x4"
 
 
@@ -24,22 +25,24 @@ SCRATCH = {
     "w0": _s(4 * 704, bf), "w1": _s(4 * 704, bf), "w2": _s(4 * 868, bf), "w3": _s(4 * 416, bf),
     "uq": _s(128, x4), "up": _s(128, u8), "uq2": _s(128, x4), "up2": _s(128, u8),
     "vq": _s(128, x4), "vp": _s(128, u8),
-    "xq": _s(P, x4), "xp": _s(P, u8), "zt": _s(3 * 4 * A, bf), "zq": _s(3 * A, x4), "zp": _s(3 * A, u8),
-    "eq": _s(512, x4), "ep": _s(512, u8), "ey": _s(516, bf), "ones": _s(516, bf),
+    "xq": _s(P, x4), "xp": _s(P, u8), "zq": _s(3 * A, x4), "zp": _s(3 * A, u8),
+    "z0": _s(OFF + 4 * A, bf), "z1": _s(OFF + 4 * A, bf), "z2": _s(OFF + 4 * A, bf), "fd": _s(256, bf),
+    "eq": _s(512, x4), "ep": _s(512, u8), "ey": _s(516, bf), "ones": _s(768, bf),
     "ft": _s(4 * A, bf), "fq2": _s(A, x4), "fp2": _s(A, u8), "fq0": _s(160, x4), "fp0": _s(160, u8),
     "fq1": _s(160, x4), "fp1": _s(160, u8), "lc": _s(A, x4), "lp": _s(A, u8),
     "rq2": _s(14, i32), "rq0": _s(8, u16), "rq1": _s(8, u16), "f2l": _s(56, u16),
     "sa0": _s(16, u16), "sa1": _s(16, u16),
-    "iot": _s(MC, f32), "tb": _s(MC, f32), "at": _s(OFF + MC, f32), "sl": _s(416, f32),
-    "jc0": _s(A, f32), "jc2": _s(A, f32), "j2": _s(A, f32), "val": _s(3 * A, f32),
+    "iot": _s(MC, f32), "at": _s(OFF + MC, f32), "sl": _s(416, f32),
+    "j2": _s(64, f32), "k8": _s(A, bf), "val": _s(3 * A, f32),
     "e0": _s(640, f32), "e1": _s(640, f32), "e2": _s(640, f32),
     "tags": _s(416, f32), "otb": _s(P, f32), "yb": _s(P, f32),
-    "ci": _s(16, i32), "cf": _s(40, f32), "ir": _s(96, f32), "pk": _s(40, u16), "pkp": _s(24, u16),
+    "ci": _s(16, i32), "cf": _s(48, f32), "ir": _s(96, f32), "pk": _s(40, u16), "pkp": _s(24, u16),
     "uu": _s(96, f32), "ut": _s(96, f32), "g3": _s(128, f32), "seg1": _s(1024, bf), "seg2": _s(612, bf),
     "ta": _s(480, f32), "tp": _s(288, f32), "t1": _s(288, f32), "t2": _s(224, f32), "tk": _s(96, f32), "tv": _s(96, f32), "te": _s(96, f32),
-    "mis": _s(A, f32), "qq": _s(A, f32), "alt": _s(A, f32), "src": _s(256, f32),
+    "mis": _s(A, f32), "qq": _s(80, f32), "alt": _s(80, f32), "src": _s(256, f32),
     "lz": _s(240, u16), "lk": _s(96, u16), "le": _s(288, u16), "lv": _s(48, u16),
-    "pen": _s(3 * 416, bf), "kk": _s(P, f32), "m1": _s(128, f32), "mb": _s(160, f32), "ky": _s(16, f32),
+    "pen": _s(3 * 416, bf), "kk": _s(P, f32), "sg3": _s(P, bf), "mb": _s(480, f32), "k47": _s(P, bf), "k03": _s(A, bf),
+    "vd": _s(A, f32), "ky": _s(16, f32),
     "c1": _s(612, bf), "s1": _s(612, bf), "cn": _s(8, f32), "lt": _s(8, u16), "rw": _s(8 * 128, bf),
     "jn1": _s(1024, bf), "jn2": _s(1024, bf),
     "sm": _s(8, f32), "o6": _s(8, u16), "cb": _s(128, f32), "dl": _s(96, f32), "dk": _s(8, f32), "gb": _s(120, f32),
@@ -50,7 +53,7 @@ SCRATCH = {
 DMAS = ["tg", "ad", "x", "u", "m", "wc", "ws", "v", "oy", "oz", "oc", "os", "ot", "p0", "p1", "p2"]
 SEMAPHORES = ["cV", "cS", "cT", "cG", "sent", "a_rq2", "a_rq0", "a_rq1", "a_f2", "a_f0", "a_f1"] + ["d_" + n for n in DMAS]
 CYC, FIX, GAT, SCA, SAME, CROSS, FLY, BW = 1.04e-3, 0.06, 1.56, 3.8, 0.05, 0.15, 2.0, 190e3
-SEED, ITER, TEMP = 11, 11000, 0.5
+SEED, ITER, TEMP = 5, 40000, 0.6
 PLAN = {}
 
 
@@ -77,25 +80,34 @@ def schedule(nodes):
         for d, w in pre[k]:
             post[d].append((k, w))
 
-    def plan(bias):
-        way = [0.0] * len(nodes)
-        for k in reversed(every):
-            way[k] = cost[k] + 1e-6 + bias.get(group[k], 0.0) + max([way[u] + w for u, w in post[k]] + [nodes[k]["lat"]])
-        start, slots, span = [0.0] * len(nodes), {}, 0.0
-        for k in sorted(every, key=lambda j: (-way[j], j)):
-            t0 = max([start[d] + cost[d] + w for d, w in pre[k]] + [0.0])
-            sl = slots.setdefault(queue[k], [])
-            i = 0
-            for a, b in sl:
-                if b > t0:
-                    if t0 + cost[k] <= a:
-                        break
-                    t0 = b
-                i += 1
-            sl.insert(i, (t0, t0 + cost[k]))
+    lat = [nd["lat"] for nd in nodes]
+
+    def lay(order, links, first):
+        start, slots = [0.0] * len(nodes), {}
+        for k in order:
+            t0, c = first[k], cost[k]
+            for d, w in links[k]:
+                e = start[d] + cost[d] + w
+                if e > t0:
+                    t0 = e
+            if c > 0.0:
+                sl = slots.setdefault(queue[k], [])
+                i = len(sl)
+                while i > 0 and sl[i - 1][1] > t0:
+                    i -= 1
+                while i < len(sl) and t0 + c > sl[i][0]:
+                    t0 = sl[i][1]
+                    i += 1
+                sl.insert(i, (t0, t0 + c))
             start[k] = t0
-            span = max(span, t0 + cost[k] + nodes[k]["lat"])
-        return span, sorted(every, key=lambda j: (start[j], j))
+        return start
+
+    zero = [0.0] * len(nodes)
+
+    def both(start):
+        back = lay(sorted(every, key=lambda j: (-start[j] - cost[j], -j)), post, lat)
+        start = lay(sorted(every, key=lambda j: (-back[j] - cost[j], j)), pre, zero)
+        return max(start[k] + cost[k] + lat[k] for k in every), start
 
     seed = [SEED]
 
@@ -104,19 +116,42 @@ def schedule(nodes):
         return (seed[0] >> 9) % n
 
     names = sorted(set(group))
-    best = {}
-    span, order = top = plan(best)
+    way = [0.0] * len(nodes)
+    for k in reversed(every):
+        way[k] = cost[k] + 1e-6 + max([way[u] + w for u, w in post[k]] + [lat[k]])
+    span, cur = top = both(lay(sorted(every, key=lambda j: (-way[j], j)), pre, zero))
     for it in range(ITER):
-        b = dict(best)
-        for _ in range(1 + rnd(3)):
-            nm = names[rnd(len(names))]
-            b[nm] = max(0.0, b.get(nm, 0.0) + (rnd(2001) / 1000.0 - 1.0) * (0.1, 0.5, 2.0, 6.0)[rnd(4)])
-        sp, od = plan(b)
+        key = list(cur)
+        for _ in range(1 + rnd(2)):
+            by = (rnd(2001) / 1000.0 - 1.0) * (0.3, 1.0, 3.0, 6.0)[rnd(4)]
+            if rnd(2):
+                nm = names[rnd(len(names))]
+                for k in every:
+                    if group[k] == nm:
+                        key[k] += by
+            else:
+                key[rnd(len(nodes))] += by
+        if rnd(2):
+            for k in every:
+                for d, w in pre[k]:
+                    if key[d] > key[k]:
+                        key[k] = key[d]
+        else:
+            for k in reversed(every):
+                for u, w in post[k]:
+                    if key[u] < key[k]:
+                        key[k] = key[u]
+        st = lay(sorted(every, key=lambda j: (key[j], j)), pre, zero)
+        sp = max(st[k] + cost[k] + lat[k] for k in every)
+        if rnd(3) == 0:
+            s2, t2 = both(st)
+            if s2 < sp:
+                sp, st = s2, t2
         if sp <= span + TEMP * (1 - it / ITER) * rnd(1000) / 1000.0:
-            best, span = b, sp
+            cur, span = st, sp
             if sp < top[0]:
-                top = (sp, od)
-    return top
+                top = (sp, st)
+    return top[0], sorted(every, key=lambda j: (top[1][j], j))
 
 
 def rank_program(g, core, T, topo):
@@ -221,6 +256,15 @@ def rank_program(g, core, T, topo):
         else:
             op("S", lambda o, x, s, b: g.scalar.activation(o, x, f, bias=b, scale=s), [out], [a, scale, bias])
 
+    nl = [0]
+
+    def lin(out, a, s, b):
+        nl[0] += 1
+        if LIN[nl[0] - 1] == "V":
+            ts(out, a, s, Op.mult, b, Op.add)
+        else:
+            act(out, a, Fn.Identity, s, b)
+
     def move(q, out, a):
         if q == "V":
             cp(out, a)
@@ -266,7 +310,7 @@ def rank_program(g, core, T, topo):
     cf = lambda k: v("cf", k, k + 1)
     pk = lambda a, b: v("pk", a, b)
     (M0, CA, CB_, G16, GOF, GOF4, NGOF, QI, M8, AA, BB, C0, C2, TH, SP, JB, K0, K1, R16, B2, HF, RF, TMP, TM2,
-     B14, R24, B8, B6, P16, MS, MB, M47, A1) = [cf(k) for k in range(33)]
+     B14, R24, B8, B6, P16, MS, MB, M47, A1, CV, N47, S31, PAR, N03, C1, R1, M12, N8, M811, G4) = [cf(k) for k in range(44)]
     PK14, PK6, PKA, PKB, PKE, PKU, PK8 = pk(0, 5), pk(14, 15), pk(16, 17), pk(18, 19), pk(20, 21), pk(22, 30), pk(30, 31)
     W = ["w0", "w1", "w2", "w3"]
     E = ["e0", "e1", "e2"]
@@ -275,9 +319,10 @@ def rank_program(g, core, T, topo):
     def constants():
         iota(ci(0), [[0, 1]], 0, 1)
         iota(v("iot", 0, 416), [[1, 416]])
-        fill(v("at", OFF, OFF + 320), MISS)
-        op("V", lambda o: V.memset(o, float(MISS)), [v("at", OFF + 320, OFF + MC)], [])
-        iota(v("iot", 416, MC), [[1, MC - 416]], 416)
+        fill(v("at", OFF, OFF + ATG), MISS)
+        op("V", lambda o: V.memset(o, float(MISS)), [v("at", OFF + ATG, OFF + MC)], [])
+        act(v("iot", 416, 832), v("iot", 0, 416), Fn.Identity, 1.0, 416.0)
+        iota(v("iot", 832, MC), [[1, MC - 832]], 832)
         ts(ci(1), ci(0), 15, Op.bitwise_and)
         ts(ci(2), ci(0), 112, Op.bitwise_and)
         ts(ci(3), ci(0), 4, Op.logical_shift_right)
@@ -285,39 +330,53 @@ def rank_program(g, core, T, topo):
         ts(ci(7), ci(0), 1, Op.logical_shift_right, 7, Op.bitwise_and)
         ts(M0, ci(1), 4.0, Op.is_lt)
         ts(M8, ci(1), 8.0, Op.is_lt)
-        tt(ci(4), ci(0), ci(3), Op.add)
+        ts(RF, ci(1), 0.0, Op.add)
         ts(G16, ci(2), 0.0, Op.add)
-        ts(GOF, ci(2), float(OFF), Op.add)
-        ts(CA, M0, 3.0, Op.mult, 1.0, Op.add)
-        ts(CB_, ci(1), M0, Op.mult)
-        ts(BB, M0, 4.0, Op.mult)
-        ts(TMP, M8, 3.0, Op.mult, 1.0, Op.add)
+        tt(ci(4), ci(0), ci(3), Op.add)
         ts(ci(5), ci(4), 1, Op.bitwise_and)
-        ts(C0, ci(1), M8, Op.mult, GOF, Op.add)
-        ts(QI, CA, 415.0, Op.mult, CB_, Op.add)
-        ts(AA, TMP, BB, Op.subtract)
-        ts(GOF4, ci(2), float(OFF + 4), Op.add)
-        ts(MS, CA, 2.0 ** -16, Op.mult)
-        ts(MB, CA, -0.125, Op.mult)
-        ts(R16, ci(1), 16.0, Op.mult)
+        ts(PAR, ci(5), 0.0, Op.add)
         ts(P16, ci(6), 16.0, Op.mult)
-        ts(B14, ci(5), 240.0, Op.mult, R16, Op.add)
-        ts(B8, ci(5), 144.0, Op.mult, R16, Op.add)
-        ts(B6, ci(5), 112.0, Op.mult, R16, Op.add)
-        ts(B2, ci(5), 48.0, Op.mult, P16, Op.add)
         ts(TM2, ci(7), 4.0, Op.is_ge, 8.0, Op.mult)
         ts(HF, ci(7), TM2, Op.max)
-        ts(RF, ci(1), 0.0, Op.add)
-        ts(K0, ci(1), -2.0, Op.mult, 31.5, Op.add)
-        ts(K1, ci(1), -2.0, Op.mult, 30.5, Op.add)
-        ts(C2, M0, float(4 * HB[2] - OFF), Op.mult, C0, Op.add)
-        ts(TH, M0, 1788.0, Op.mult, CB_, Op.add)
-        ts(SP, M0, 16383.0, Op.mult, 1.0, Op.add)
-        ts(JB, M0, 1664.0, Op.mult, CB_, Op.add)
-        ts(NGOF, GOF, -1.0, Op.mult)
+        lin(M47, M0, -1.0, M8)
+        lin(CA, M0, 3.0, 1.0)
+        lin(A1, M47, -1.0, CA)
+        lin(N47, M47, -1.0, 1.0)
+        lin(CB_, RF, M0, 0.0)
+        lin(S31, CA, 31.0, CB_)
+        lin(GOF, G16, 1.0, float(OFF))
+        lin(BB, M0, 4.0, 0.0)
+        lin(TMP, M8, 3.0, 1.0)
+        lin(AA, BB, -1.0, TMP)
+        lin(C0, RF, M8, GOF)
+        lin(N03, M0, -1.0, 1.0)
+        lin(CV, C0, N03, BB)
+        lin(C1, BB, -1.0, C0)
+        lin(C2, M0, float(4 * HB[2] - OFF), C1)
+        ts(M12, ci(1), 12.0, Op.is_lt)
+        lin(M811, M8, -1.0, M12)
+        lin(N8, M8, -1.0, 1.0)
+        lin(TH, M811, 3.0, N8)
+        lin(SP, RF, 1.0, -8.0)
+        lin(JB, SP, M811, 0.0)
+        lin(QI, TH, 415.0, JB)
+        lin(R1, RF, 1.0, 1.0)
+        lin(G4, G16, -4.0, 0.0)
+        lin(GOF4, G16, 1.0, float(OFF + 4))
+        lin(MS, TH, 2.0 ** -16, M8)
+        lin(MB, TH, -0.125, 0.0)
+        lin(R16, RF, 16.0, 0.0)
+        lin(B14, PAR, 240.0, R16)
+        lin(B8, PAR, 144.0, R16)
+        lin(B6, PAR, 112.0, R16)
+        lin(B2, PAR, 48.0, P16)
+        lin(K0, RF, -2.0, 31.5)
+        lin(K1, RF, -2.0, 30.5)
+        lin(NGOF, GOF, -1.0, 0.0)
+        lin(R24, RF, 24.0, 0.0)
         iota(v("ir"), [[0, 6], [1, 16]])
         iota(v("ci", 8, 16), [[16, 8]])
-        ts(PK14, v("iot", 0, 5), B14, Op.add, 479.0, Op.min)
+        ts(PK14, v("iot", 0, 5), B14, Op.add, 471.0, Op.min)
         ts(PK8, B8, 287.0, Op.min)
         ts(PK6, B6, -160.0, Op.add)
         ts(PKA, ci(7), B2, Op.add, 4.0, Op.add)
@@ -328,38 +387,36 @@ def rank_program(g, core, T, topo):
             iota(v(E[t], 32, 416), [[4, 16], [64, 24]], 128, 1)
             iota(v(E[t], 416, 448), [[4, 32]], 1664, 1)
             fill(v(E[t], 448, 464), 0)
-            fill(v(W[t], 4 * ZC[t], 4 * HB[t]), 0)
+            fill(v(W[t], 4 * (ZC[t] if t == 2 else 416), 4 * HB[t]), 0)
         for t in range(4):
             fill(v(W[t], 0, 128), 0)
         iota(v("otb"), [[1, 24], [24, 16]], 32)
-        tt(M47, M8, M0, Op.subtract)
-        tt(A1, CA, M47, Op.subtract)
         act(v("sl", 0, 32), v("iot", 0, 32), Fn.Identity, CA, CB_)
-        act(v("yb"), v("iot", 32, 416), Fn.Identity, A1, CB_)
-        act(v("kk"), v("otb"), Fn.Identity, M47)
-        tt(v("sl", 32, 416), v("yb"), v("kk"), Op.add)
-        ts(R24, ci(1), 24.0, Op.mult)
+        act(v("kk"), v("otb"), Fn.Identity, M47, A1)
+        op("V", lambda o: V.memset(o, 1.0), [v("ones")], [])
+        ts(v("k47"), v("ones", 0, P), N47, Op.mult)
+        scan(v("sl", 32, 416), v("k47"), v("kk"), S31, Op.mult, Op.add)
         ts(v("pkp"), v("iot", 0, 24), R24, Op.add)
-        act(v("tb"), v("iot"), Fn.Identity, AA)
-        act(v("jc0"), v("iot", 0, A), Fn.Identity, BB, C0)
-        act(v("jc2"), v("iot", 0, A), Fn.Identity, BB, C2)
-        act(v("j2"), v("iot", 0, A), Fn.Identity, BB, JB)
-        for name, lo, hi in (("src", 0, 16), ("src", 240, 256), ("mb", 0, 16), ("mb", 144, 160), ("cb", 0, 16), ("cb", 112, 128),
+        act(v("k03"), v("otb", 0, A), Fn.Identity, 0.0, M0)
+        act(v("k8"), v("otb", 0, A), Fn.Identity, 0.0, N8)
+        iota(v("j2"), [[1, 4], [64, 16]], 1664, 4)
+        act(v("j2"), v("j2"), Fn.Identity, 1.0, G4)
+        for name, lo, hi in (("src", 0, 16), ("src", 240, 256), ("mb", 0, 48), ("mb", 432, 480), ("cb", 0, 16), ("cb", 112, 128),
                              ("vb", 0, 16), ("eb", 0, 16), ("eb", 48, 64)):
             fill(v(name, lo, hi), 0)
         fill(v("vb", 48, 80), MISS)
-        fill(v("ones"), 1)
-        keep(v("ey"), v("ones"), [[1, 516]], Op.is_equal, -3, -4)
+        keep(v("ey"), v("ones", 0, 516), [[1, 516]], Op.is_equal, -3, -4)
         for b in range(4):
             quant(v("eq", 128 * b, 128 * b + 128), v("ep", 128 * b, 128 * b + 128), v("ey", 3 - b, 515 - b))
+        act(v("sg3"), v("otb"), Fn.Identity, 0.0, 0.0)
+        act(v("sg3", 0, P, 3), v("otb", 0, 128), Fn.Identity, 0.0, 2.0 ** 95)
         iota(v("g3", 0, 32), [[1, 32]])
         fill(v("g3", 32, 128), -1)
         for name, nv, width in (("seg1", 8 - min(NS), 128), ("seg2", 6 - min(N2), 102)):
-            fill(v(name, 0, width * nv), 1)
-            keep(v(name, 0, width * nv), v(name, 0, width * nv), [[0, nv], [1, width]], Op.is_gt, 0, 0)
-        ts(v("uu"), v("ir"), RF, Op.is_lt, 2.0 ** 90, Op.mult)
-        ts(v("ut"), v("ir"), RF, Op.is_equal, 2.0 ** 95, Op.mult)
-        tt(v("uu"), v("uu"), v("ut"), Op.subtract)
+            keep(v(name, 0, width * nv), v("ones", 0, width * nv), [[0, nv], [1, width]], Op.is_gt, 0, 0)
+        act(v("uu"), v("ir"), Fn.Relu, -1.0, R1)
+        act(v("ut"), v("uu"), Fn.Square, 1.0, -0.75)
+        act(v("uu"), v("ut"), Fn.Identity, 2.0 ** 92, -0.5625 * 2.0 ** 92)
 
     def sides():
         quant(v("uq"), v("up"), v("us"))
@@ -375,23 +432,22 @@ def rank_program(g, core, T, topo):
 
     def lookup(t):
         look = ind(AT, v("adu", 14 * t, 14 * t + 14))
-        if MISS_ON[t] == "S":
-            act(v("mis"), look, Fn.Relu, MS, MB)
-        else:
-            ts(v("mis"), look, 8192.0, Op.is_ge, CA, Op.mult)
-        scan(v("qq"), v("mis"), v("mis"), QI, Op.add, Op.max)
-        if t == 2:
-            ts(v("mis"), v("qq"), TH, Op.subtract, SP, Op.mult)
-            tt(v("alt"), v("mis"), v("j2"), Op.max)
-            tt(v("src", 16, 240), look, v("alt"), Op.min)
-        else:
-            tt(v("src", 16, 240), look, v("qq"), Op.min)
+        act(v("mis"), look, Fn.Relu, MS, MB)
+        scan(v("src", 16, 240), v("k8"), v("mis"), QI, Op.mult, Op.add)
         turn("ta", "src", 16, A)
-        ts(v("lz", 80 * t, 80 * t + 80), ind(v("ta"), PK14), float(4 * ZC[t]), Op.min)
+        if t == 2:
+            ts(v("alt", 0, 64), ind(v("ta", 8), pk(0, 4)), 1791.5, Op.subtract, 16384.0, Op.mult)
+            tt(v("qq", 0, 64), v("alt", 0, 64), v("j2"), Op.max)
+            cp(v("qq", 64, 80), ind(v("ta", 8), pk(4, 5)))
+        else:
+            cp(v("qq"), ind(v("ta", 8), PK14))
+        tt(v("alt"), ind(v("ta"), PK14), v("qq"), Op.min)
+        ts(v("lz", 80 * t, 80 * t + 80), v("alt"), float(4 * ZC[t]), Op.min)
 
     def table(t):
         val = v("val", A * t, A * t + A)
-        tt(val, ind(v("tb"), v("adu", 14 * t, 14 * t + 14)), v("jc2" if t == 2 else "jc0"), Op.add)
+        act(v("vd"), ind(v("iot"), v("adu", 14 * t, 14 * t + 14)), Fn.Identity, AA, CV)
+        scan(val, v("k03"), v("vd"), C2 if t == 2 else C1, Op.mult, Op.add)
         scat(v(E[t]), v("lz", 80 * t + 64, 80 * t + 78), val)
 
     def served(t):
@@ -434,14 +490,17 @@ def rank_program(g, core, T, topo):
         for b in range(4):
             bank = 512 * (4 + b % 3)
             mm(v("ps", bank, bank + wq), v("eq", 128 * b, 128 * b + 128), v("ep", 128 * b, 128 * b + 128), lc, lp)
-            move("S", v(W[t], 4 * 416 + b, 4 * (416 + w), 4), v("ps", bank + wq - w, bank + wq))
+            to = v(W[t], 4 * 416 + b, 4 * (416 + w), 4) if t == 2 else v("fd", 128 * t + K * b, 128 * t + K * b + K)
+            move("S", to, v("ps", bank + wq - w, bank + wq))
 
     def layer(t):
-        z0 = 4 * A * t
+        z0, zt = OFF, "z%d" % t
         for b in range(4):
-            move(RD[t][b], v("zt", z0 + b, z0 + 4 * A, 4), ind(v(W[t], 0, 4 * ZC[t] + 16), v("lz", 80 * t + 16 * b, 80 * t + 16 * b + 14)))
+            move(RD[t][b], v(zt, z0 + b, z0 + 4 * A, 4), ind(v(W[t], 0, 4 * ZC[t] + 16), v("lz", 80 * t + 16 * b, 80 * t + 16 * b + 14)))
         zq, zp = v("zq", A * t, A * t + A), v("zp", A * t, A * t + A)
-        quant(zq, zp, v("zt", z0, z0 + 4 * A))
+        if t < 2:
+            scat(v(zt), v("lk", 32 * t, 32 * t + 8), v("fd", 128 * t, 128 * t + 128))
+        quant(zq, zp, v(zt, z0, z0 + 4 * A))
         for b in range(4):
             mm(v("ps", 512 * b, 512 * b + A), v("wq", 128 * b, 128 * b + 128), v("wp", 128 * b, 128 * b + 128), zq, zp)
         for b in range(4):
@@ -466,11 +525,11 @@ def rank_program(g, core, T, topo):
     sm = lambda k: v("sm", k, k + 1)
 
     def blocks(t):
-        mins = v("mb", 16, 144)
+        mins = v("mb", 50, 432, 3)
         tt(v("kk"), v("ps", 3584, 3584 + P), v("pen", 416 * t, 416 * t + P), Op.add)
-        tt(v("m1"), v("kk", 0, P, 3), v("kk", 1, P, 3), Op.min)
-        tt(mins, v("m1"), v("kk", 2, P, 3), Op.min)
-        turn("t1", "mb", 16, 128)
+        scan(v("mb", 48, 432), v("sg3"), v("kk"), 0.0, Op.add, Op.min)
+        op("V", V.transpose, [v("t1", 0, 128)], [mins])
+        op("V", V.transpose, [v("t1", 128, 288)], [v("mb", 2, 480, 3)])
         cp(v("ky"), ind(v("t1"), PK8))
         below(8, NS[t], 128, lambda c: mins, lambda c: v("ky", c, c + 1), "jn1", "jn2", "seg1", "lt", 127.0)
         act(rw(2), ind(v("iot", 0, 128), v("lt")), Fn.Identity, -1.0)
@@ -519,7 +578,9 @@ def rank_program(g, core, T, topo):
             dma("Y" if lo else "S", "oz" if lo else "oy", T.y[:, lo:lo + 192], yb[0], 512 * 192, rd=yb[1])
 
     def store():
-        dma("Y", "oc", T.oc[:], b8(v("xq"))[0], 512 * P, rd=v("xq")[1])
+        for lo in (0, 192):
+            q_ = v("xq", lo, lo + 192)
+            dma("S" if lo else "Y", "oc", T.oc[:, 4 * lo:4 * lo + 768], b8(q_)[0], 512 * 192, rd=q_[1])
         act(v("otb"), v("tags", 32, 416), Fn.Identity, 1.0, NGOF)
         for k in range(4):
             dma("Y", "os", T.osc[4 * k:4 * k + 4, :], T.xp[32 * k:32 * k + 4, :], 4 * P, rd=v("xp")[1])

@@ -1,16 +1,18 @@
-from concourse.mybir import dt, AluOpType as Op, AxisListType, ActivationFunctionType as Fn
+from concourse.mybir import dt, AluOpType as Op, ActivationFunctionType as Fn
 
 MC, P, A, K = 896, 384, 224, 32
-OFF = 1920
-THR = 1916.0
-MISS = 73728
-HB = (480, 480, 644)
-ZC = (448, 448, 640)
+OFF = 2592
+THR = 2580.0
+SC = 2.0 ** 71
+PAD, ZB, HB, ZC = 912, 1680, 648, 416
+LAND = (160, 320)
 NS = (3, 3, 3)
-N2 = (0, 0, 0)
-RD = RL = WR = ("SSSS", "SSSS", "SSSS")
-LIN = "V" * 6 + "S" * 40
-ATG = 320
+RD = ("SSSS", "SS", "SSSS")
+WR = ("SSSSSV", "SSSS", "SSSS")
+RL = ("SSSS", "SSSS", "SSSS")
+MG = ("SVSS", "SSSS")
+PICK = dict(qq="V", ky="V", gb="V", rw="V", svh="S", st="SSSS", ot="S", seg="G", y="SSV")
+LIN = "S" * 40
 f32, bf, i32, u16, u8, x4 = "float32", "bfloat16", "int32", "uint16", "uint8", "float8_e4m3fn_x4"
 
 
@@ -22,136 +24,54 @@ SCRATCH = {
     "tgi": _s(24, i32), "adi": _s(42, i32), "tgu": _s(24, u16), "adu": _s(42, u16),
     "ms": _s(4 * (MC + 2 * K), bf), "us": _s(512, bf), "vs": _s(512, bf),
     "wq": _s(512, x4), "wp": _s(512, u8),
-    "w0": _s(4 * 704, bf), "w1": _s(4 * 704, bf), "w2": _s(4 * 868, bf), "w3": _s(4 * 416, bf),
+    "w0": _s(4400, bf), "w1": _s(4400, bf), "w2": _s(4400, bf), "w3": _s(2576, bf),
     "uq": _s(128, x4), "up": _s(128, u8), "uq2": _s(128, x4), "up2": _s(128, u8),
     "vq": _s(128, x4), "vp": _s(128, u8),
     "xq": _s(P, x4), "xp": _s(P, u8), "zq": _s(3 * A, x4), "zp": _s(3 * A, u8),
-    "z0": _s(OFF + 4 * A, bf), "z1": _s(OFF + 4 * A, bf), "z2": _s(OFF + 4 * A, bf), "fd": _s(256, bf),
-    "eq": _s(512, x4), "ep": _s(512, u8), "ey": _s(516, bf), "ones": _s(768, bf),
-    "ft": _s(4 * A, bf), "fq2": _s(A, x4), "fp2": _s(A, u8), "fq0": _s(160, x4), "fp0": _s(160, u8),
-    "fq1": _s(160, x4), "fp1": _s(160, u8), "lc": _s(A, x4), "lp": _s(A, u8),
-    "rq2": _s(14, i32), "rq0": _s(8, u16), "rq1": _s(8, u16), "f2l": _s(56, u16),
-    "sa0": _s(16, u16), "sa1": _s(16, u16),
-    "iot": _s(MC, f32), "at": _s(OFF + MC, f32), "sl": _s(416, f32),
-    "j2": _s(64, f32), "k8": _s(A, bf), "val": _s(3 * A, f32),
-    "e0": _s(640, f32), "e1": _s(640, f32), "e2": _s(640, f32),
-    "tags": _s(416, f32), "otb": _s(P, f32), "yb": _s(P, f32),
-    "ci": _s(16, i32), "cf": _s(48, f32), "ir": _s(96, f32), "pk": _s(40, u16), "pkp": _s(24, u16),
-    "uu": _s(96, f32), "ut": _s(96, f32), "g3": _s(128, f32), "seg1": _s(1024, bf), "seg2": _s(612, bf),
-    "ta": _s(480, f32), "tp": _s(288, f32), "t1": _s(288, f32), "t2": _s(224, f32), "tk": _s(96, f32), "tv": _s(96, f32), "te": _s(96, f32),
-    "mis": _s(A, f32), "qq": _s(80, f32), "alt": _s(80, f32), "src": _s(256, f32),
-    "lz": _s(240, u16), "lk": _s(96, u16), "le": _s(288, u16), "lv": _s(48, u16),
-    "pen": _s(3 * 416, bf), "kk": _s(P, f32), "sg3": _s(P, bf), "mb": _s(480, f32), "k47": _s(P, bf), "k03": _s(A, bf),
-    "vd": _s(A, f32), "ky": _s(16, f32),
-    "c1": _s(612, bf), "s1": _s(612, bf), "cn": _s(8, f32), "lt": _s(8, u16), "rw": _s(8 * 128, bf),
+    "z2": _s(4 * A, bf), "fd": _s(256, bf), "ft": _s(4 * A, bf),
+    "fq2": _s(A, x4), "fp2": _s(A, u8), "lc": _s(A, x4), "lp": _s(A, u8), "fq": _s(352, x4), "fp": _s(352, u8),
+    "eq": _s(512, x4), "ep": _s(512, u8), "ey": _s(516, bf),
+    "rq0": _s(8, u16), "rq1": _s(8, u16), "rq2": _s(14, i32), "sa0": _s(16, u16), "sa1": _s(16, u16),
+    "r2": _s(56, i32), "f2l": _s(56, u16),
+    "iot": _s(MC, f32), "at": _s(OFF + MC, f32), "st": _s(416, f32), "tr": _s(P, f32), "es": _s(432, f32),
+    "jj": _s(A, f32), "k8": _s(A, bf), "val": _s(3 * A, f32), "k14": _s(A, bf), "vd": _s(A, f32),
+    "e0": _s(640, f32), "e1": _s(640, f32), "e2": _s(640, f32), "ex": _s(64, f32),
+    "otb": _s(416, f32), "yb": _s(P, f32), "dj": _s(64, f32), "j2": _s(A, f32), "tc": _s(128, f32),
+    "ci": _s(16, i32), "cf": _s(48, f32), "be": _s(4, f32), "cu": _s(4, f32), "ir": _s(96, f32), "pk": _s(24, u16),
+    "uu": _s(192, bf), "g3": _s(128, f32), "seg1": _s(1024, bf), "seg2": _s(648, bf),
+    "ar": _s(1840, f32), "tp": _s(288, f32), "tz": _s(168, f32), "t1": _s(288, f32), "tk": _s(96, f32), "tv": _s(96, f32),
+    "mis": _s(A, f32), "qq": _s(16, f32), "alt": _s(16, f32),
+    "lz": _s(240, u16), "lb": _s(48, u16), "lk": _s(96, u16), "le": _s(288, u16),
+    "kk": _s(P, f32), "sg3": _s(P, bf), "ky": _s(16, f32),
+    "c1": _s(648, bf), "s1": _s(648, bf), "cn": _s(8, f32), "lt": _s(8, u16), "rw": _s(8 * 128, bf),
     "jn1": _s(1024, bf), "jn2": _s(1024, bf),
-    "sm": _s(8, f32), "o6": _s(8, u16), "cb": _s(128, f32), "dl": _s(96, f32), "dk": _s(8, f32), "gb": _s(120, f32),
-    "cp": _s(96, f32), "rk": _s(8, u16), "sv": _s(96, f32), "dr": _s(96, f32), "vb": _s(80, f32), "eb": _s(64, f32),
+    "sm": _s(8, f32), "o6": _s(8, u16), "dk": _s(8, f32), "gb": _s(236, f32),
+    "cp": _s(96, f32), "rk": _s(8, u16), "sv": _s(96, f32), "sh": _s(32, f32), "mx": _s(32, f32),
     "hs": _s(3 * 128, bf),
     "ps": ("psum", [128, 4096], f32),
 }
-DMAS = ["tg", "ad", "x", "u", "m", "wc", "ws", "v", "oy", "oz", "oc", "os", "ot", "p0", "p1", "p2"]
-SEMAPHORES = ["cV", "cS", "cT", "cG", "sent", "a_rq2", "a_rq0", "a_rq1", "a_f2", "a_f0", "a_f1"] + ["d_" + n for n in DMAS]
-CYC, FIX, GAT, SCA, SAME, CROSS, FLY, BW = 1.04e-3, 0.06, 1.56, 3.8, 0.05, 0.15, 2.0, 190e3
-SEED, ITER, TEMP = 5, 40000, 0.6
-PLAN = {}
+ROWS = {"ta": (0, 496), "src": (496, 256), "mb": (752, 480), "cb": (1232, 264), "t2": (1496, 256), "vb": (1760, 80)}
+DMAS = ["tg", "ad", "x", "u", "m", "wc", "wd", "ws", "v", "oy", "oz", "oc", "os", "ot", "p0", "p1", "p2", "q1",
+        "j1", "j2", "tr", "ec", "r2"]
+SEMAPHORES = ["cV", "cS", "cT", "cG", "sent", "a_rq0", "a_rq1", "a_rq2", "a_f0", "a_f1", "a_f2"] + ["d_" + n for n in DMAS]
+CYC, FIX, GAT, SCA = 1.04e-3, 0.06, 1.56, 3.8
+ORDER = (
+    "(f(j(b)g(a(l(k(m(n)l)m(p(o)k)h)p)i)o(g+l*f+f(h)n)j(c(d(e(q(t(r(s(u(w(x)d+m*h+k,c*i,i+q,b(y)z(v(z)c)b)s)a(i,o*g,n*c)q)u*z,p"
+    "*t*q)r*e.g*w)t*u,u,v*b)x)f*a*v,e,s)e,w,x,k+y*j,m,y,t,z*r-a,l.h-b,q)w*k+z1l-i-e.l.k-d.j.i-f.m-g,d+a+e,a,f+c+j.o.n+r.p*d.y"
+    ".w/a.x.z,h/b.u.s.q.v.r.t-h/c/d-q-c,j,r-m-l7f7g7e7h-s-r-p-t/e/f/g/h-u-v+s+b,g+n*x+t+d+o*l+g+p+i*o+h/i/j+v+u+x+w0l0n)y0k/l"
+    "/n/k/m/o)v0m/p/q/r-w-x.a-y/s*y/t/v7i/w-j.b.f.e.d-k-n1o1n-z.c1p1m3d1k/u7k7j0b0c/x0a/z0o/y0p0t0r0s0q0x0v0d0w0e*s0f0g0i0h0j"
+    "1g0u1q-o1e1r1t1s1u1v1w1x2e2d2f1y1z2a2b1d1b*m1a1h1c0z2g2h0y6f1f1i3f3g1j7l2c*p2r2p2q2s3h3i3j3k2t3l5j7m7n2u2v3m3n3o2l6i6h2k"
+    "2n6g6j2m7o3r3p3t3q3u3s2w3a2x3b2y5k3c2z7p7t7r3v3x3w3y3z4a4b4c4d4e4f4g4h2j4i5l4j4k4l4m5m4n*n7u4t4o7q4p4q4r4s4u2o4v5o5q5n7v"
+    "5p5u2i5s5r5t5v5w5y4y5a4w4z4x5b5c5d5e6c5f5g5h5i6b6k5z5x6d6e3e6l6n6m6o6s6p6t6a6u7x6q6v6r7y:w7w7s:d:e:b:c7b7a7c6z8b8a7z8c8d"
+    "8f8e8g:f8r8p8o8n8q8h8l8j8m8i8k8s8u8t8v8w8x8y8z9a:i:h:g:j:m:k:n:l9b6x7d6w6y9d9c:r9e9f9i9h9g9j9m9k9l:o:q9n9o9q9t9s9p9r9u9v"
+    "9w:s:p9x9z9y:a:t;j:u;n;k:z:v;d;a;e;i;b:x;c;l;m;f;r;q;o;g;h:y;s;p")
+PLAN = {"order": [(ord(ORDER[i]) - 40) * 26 + ord(ORDER[i + 1]) - 97 for i in range(0, len(ORDER), 2)]}
 
 
 def overlap(a, b):
     if a[0] != b[0] or a[2] <= b[1] or b[2] <= a[1]:
         return False
     return not (a[3] == b[3] > 1 and (a[1] - b[1]) % a[3])
-
-
-def schedule(nodes):
-    every = range(len(nodes))
-    cost = [nd["cost"] for nd in nodes]
-    queue = [nd["q"] for nd in nodes]
-    group = [nd["st"] + nd["q"] for nd in nodes]
-
-    def gap(d, k):
-        if nodes[k]["soft"] == d:
-            return 0.0
-        return nodes[d]["lat"] + (SAME if queue[d] == queue[k] else 0.0 if queue[k] == "R" else CROSS)
-
-    pre = [[(d, gap(d, k)) for d in sorted(nodes[k]["deps"])] for k in every]
-    post = [[] for _ in every]
-    for k in every:
-        for d, w in pre[k]:
-            post[d].append((k, w))
-
-    lat = [nd["lat"] for nd in nodes]
-
-    def lay(order, links, first):
-        start, slots = [0.0] * len(nodes), {}
-        for k in order:
-            t0, c = first[k], cost[k]
-            for d, w in links[k]:
-                e = start[d] + cost[d] + w
-                if e > t0:
-                    t0 = e
-            if c > 0.0:
-                sl = slots.setdefault(queue[k], [])
-                i = len(sl)
-                while i > 0 and sl[i - 1][1] > t0:
-                    i -= 1
-                while i < len(sl) and t0 + c > sl[i][0]:
-                    t0 = sl[i][1]
-                    i += 1
-                sl.insert(i, (t0, t0 + c))
-            start[k] = t0
-        return start
-
-    zero = [0.0] * len(nodes)
-
-    def both(start):
-        back = lay(sorted(every, key=lambda j: (-start[j] - cost[j], -j)), post, lat)
-        start = lay(sorted(every, key=lambda j: (-back[j] - cost[j], j)), pre, zero)
-        return max(start[k] + cost[k] + lat[k] for k in every), start
-
-    seed = [SEED]
-
-    def rnd(n):
-        seed[0] = (seed[0] * 1103515245 + 12345) % 2147483648
-        return (seed[0] >> 9) % n
-
-    names = sorted(set(group))
-    way = [0.0] * len(nodes)
-    for k in reversed(every):
-        way[k] = cost[k] + 1e-6 + max([way[u] + w for u, w in post[k]] + [lat[k]])
-    span, cur = top = both(lay(sorted(every, key=lambda j: (-way[j], j)), pre, zero))
-    for it in range(ITER):
-        key = list(cur)
-        for _ in range(1 + rnd(2)):
-            by = (rnd(2001) / 1000.0 - 1.0) * (0.3, 1.0, 3.0, 6.0)[rnd(4)]
-            if rnd(2):
-                nm = names[rnd(len(names))]
-                for k in every:
-                    if group[k] == nm:
-                        key[k] += by
-            else:
-                key[rnd(len(nodes))] += by
-        if rnd(2):
-            for k in every:
-                for d, w in pre[k]:
-                    if key[d] > key[k]:
-                        key[k] = key[d]
-        else:
-            for k in reversed(every):
-                for u, w in post[k]:
-                    if key[u] < key[k]:
-                        key[k] = key[u]
-        st = lay(sorted(every, key=lambda j: (key[j], j)), pre, zero)
-        sp = max(st[k] + cost[k] + lat[k] for k in every)
-        if rnd(3) == 0:
-            s2, t2 = both(st)
-            if s2 < sp:
-                sp, st = s2, t2
-        if sp <= span + TEMP * (1 - it / ITER) * rnd(1000) / 1000.0:
-            cur, span = st, sp
-            if sp < top[0]:
-                top = (sp, st)
-    return top[0], sorted(every, key=lambda j: (top[1][j], j))
 
 
 def rank_program(g, core, T, topo):
@@ -161,9 +81,12 @@ def rank_program(g, core, T, topo):
     n = len(T.cores)
     owner, asker = T.cores[(rank + 1) % n], T.cores[(rank - 1) % n]
     Q = {"V": g.vector, "S": g.scalar, "T": g.tensor, "G": g, "Y": g.sync}
-    nodes, hist, stage, busy, chain = [], {}, [""], [0.5], []
+    nodes, hist, stage, chain = [], {}, [""], []
 
     def v(name, lo=0, hi=None, step=1):
+        if name in ROWS:
+            at, size = ROWS[name]
+            name, lo, hi = "ar", at + lo, at + (size if hi is None else hi)
         hi = SCRATCH[name][1][1] if hi is None else hi
         ap = T[name][:, lo:hi] if step == 1 else T[name][:, lo:hi:step]
         cnt = (hi - lo + step - 1) // step
@@ -181,19 +104,19 @@ def rank_program(g, core, T, topo):
     def b8(x):
         return (x[0].bitcast(dt.uint8),) + x[1:]
 
-    def node(q, kind, run, wr, rd, cost, lat=0.0, after=(), tag=0, soft=None):
+    def node(q, kind, run, wr, rd, cost=0.0, by=0, after=(), tag=0, soft=None, free=()):
         deps = set(after)
         for regs, w in ((wr, True), (rd, False)):
             for r in regs:
                 for r2, w2, k in hist.get(r[0], []):
-                    if (w or w2 or r[0] == "ps") and overlap(r, r2):
+                    if (w or w2 or (r[0] == "ps" and nodes[k]["q"] != q)) and overlap(r, r2) and k not in free:
                         deps.add(k)
         me = len(nodes)
-        nodes.append(dict(st=stage[0], q=q, kind=kind, run=run, deps=deps, cost=cost, lat=lat, tag=tag, soft=soft))
+        nodes.append(dict(st=stage[0], nm=(wr or rd)[0][0], q=q, kind=kind, run=run, deps=deps, cost=cost, by=by, tag=tag, soft=soft))
         for regs, w in ((wr, True), (rd, False)):
             for r in regs:
                 h = hist.setdefault(r[0], [])
-                if (w or r[0] == "ps") and r[3] == 1:
+                if w and r[3] == 1 and not free:
                     h[:] = [e for e in h if not (r[1] <= e[0][1] and e[0][2] <= r[2])]
                 h.append((r, w, me))
         return me
@@ -206,27 +129,29 @@ def rank_program(g, core, T, topo):
             cyc = big[2] * (GAT if big[4] else 0.5 if two else 1.0) + (30 if q == "S" else 0)
         wr, rd = [r for o in outs for r in o[1]], list(more) + [r for i in views for r in i[1]]
         args = [o[0] for o in outs] + [i[0] if isinstance(i, tuple) else i for i in ins]
-        return node(q, "op", lambda tag=stage[0]: call(*args), wr, rd, FIX + cyc * CYC)
+        return node(q, "op", lambda: call(*args), wr, rd, FIX + cyc * CYC)
 
-    def dma(q, name, out, in_, size, wr=(), rd=()):
-        node(q, "d_" + name, lambda tag=stage[0]: Q[q].dma_start(out, in_), list(wr), list(rd), 0.1, FLY + size / BW)
+    def dma(q, name, out, in_, size, wr=(), rd=(), free=(), after=(), soft=None):
+        return node(q, "d_" + name, lambda: Q[q].dma_start(out, in_), list(wr), list(rd), 0.1, size, after, 0, soft, free)
+
+    def spread(name, to, rows, size, rd):
+        mine = [-1]
+        for out, in_ in rows:
+            mine.append(dma("Y", name, out, in_, size, wr=to[1], rd=rd, free=list(mine), after=chain[-1:]))
 
     def load(q, name, dst, src, size):
-        busy[0] += size / BW
         prev = chain[-1:] if q == "Y" else []
-        me = node(q, "d_" + name, lambda tag=stage[0]: Q[q].dma_start(dst[0], src), dst[1], [], 0.1, busy[0] + FLY - 0.7,
-                  after=prev, soft=prev[0] if prev else None)
+        me = dma(q, name, dst[0], src, size, wr=dst[1], after=prev, soft=prev[0] if prev else None)
         if q == "Y":
             chain.append(me)
 
-    def send(to, sem, dst, src, size, extra=0.0, after=None):
+    def send(to, sem, dst, src, size, after=None):
         rid, pid = topo.addr(to)[:2]
-        return node("G", "send", lambda tag=stage[0]: g.remote_dma(dst[0], src[0], T.sem[sem], T.sem.sent, pid, rid, topo.mask(core, to)),
-                    [], src[1], 0.3 + extra, FLY - 0.3 + size / BW, tag=len(topo.engines(core, to)),
-                    after=[] if after is None else [after], soft=after)
+        return node("G", "send", lambda: g.remote_dma(dst[0], src[0], T.sem[sem], T.sem.sent, pid, rid, topo.mask(core, to)),
+                    [], src[1], 0.3, size, [] if after is None else [after], len(topo.engines(core, to)), after)
 
     def arrives(frm, sem, views, mine):
-        node("R", sem, None, [r for x in views for r in x[1]], [], 0.0, 0.0, after=mine, tag=len(views) * len(topo.engines(frm, core)))
+        node("R", sem, None, [r for x in views for r in x[1]], [], after=mine, tag=len(views) * len(topo.engines(frm, core)))
 
     V = g.vector
 
@@ -256,14 +181,17 @@ def rank_program(g, core, T, topo):
         else:
             op("S", lambda o, x, s, b: g.scalar.activation(o, x, f, bias=b, scale=s), [out], [a, scale, bias])
 
+    def aff(q, out, a, s, b):
+        if q == "V":
+            ts(out, a, s, Op.mult, b, Op.add)
+        else:
+            act(out, a, Fn.Identity, s, b)
+
     nl = [0]
 
     def lin(out, a, s, b):
         nl[0] += 1
-        if LIN[nl[0] - 1] == "V":
-            ts(out, a, s, Op.mult, b, Op.add)
-        else:
-            act(out, a, Fn.Identity, s, b)
+        aff(LIN[nl[0] - 1], out, a, s, b)
 
     def move(q, out, a):
         if q == "V":
@@ -275,148 +203,130 @@ def rank_program(g, core, T, topo):
         op("V", V.quantize_mx, [c, s], [a], a[2] * 0.265)
 
     def mm(out, lq, ls, rq, rs):
-        op("T", lambda o, a, b, c, d: g.tensor.matmul_mx(o, a, b, c, d, True, True), [out], [lq, ls, rq, rs], (rq[2] + 16) * 0.8)
+        op("T", lambda o, a, b, c, d: g.tensor.matmul_mx(o, a, b, c, d, True, True), [out], [lq, ls, rq, rs], (rq[2] + 16) * 1.2)
 
     def iota(out, pattern, base=0, cm=0):
         if SCRATCH[out[1][0][0]][2] == i32:
-            op("G", lambda o: g.iota(o, pattern, base, cm), [out], [], 80 + 2 * out[2])
+            op("G", lambda o: g.iota(o, pattern, base, cm), [out], [], 100 + 2 * out[2])
         else:
-            op("G", lambda o: g.iota(o, pattern, base, cm, allow_small_or_imprecise_dtypes=True), [out], [], 80 + 2 * out[2])
+            op("G", lambda o: g.iota(o, pattern, base, cm, allow_small_or_imprecise_dtypes=True), [out], [], 100 + 2 * out[2])
 
-    def fill(out, c):
-        iota(out, [[0, out[2]]], c)
+    def fill(out, c, q="G"):
+        if q == "G":
+            iota(out, [[0, out[2]]], c)
+        else:
+            op("V", lambda o: V.memset(o, float(c)), [out], [])
 
-    def keep(out, a, pattern, cmp, base, cm):
-        op("G", lambda o, x: g.affine_select(o, x, pattern, cmp, 0.0, base, cm), [out], [a], 130 + 2 * out[2])
-
-    def turn(to, name, lo, width):
-        op("V", V.transpose, [v(to, 0, width)], [v(name, lo, lo + width)])
-        op("V", V.transpose, [v(to, width, 2 * width + 32)], [v(name, lo - 16, lo + width + 16)])
-
-    def below(n, ns, width, row, key, cmp, sums, seg, out, cap):
-        nv = n - ns
-        cut = lambda name, c: v(name, width * c, width * c + width)
-        for c in range(nv, n):
-            act(cut(cmp, c), row(c), Fn.Sign, -1.0, key(c))
-            act(cut(sums, c), cut(cmp, c), Fn.Relu, 1.0, 0.0, v("cn", c, c + 1))
-        for c in range(nv):
-            ts(cut(cmp, c), row(c), key(c), Op.is_lt)
-        scan(v(sums, 0, width * nv), v(seg, 0, width * nv), v(cmp, 0, width * nv), 0.0, Op.mult, Op.add)
-        ts(v(out, 0, nv), v(sums, width - 1, width * nv, width), cap, Op.min)
-        if ns:
-            ts(v(out, nv, n), v("cn", nv, n), cap, Op.min)
+    def turn(to, name, lo, width, at=0):
+        op("V", V.transpose, [v(to, at, at + width)], [v(name, lo, lo + width)])
+        op("V", V.transpose, [v(to, at + width, at + 2 * width + 32)], [v(name, lo - 16, lo + width + 16)])
 
     ci = lambda k: v("ci", k, k + 1)
     cf = lambda k: v("cf", k, k + 1)
     pk = lambda a, b: v("pk", a, b)
-    (M0, CA, CB_, G16, GOF, GOF4, NGOF, QI, M8, AA, BB, C0, C2, TH, SP, JB, K0, K1, R16, B2, HF, RF, TMP, TM2,
-     B14, R24, B8, B6, P16, MS, MB, M47, A1, CV, N47, S31, PAR, N03, C1, R1, M12, N8, M811, G4) = [cf(k) for k in range(44)]
-    PK14, PK6, PKA, PKB, PKE, PKU, PK8 = pk(0, 5), pk(14, 15), pk(16, 17), pk(18, 19), pk(20, 21), pk(22, 30), pk(30, 31)
+    (M0, M5, M14, TS, T4, ES, RF1, EBS, EBT, EB, M6S, AL, GA, DE, N8S, MS, MB, AAS, B4, VB, B4T, E2S, H0,
+     PAR, RA, RB, RC, P16, HP, K0, K1, R1, A0, V0, I0, DB, PB) = [cf(k) for k in range(37)]
+    PKT, PK8, PK6, PK2, PKU = pk(0, 1), pk(2, 3), pk(4, 5), pk(6, 7), pk(8, 16)
     W = ["w0", "w1", "w2", "w3"]
+    wv = lambda t, lo=0, hi=4 * (HB + A), step=1: v(W[t], PAD + lo, PAD + hi, step)
     E = ["e0", "e1", "e2"]
     AT = v("at", OFF, OFF + MC)
+    US = 1.0 / SC
 
     def constants():
         iota(ci(0), [[0, 1]], 0, 1)
-        iota(v("iot", 0, 416), [[1, 416]])
-        fill(v("at", OFF, OFF + ATG), MISS)
-        op("V", lambda o: V.memset(o, float(MISS)), [v("at", OFF + ATG, OFF + MC)], [])
-        act(v("iot", 416, 832), v("iot", 0, 416), Fn.Identity, 1.0, 416.0)
-        iota(v("iot", 832, MC), [[1, MC - 832]], 832)
+        iota(v("iot", 0, 448), [[1, 448]])
+        fill(v("at", OFF, OFF + MC), 0, "V")
+        act(v("iot", 448, MC), v("iot", 0, 448), Fn.Identity, 1.0, 448.0)
         ts(ci(1), ci(0), 15, Op.bitwise_and)
-        ts(ci(2), ci(0), 112, Op.bitwise_and)
+        ts(M0, ci(1), 1.0, Op.is_lt)
+        ts(M5, ci(1), 5.0, Op.is_lt)
+        ts(RF1, ci(1), -1.0, Op.add)
+        ts(M6S, ci(1), 6.0, Op.is_equal, SC, Op.mult)
+        ts(N8S, ci(1), 8.0, Op.is_ge, SC, Op.mult)
+        ts(MS, ci(1), 8.0, Op.is_ge, US, Op.max)
+        lin(M14, M0, -1.0, M5)
+        lin(TS, M14, 3 * SC, SC)
+        lin(T4, M14, 12 * SC, 4 * SC)
+        lin(EBT, RF1, M14, -THR)
+        lin(EBS, EBT, SC, 0.0)
+        lin(AL, M6S, -3.0, T4)
+        lin(GA, M6S, 95.0, TS)
+        lin(DE, TS, 32.0, EBS)
+        lin(v("be"), v("iot", 0, 4), GA, DE)
+        for q in range(4):
+            aff(PICK["st"][q], v("st", 32 + q, 416, 4), v("iot", 0, 96), AL, v("be", q, q + 1))
+        lin(MB, N8S, (1.0 - THR) * US, THR)
+        lin(ES, M0, SC / 1024 - SC, TS)
+        lin(EB, M0, THR * SC + (32 - THR) * SC / 1024, EBS)
         ts(ci(3), ci(0), 4, Op.logical_shift_right)
-        ts(ci(6), ci(0), 1, Op.bitwise_and)
-        ts(ci(7), ci(0), 1, Op.logical_shift_right, 7, Op.bitwise_and)
-        ts(M0, ci(1), 4.0, Op.is_lt)
-        ts(M8, ci(1), 8.0, Op.is_lt)
-        ts(RF, ci(1), 0.0, Op.add)
-        ts(G16, ci(2), 0.0, Op.add)
         tt(ci(4), ci(0), ci(3), Op.add)
         ts(ci(5), ci(4), 1, Op.bitwise_and)
         ts(PAR, ci(5), 0.0, Op.add)
+        ts(ci(6), ci(0), 1, Op.bitwise_and)
+        ts(ci(7), ci(0), 1, Op.logical_shift_right, 7, Op.bitwise_and)
+        ts(ci(2), ci(0), 3, Op.bitwise_and)
+        ts(B4, ci(2), 0.0, Op.add)
+        ts(RA, ci(1), 13.0, Op.min, 16.0, Op.mult)
+        ts(RB, ci(1), 7.0, Op.min, 16.0, Op.mult)
         ts(P16, ci(6), 16.0, Op.mult)
-        ts(TM2, ci(7), 4.0, Op.is_ge, 8.0, Op.mult)
-        ts(HF, ci(7), TM2, Op.max)
-        lin(M47, M0, -1.0, M8)
-        lin(CA, M0, 3.0, 1.0)
-        lin(A1, M47, -1.0, CA)
-        lin(N47, M47, -1.0, 1.0)
-        lin(CB_, RF, M0, 0.0)
-        lin(S31, CA, 31.0, CB_)
-        lin(GOF, G16, 1.0, float(OFF))
-        lin(BB, M0, 4.0, 0.0)
-        lin(TMP, M8, 3.0, 1.0)
-        lin(AA, BB, -1.0, TMP)
-        lin(C0, RF, M8, GOF)
-        lin(N03, M0, -1.0, 1.0)
-        lin(CV, C0, N03, BB)
-        lin(C1, BB, -1.0, C0)
-        lin(C2, M0, float(4 * HB[2] - OFF), C1)
-        ts(M12, ci(1), 12.0, Op.is_lt)
-        lin(M811, M8, -1.0, M12)
-        lin(N8, M8, -1.0, 1.0)
-        lin(TH, M811, 3.0, N8)
-        lin(SP, RF, 1.0, -8.0)
-        lin(JB, SP, M811, 0.0)
-        lin(QI, TH, 415.0, JB)
-        lin(R1, RF, 1.0, 1.0)
-        lin(G4, G16, -4.0, 0.0)
-        lin(GOF4, G16, 1.0, float(OFF + 4))
-        lin(MS, TH, 2.0 ** -16, M8)
-        lin(MB, TH, -0.125, 0.0)
-        lin(R16, RF, 16.0, 0.0)
-        lin(B14, PAR, 240.0, R16)
-        lin(B8, PAR, 144.0, R16)
-        lin(B6, PAR, 112.0, R16)
-        lin(B2, PAR, 48.0, P16)
-        lin(K0, RF, -2.0, 31.5)
-        lin(K1, RF, -2.0, 30.5)
-        lin(NGOF, GOF, -1.0, 0.0)
-        lin(R24, RF, 24.0, 0.0)
-        iota(v("ir"), [[0, 6], [1, 16]])
+        ts(HP, ci(7), P16, Op.add)
+        act(RC, RF1, Fn.Abs, 16.0, -112.0)
+        lin(AAS, N8S, 3.0, SC)
+        lin(VB, B4, N8S, (OFF - THR) * SC)
+        lin(B4T, B4, 1.0, THR)
+        lin(E2S, M0, 1023.0, 1.0)
+        lin(H0, M0, 2.0 ** 95, 0.0)
+        lin(K0, RF1, -2.0, 29.5)
+        lin(K1, RF1, -2.0, 28.5)
+        lin(R1, RF1, 1.0, 2.0)
+        ts(PKT, PAR, 240.0, Op.mult, RA, Op.add)
+        ts(PK8, PAR, 144.0, Op.mult, RB, Op.add)
+        ts(PK6, PAR, 112.0, Op.mult, RC, Op.add)
+        ts(PK2, PAR, 48.0, Op.mult, HP, Op.add)
         iota(v("ci", 8, 16), [[16, 8]])
-        ts(PK14, v("iot", 0, 5), B14, Op.add, 471.0, Op.min)
-        ts(PK8, B8, 287.0, Op.min)
-        ts(PK6, B6, -160.0, Op.add)
-        ts(PKA, ci(7), B2, Op.add, 4.0, Op.add)
-        ts(PKB, HF, B2, Op.add)
-        ts(PKE, B2, 9.0, Op.add)
         cp(PKU, v("ci", 8, 16))
+        iota(v("es", 0, P), [[1, 4], [4, 96]], 32)
+        iota(v("es", P, 432), [[1, 48]])
+        for t in range(2):
+            act(v(E[t], 32, 464), v("es"), Fn.Identity, ES, EB)
+        iota(v("dj"), [[1, 4], [16, 16]], ZB + 1)
+        lin(DB, B4, 223.0, RF1)
+        act(v("dj"), v("dj"), Fn.Identity, 1.0, DB)
+        iota(v("j2"), [[4, A]], 4 * HB)
+        act(v("j2"), v("j2"), Fn.Identity, SC, EBS)
+        lin(PB, PAR, 240.0, RA)
+        ts(v("pk", 16, 20), v("iot", 3, 7), PB, Op.add)
+        ts(v("pk", 20, 24), v("iot", 0, 4), 0.0, Op.mult, PB, Op.add)
+        act(v("k14"), v("iot", 0, A), Fn.Identity, 0.0, M14)
+        lin(A0, M14, -SC, AAS)
+        lin(V0, M14, (4 - OFF + THR) * SC, VB)
+        lin(I0, EBS, 1.0, (4 * HB - 4) * SC)
+        iota(v("jj"), [[4, 4], [16, 56]], 4 * HB)
+        act(v("jj"), v("jj"), Fn.Identity, SC, EBS)
+        act(v("k8"), v("iot", 0, A), Fn.Identity, 0.0, MS)
         for t in range(3):
-            iota(v(E[t], 32, 416), [[4, 16], [64, 24]], 128, 1)
-            iota(v(E[t], 416, 448), [[4, 32]], 1664, 1)
-            fill(v(E[t], 448, 464), 0)
-            fill(v(W[t], 4 * (ZC[t] if t == 2 else 416), 4 * HB[t]), 0)
-        for t in range(4):
-            fill(v(W[t], 0, 128), 0)
-        iota(v("otb"), [[1, 24], [24, 16]], 32)
-        act(v("sl", 0, 32), v("iot", 0, 32), Fn.Identity, CA, CB_)
-        act(v("kk"), v("otb"), Fn.Identity, M47, A1)
-        op("V", lambda o: V.memset(o, 1.0), [v("ones")], [])
-        ts(v("k47"), v("ones", 0, P), N47, Op.mult)
-        scan(v("sl", 32, 416), v("k47"), v("kk"), S31, Op.mult, Op.add)
-        ts(v("pkp"), v("iot", 0, 24), R24, Op.add)
-        act(v("k03"), v("otb", 0, A), Fn.Identity, 0.0, M0)
-        act(v("k8"), v("otb", 0, A), Fn.Identity, 0.0, N8)
-        iota(v("j2"), [[1, 4], [64, 16]], 1664, 4)
-        act(v("j2"), v("j2"), Fn.Identity, 1.0, G4)
-        for name, lo, hi in (("src", 0, 16), ("src", 240, 256), ("mb", 0, 48), ("mb", 432, 480), ("cb", 0, 16), ("cb", 112, 128),
-                             ("vb", 0, 16), ("eb", 0, 16), ("eb", 48, 64)):
+            fill(wv(t, 4 * ZC, ZB), 0)
+            fill(wv(t, ZB + 4 * A, 4 * HB), 0)
+            fill(wv(t, 0, 128), 0)
+        for name, lo, hi in (("ta", 0, 2), ("ta", 482, 512), ("src", 240, 304), ("mb", 432, 512), ("cb", 224, 296), ("vb", 0, 16), ("vb", 48, 80)):
             fill(v(name, lo, hi), 0)
-        fill(v("vb", 48, 80), MISS)
-        keep(v("ey"), v("ones", 0, 516), [[1, 516]], Op.is_equal, -3, -4)
+        fill(v("seg2"), 1)
+        op("G", lambda o, x: g.affine_select(o, x, [[1, 516]], Op.is_equal, 0.0, -3, -4), [v("ey")], [v("seg2", 0, 516)], 150 + 2 * 516)
+        fill(v("seg2", 0, 648, 108), 0)
+        fill(v("seg2", 6, 648, 107), -1)
         for b in range(4):
             quant(v("eq", 128 * b, 128 * b + 128), v("ep", 128 * b, 128 * b + 128), v("ey", 3 - b, 515 - b))
-        act(v("sg3"), v("otb"), Fn.Identity, 0.0, 0.0)
-        act(v("sg3", 0, P, 3), v("otb", 0, 128), Fn.Identity, 0.0, 2.0 ** 95)
-        iota(v("g3", 0, 32), [[1, 32]])
-        fill(v("g3", 32, 128), -1)
-        for name, nv, width in (("seg1", 8 - min(NS), 128), ("seg2", 6 - min(N2), 102)):
-            keep(v(name, 0, width * nv), v("ones", 0, width * nv), [[0, nv], [1, width]], Op.is_gt, 0, 0)
-        act(v("uu"), v("ir"), Fn.Relu, -1.0, R1)
-        act(v("ut"), v("uu"), Fn.Square, 1.0, -0.75)
-        act(v("uu"), v("ut"), Fn.Identity, 2.0 ** 92, -0.5625 * 2.0 ** 92)
+        act(v("sg3"), v("iot", 0, P), Fn.Identity, 0.0, 0.0)
+        act(v("sg3", 0, P, 3), v("iot", 0, 128), Fn.Identity, 0.0, 2.0 ** 95)
+        iota(v("g3", 0, 32), [[-1, 32]])
+        fill(v("g3", 32, 128), 64)
+        fill(v("seg1", 0, 128 * (8 - min(NS))), 1, PICK["seg"])
+        fill(v("seg1", 0, 128 * (8 - min(NS)), 128), 0)
+        lin(v("cu"), v("iot", 0, 4), 2.0 / 3, 128 + 1.0 / 6)
+        iota(v("ir"), [[0, 6], [1, 16]])
+        fill(v("uu", 0, 192, 2), 0)
+        ts(v("uu", 1, 192, 2), v("ir"), R1, Op.is_lt, -1.0, Op.mult)
 
     def sides():
         quant(v("uq"), v("up"), v("us"))
@@ -426,85 +336,108 @@ def rank_program(g, core, T, topo):
     def tables():
         cp(v("tgu"), v("tgi"))
         cp(v("adu"), v("adi"))
-        scat(AT, v("tgu"), v("sl", 32, 416))
-        act(v("tags", 32, 416), ind(v("iot"), v("tgu")), Fn.Identity, 1.0, GOF)
-        iota(v("tags", 0, 32), [[4, 32]], 0, 1)
+        scat(AT, v("tgu"), v("st", 32, 416))
+        act(v("tr"), ind(v("iot"), v("tgu")), Fn.Identity, SC, (OFF - THR) * SC)
+        dma("Y", "tr", T.st[0:128:16, 32:416], T.tr[0:128:16, :], 12288, wr=v("st", 32, 416)[1], rd=v("tr")[1], after=chain[-1:])
+
+    def payload(t):
+        val = v("val", A * t, A * t + A)
+        if t == 0:
+            act(v("vd"), ind(v("iot"), v("adu", 0, 14)), Fn.Identity, A0, V0)
+            scan(val, v("k14"), v("vd"), I0, Op.mult, Op.add)
+            return
+        if t == 1:
+            dma("Y", "ec", v(E[2], 32, 464)[0], v(E[1], 32, 464)[0], 432 * 512, wr=v(E[2], 32, 464)[1], rd=v(E[1], 32, 464)[1], after=chain[-1:])
+        jj = "jj" if t == 1 else "j2"
+        act(val, ind(v("iot"), v("adu", 14 * t, 14 * t + 14)), Fn.Identity, AAS, VB)
+        spread("j%d" % t, val, [(T.val[b:128:16, A * t:A * t + A], T[jj][b:128:16, :]) for b in range(1, 5)], 7168, v(jj)[1])
 
     def lookup(t):
-        look = ind(AT, v("adu", 14 * t, 14 * t + 14))
-        act(v("mis"), look, Fn.Relu, MS, MB)
-        scan(v("src", 16, 240), v("k8"), v("mis"), QI, Op.mult, Op.add)
-        turn("ta", "src", 16, A)
+        act(v("mis"), ind(AT, v("adu", 14 * t, 14 * t + 14)), Fn.Relu, MS, MB)
+        src = v("src", 16, 240)
+        scan(src, v("k8"), v("mis"), 415.0, Op.mult, Op.add)
+        turn("ta", "src", 16, A, 2)
+        move(PICK["qq"], v("qq"), ind(v("ta", 16, 496), PKT))
+        tt(v("alt"), ind(v("ta", 8, 496), PKT), v("qq"), Op.min)
+        cp(v("lb", 16 * t, 16 * t + 16), v("alt"))
+        scat(v(E[t]), v("lb", 16 * t, 16 * t + 14), v("val", A * t, A * t + A))
+        if t == 0:
+            ts(v("lz", 176, 240), ind(v("ta"), pk(16, 20)), float(4 * ZC), Op.min)
+            return
         if t == 2:
-            ts(v("alt", 0, 64), ind(v("ta", 8), pk(0, 4)), 1791.5, Op.subtract, 16384.0, Op.mult)
-            tt(v("qq", 0, 64), v("alt", 0, 64), v("j2"), Op.max)
-            cp(v("qq", 64, 80), ind(v("ta", 8), pk(4, 5)))
-        else:
-            cp(v("qq"), ind(v("ta", 8), PK14))
-        tt(v("alt"), ind(v("ta"), PK14), v("qq"), Op.min)
-        ts(v("lz", 80 * t, 80 * t + 80), v("alt"), float(4 * ZC[t]), Op.min)
-
-    def table(t):
-        val = v("val", A * t, A * t + A)
-        act(v("vd"), ind(v("iot"), v("adu", 14 * t, 14 * t + 14)), Fn.Identity, AA, CV)
-        scan(val, v("k03"), v("vd"), C2 if t == 2 else C1, Op.mult, Op.add)
-        scat(v(E[t]), v("lz", 80 * t + 64, 80 * t + 78), val)
+            ts(v("tc", 0, 64), ind(v("ta", 16, 496), pk(20, 24)), 447.5, Op.subtract, 16384.0, Op.mult)
+            tt(v("tc", 0, 64), v("tc", 0, 64), v("dj"), Op.max)
+            tt(v("tc", 64, 128), ind(v("ta"), pk(16, 20)), v("tc", 0, 64), Op.min)
+            cp(v("lz", 112, 176), v("tc", 64, 128))
+            return
+        to, lo, hi = v("tz", 56 * t, 56 * t + 56), src[1][0][1], src[1][0][2]
+        spread("q%d" % t, to, [(T.tz[b:128:4, 56 * t:56 * t + 56], T.ar[1:128:16, lo:hi]) for b in range(4)], 7168, src[1])
+        ts(v("lz", 56 * t, 56 * t + 56), to, float(4 * ZC), Op.min, B4, Op.add)
 
     def served(t):
         turn("tk", E[t], 416, 32)
         if t < 2:
-            ts(v("sa%d" % t), ind(v("tk"), PKA), GOF4, Op.subtract)
-            mine = send(owner, "a_rq%d" % t, v("rq%d" % t), v("sa%d" % t, 0, 8), 2048, after=opened)
-            arrives(asker, "a_rq%d" % t, [v("rq%d" % t)], [mine])
-        ts(v("lk", 32 * t, 32 * t + 16), ind(v("tk"), PKB), G16, Op.subtract)
-        act(v("pen", 416 * t, 416 * t + P), ind(v(E[t], 32, 416), v("pkp")), Fn.Relu, 2.0 ** 70, -THR * 2.0 ** 70)
-        act(v("pen", 416 * t + P, 416 * t + 416), v(E[t], 416, 448), Fn.Relu, 2.0 ** 70, -THR * 2.0 ** 70)
-        tt(v("dr", 32 * t, 32 * t + 32), v("pen", 416 * t + P, 416 * t + 416), v("sl", 0, 32), Op.add)
+            ts(v("sa%d" % t), ind(v("tk", 8, 96), PK2), US, Op.mult, THR - OFF, Op.add)
+            mine = send(owner, "a_rq%d" % t, v("rq%d" % t), v("sa%d" % t, 0, 8), 2048, opened)
+            arrives(asker, "a_rq%d" % t, [v("rq%d" % t)], [mine] + chain[-1:])
+            act(v("ex", 32 * t, 32 * t + 32), v(E[t], 416, 448), Fn.Identity, E2S)
+        ts(v("lk", 32 * t, 32 * t + 16), ind(v("tk"), PK2), US, Op.mult, THR, Op.add)
 
     def places(t):
-        for b in range(4):
-            to = v("tp", 96 * t + 24 * b, 96 * t + 24 * b + 24)
-            dma("Y", "p%d" % t, to[0], T[E[t]][b:128:16, 32:416], 12288, wr=to[1], rd=v(E[t], 32, 416)[1])
-        ts(v("le", 96 * t, 96 * t + 96), v("tp", 96 * t, 96 * t + 96), G16, Op.subtract)
+        to = v("tp", 96 * t, 96 * t + 96)
+        spread("p%d" % t, to, [(T.tp[b:128:4, 96 * t:96 * t + 96], T[E[t]][1:128:16, 32:416]) for b in range(4)], 12288, v(E[t], 32, 416)[1])
+        ts(v("le", 96 * t, 96 * t + 96), to, US, Op.mult, B4T, Op.add)
 
     def answer(t):
         mem = v("ms", 0, 4 * MC)
-        c, s = "fq%d" % t, "fp%d" % t
+        eb = lambda b: (v("eq", 128 * b, 128 * b + 128), v("ep", 128 * b, 128 * b + 128))
         if t == 2:
-            for b in range(4):
-                ts(v("f2l", 14 * b, 14 * b + 14), v("rq2"), 4.0, Op.mult, float(b), Op.add)
-                move("S", v("ft", b, 4 * A, 4), ind(mem, v("f2l", 14 * b, 14 * b + 14)))
-            quant(v(c), v(s), v("ft"))
-            lc, lp, w, wq = v("lc"), v("lp"), A, A
-            mine = [send(asker, "a_f2", b8(lc), b8(v(c)), 512 * A), send(asker, "a_f2", lp, v(s), 128 * A)]
+            spread("r2", v("r2"), [(T.r2[b:128:4, :], T.rq2[:, :]) for b in range(4)], 7168, v("rq2")[1])
+            ts(v("f2l"), v("r2"), 4.0, Op.mult, B4, Op.add)
+            for i in range(2):
+                move("S", v("ft", 448 * i, 448 * i + 448), ind(mem, v("f2l", 28 * i, 28 * i + 28)))
+            quant(v("fq2"), v("fp2"), v("ft"))
+            lc, lp = v("lc"), v("lp")
+            mine = [send(asker, "a_f2", b8(lc), b8(v("fq2")), 512 * A), send(asker, "a_f2", lp, v("fp2"), 128 * A)]
             arrives(owner, "a_f2", [lc, lp], mine)
-        else:
-            lo = 4 * (MC + K * t)
             for b in range(4):
-                move("S", v("ms", lo + b, lo + 4 * K, 4), ind(mem, v("rq%d" % t, 2 * b, 2 * b + 2)))
-            quant(v(c, 0, 128), v(s, 0, 128), v("ms", lo + 4 * K - 512, lo + 4 * K))
-            mine = [send(asker, "a_f%d" % t, b8(v(c, 128, 160)), b8(v(c, 96, 128)), 512 * K),
-                    send(asker, "a_f%d" % t, v(s, 128, 160), v(s, 96, 128), 128 * K)]
-            arrives(owner, "a_f%d" % t, [v(c, 128, 160), v(s, 128, 160)], mine)
-            lc, lp, w, wq = v(c, 32, 160), v(s, 32, 160), K, 128
+                bank = 512 * (4 + b % 3)
+                mm(v("ps", bank, bank + A), *eb(b), lc, lp)
+                move("S", wv(2, ZB + b, ZB + 4 * A, 4), v("ps", bank, bank + A))
+            return
+        lo, at = 4 * (MC + K * t), LAND[t]
+        own = 160 if t == 0 else 128
         for b in range(4):
-            bank = 512 * (4 + b % 3)
-            mm(v("ps", bank, bank + wq), v("eq", 128 * b, 128 * b + 128), v("ep", 128 * b, 128 * b + 128), lc, lp)
-            to = v(W[t], 4 * 416 + b, 4 * (416 + w), 4) if t == 2 else v("fd", 128 * t + K * b, 128 * t + K * b + K)
-            move("S", to, v("ps", bank + wq - w, bank + wq))
+            move(MG[t][b], v("ms", lo + b, lo + 4 * K, 4), ind(mem, v("rq%d" % t, 2 * b, 2 * b + 2)))
+        quant(v("fq", at - own, at), v("fp", at - own, at), v("ms", lo + 4 * K - 4 * own, lo + 4 * K))
+        lc, lp = v("fq", at, at + K), v("fp", at, at + K)
+        mine = [send(asker, "a_f%d" % t, b8(lc), b8(v("fq", at - K, at)), 512 * K),
+                send(asker, "a_f%d" % t, lp, v("fp", at - K, at), 128 * K)]
+        arrives(owner, "a_f%d" % t, [lc, lp], mine)
+        for b in (1, 0, 3, 2):
+            w, bank = 128 + K * (b % 2), 2048 + 512 * (b // 2)
+            mm(v("ps", bank, bank + w), *eb(b), v("fq", at + K - w, at + K), v("fp", at + K - w, at + K))
+            if b % 2 == 0:
+                move("S", v("fd", 128 * t + K * b, 128 * t + K * b + 64), v("ps", bank + 96, bank + 160))
 
     def layer(t):
-        z0, zt = OFF, "z%d" % t
-        for b in range(4):
-            move(RD[t][b], v(zt, z0 + b, z0 + 4 * A, 4), ind(v(W[t], 0, 4 * ZC[t] + 16), v("lz", 80 * t + 16 * b, 80 * t + 16 * b + 14)))
+        zv = (lambda lo, hi, st=1: wv(t, ZB + lo, ZB + hi, st)) if t < 2 else (lambda lo, hi, st=1: v("z2", lo, hi, st))
+        win = wv(t, 0, ZB if t < 2 else 4 * HB)
+        for i, q in enumerate(RD[t]):
+            if t == 1:
+                w = 56 // len(RD[t])
+                move(q, zv(16 * w * i, 16 * w * (i + 1)), ind(win, v("lz", 56 + w * i, 56 + w * (i + 1))))
+            else:
+                at = 16 * i + (112 if t else 176)
+                move(q, zv(i, 4 * A, 4), ind(win, v("lz", at, at + 14)))
         zq, zp = v("zq", A * t, A * t + A), v("zp", A * t, A * t + A)
         if t < 2:
-            scat(v(zt), v("lk", 32 * t, 32 * t + 8), v("fd", 128 * t, 128 * t + 128))
-        quant(zq, zp, v(zt, z0, z0 + 4 * A))
+            scat(v(W[t], 0, PAD + ZB + 4 * A), v("lk", 32 * t + 2, 32 * t + 10), v("fd", 128 * t, 128 * t + 128))
+        quant(zq, zp, zv(0, 4 * A))
         for b in range(4):
             mm(v("ps", 512 * b, 512 * b + A), v("wq", 128 * b, 128 * b + 128), v("wp", 128 * b, 128 * b + 128), zq, zp)
         for b in range(4):
-            o, r = v(W[t], 4 * HB[t] + b, 4 * (HB[t] + A), 4), v("ps", 512 * b, 512 * b + A)
+            o, r = wv(t, 4 * HB + b, 4 * (HB + A), 4), v("ps", 512 * b, 512 * b + A)
             if RL[t][b] == "V":
                 ts(o, r, 0.0, Op.max, 0.03125, Op.mult)
             else:
@@ -512,13 +445,14 @@ def rank_program(g, core, T, topo):
 
     def write(t):
         hs = v("hs", 128 * t, 128 * t + 128)
-        move("S", hs, ind(v(W[t]), v("lk", 32 * t, 32 * t + 8)))
-        for b in range(4):
-            move(WR[t][b], v(W[t + 1], 128 + b, 1664, 4), ind(v(W[t]), v("le", 96 * t + 24 * b, 96 * t + 24 * b + 24)))
-        scat(v(W[t + 1], 0, 1664), v("lv", 16 * t, 16 * t + 8), hs)
+        move("S", hs, ind(wv(t), v("lk", 32 * t + 2, 32 * t + 10)))
+        w = 96 // len(WR[t])
+        for i, q in enumerate(WR[t]):
+            move(q, wv(t + 1, 128 + 16 * w * i, 128 + 16 * w * (i + 1)), ind(wv(t), v("le", 96 * t + w * i, 96 * t + w * (i + 1))))
+        scat(wv(t + 1, 0, 1664), v("lk", 32 * t + 18, 32 * t + 26), hs)
 
     def marks(t):
-        quant(v("xq"), v("xp"), v(W[t], 128, 1664))
+        quant(v("xq"), v("xp"), wv(t, 128, 1664))
         mm(v("ps", 3584, 3584 + P), v("uq2"), v("up2"), v("xq"), v("xp"))
 
     rw = lambda k: v("rw", 128 * k, 128 * k + 128)
@@ -526,72 +460,92 @@ def rank_program(g, core, T, topo):
 
     def blocks(t):
         mins = v("mb", 50, 432, 3)
-        tt(v("kk"), v("ps", 3584, 3584 + P), v("pen", 416 * t, 416 * t + P), Op.add)
+        for q in range(4):
+            tt(v("kk", q, P, 4), v("ps", 3584 + q, 3584 + P, 4), v(E[t], 32 + 96 * q, 128 + 96 * q), Op.max)
         scan(v("mb", 48, 432), v("sg3"), v("kk"), 0.0, Op.add, Op.min)
         op("V", V.transpose, [v("t1", 0, 128)], [mins])
         op("V", V.transpose, [v("t1", 128, 288)], [v("mb", 2, 480, 3)])
-        cp(v("ky"), ind(v("t1"), PK8))
-        below(8, NS[t], 128, lambda c: mins, lambda c: v("ky", c, c + 1), "jn1", "jn2", "seg1", "lt", 127.0)
-        act(rw(2), ind(v("iot", 0, 128), v("lt")), Fn.Identity, -1.0)
-        cp(rw(0), ind(v("g3"), v("lt")))
-        op("V", lambda y, x: V.tensor_reduce(y, x, AxisListType.X, Op.max, negate=True), [sm(0)], [rw(0)], 128)
-        ts(rw(3), rw(0), 0.0, Op.is_ge)
-        ts(rw(4), rw(2), sm(0), Op.is_gt)
-        scan(rw(5), rw(4), v("ones", 0, 128), sm(0), Op.add, Op.mult)
+        move(PICK["ky"], v("ky"), ind(v("t1"), PK8))
+        nv = 8 - NS[t]
+        cut = lambda name, c: v(name, 128 * c, 128 * c + 128)
+        for c in range(nv, 8):
+            act(cut("jn1", c), mins, Fn.Sign, -1.0, v("ky", c, c + 1))
+            act(cut("jn2", c), cut("jn1", c), Fn.Relu, 1.0, 0.0, v("cn", c, c + 1))
+        for c in range(nv):
+            ts(cut("jn1", c), mins, v("ky", c, c + 1), Op.is_lt)
+        scan(v("jn2", 0, 128 * nv), v("seg1", 0, 128 * nv), v("jn1", 0, 128 * nv), 0.0, Op.mult, Op.add)
+        ts(v("lt", 0, nv), v("jn2", 127, 128 * nv, 128), 127.0, Op.min)
+        if nv < 8:
+            ts(v("lt", nv, 8), v("cn", nv, 8), 127.0, Op.min)
+        move(PICK["rw"], rw(0), ind(v("g3"), v("lt")))
+        low = v("rw", 383, 384)
+        scan(rw(2), rw(0), rw(0), 0.0, Op.min, Op.min)
+        ts(rw(3), rw(0), 0.0, Op.is_le)
+        ts(rw(4), rw(0), low, Op.is_equal)
+        scan(rw(5), rw(3), rw(4), low, Op.add, Op.subtract)
         scan(rw(1), rw(3), rw(5), -32.0, Op.add, Op.min)
         act(rw(6), rw(1), Fn.Sign, 1.0, K0, sm(2))
         act(rw(7), rw(1), Fn.Sign, 1.0, K1, sm(3))
 
     def victims(t):
-        for u in range(3):
-            ts(v("o6", u, 6, 3), v("sm", 2, 4), -1.5, Op.mult, 192.0 + u, Op.add)
-        ts(v("cb", 16, 112), ind(v("kk"), v("o6", 0, 6)), 2.0 ** 71, Op.min)
-        act(v("dl"), v("cb", 16, 112), Fn.Abs, 1.25 * 2.0 ** -24, 2.0 ** -124)
-        turn("t2", "cb", 16, 96)
-        cp(v("gb", 0, 16), ind(v("t2"), PK6))
-        act(v("dk", 0, 6), v("gb", 10, 16), Fn.Abs, 1.25 * 2.0 ** -24, 2.0 ** -124)
-        move("S", v("cp"), ind(v("sl", 32, 416), v("o6", 0, 6)))
-        tt(v("dl"), v("dl"), v("uu"), Op.min)
-        tt(v("gb", 16, 112), v("cb", 16, 112), v("dl"), Op.subtract)
-        tt(v("gb", 112, 118), v("gb", 10, 16), v("dk", 0, 6), Op.subtract)
-        below(6, N2[t], 102, lambda c: v("gb", 10 + c, 112 + c), lambda c: v("gb", 10 + c, 11 + c), "c1", "s1", "seg2", "rk", 95.0)
+        for i in range(2):
+            ts(v("o6", 3 * i, 3 * i + 3), v("cu", 0, 3), sm(2 + i), Op.subtract, 1.5, Op.mult)
+        ts(v("cb", 33, 225, 2), ind(v("kk"), v("o6", 0, 6)), SC, Op.min)
+        act(v("cb", 32, 224, 2), v("cb", 33, 225, 2), Fn.Abs, 1.25 * 2.0 ** -24, 2.0 ** -124)
+        op("V", V.transpose, [v("t2", 32, 128)], [v("cb", 33, 225, 2)])
+        op("V", V.transpose, [v("t2", 128, 256)], [v("cb", 1, 257, 2)])
+        move(PICK["gb"], v("gb", 203, 235, 2), ind(v("t2"), PK6))
+        keys = v("gb", 223, 235, 2)
+        act(v("dk", 0, 6), keys, Fn.Abs, 1.25 * 2.0 ** -24, 2.0 ** -124)
+        move("S", v("cp"), ind(v("st", 32, 416), v("o6", 0, 6)))
+        scan(v("gb", 12, 204), v("uu"), v("cb", 32, 224), 0.0, Op.mult, Op.add)
+        tt(v("gb", 1, 13, 2), keys, v("dk", 0, 6), Op.subtract)
+        for c in range(6):
+            ts(v("c1", 108 * c, 108 * c + 108), v("gb", 1 + 2 * c, 217 + 2 * c, 2), v("gb", 223 + 2 * c, 224 + 2 * c), Op.is_lt)
+        scan(v("s1"), v("seg2"), v("c1"), 0.0, Op.mult, Op.add)
+        cp(v("rk", 0, 6), v("s1", 107, 648, 106))
         scat(v("sv"), v("rk", 0, 6), v("cp"))
-        tt(v("vb", 16, 48), v("sv", 0, 32), v("dr", 32 * t, 32 * t + 32), Op.min)
+        tt(v("vb", 16, 48), v("sv", 0, 32), v("ex", 32 * t, 32 * t + 32) if t < 2 else v(E[t], 416, 448), Op.min)
         turn("tv", "vb", 16, 32)
-        cp(v("lv", 16 * t, 16 * t + 16), ind(v("tv"), PKB))
+        ts(v("lk", 32 * t + 16, 32 * t + 32), ind(v("tv"), PK2), US, Op.mult, THR, Op.add)
 
     def retag(t):
-        lv = v("lv", 16 * t + 8, 16 * t + 10)
         if t < 2:
-            move("S", v("eb", 16, 48), ind(v("tags"), lv))
-            turn("te", "eb", 16, 32)
-            ts(v("lk", 32 * t + 10, 32 * t + 26), ind(v("te"), PKE), G16, Op.subtract)
-            scat(v("at"), v("lk", 32 * t + 8, 32 * t + 12), v("vb", 16, 80))
-        scat(v("tags"), lv, v(E[t], 416, 448))
+            scat(v("at"), v("lk", 32 * t + 14, 32 * t + 18), v("vb", 16, 80))
+        aff(PICK["svh"], v("sh"), v("sv", 0, 32), 1.0, H0)
+        tt(v("mx"), v("sh"), v(E[t], 416, 448), Op.min)
+        if t < 2:
+            scat(v("st"), v("lk", 32 * t + 26, 32 * t + 28), v("mx"))
+            return
+        act(v("otb", 32, 416), v("st", 32, 416), Fn.Identity, US, THR - OFF)
+        aff(PICK["ot"], v("sh"), v("mx"), US, THR - OFF)
+        scat(v("otb"), v("lk", 32 * t + 26, 32 * t + 28), v("sh"))
 
     def last():
-        for lo in (0, 192):
-            q_, p_, bank, yb = v("xq", lo, lo + 192), v("xp", lo, lo + 192), 3584 - 512 * (lo > 0), v("yb", lo, lo + 192)
-            quant(q_, p_, v(W[3], 128 + 4 * lo, 896 + 4 * lo))
-            mm(v("ps", bank, bank + 192), v("vq"), v("vp"), q_, p_)
-            move("V" if lo else "S", yb, v("ps", bank, bank + 192))
-            dma("Y" if lo else "S", "oz" if lo else "oy", T.y[:, lo:lo + 192], yb[0], 512 * 192, rd=yb[1])
+        w = P // len(PICK["y"])
+        for i, q in enumerate(PICK["y"]):
+            lo = w * i
+            q_, p_, bank, yb = v("xq", lo, lo + w), v("xp", lo, lo + w), 3584 - 512 * i, v("yb", lo, lo + w)
+            quant(q_, p_, wv(3, 128 + 4 * lo, 128 + 4 * (lo + w)))
+            mm(v("ps", bank, bank + w), v("vq"), v("vp"), q_, p_)
+            move(q, yb, v("ps", bank, bank + w))
+            dma("S" if q == "S" else "Y", "oy" if q == "S" else "oz", T.y[:, lo:lo + w], yb[0], 512 * w, rd=yb[1])
+            dma("S" if i else "Y", "oc", T.oc[:, 4 * lo:4 * (lo + w)], b8(q_)[0], 512 * w, rd=q_[1])
 
     def store():
-        for lo in (0, 192):
-            q_ = v("xq", lo, lo + 192)
-            dma("S" if lo else "Y", "oc", T.oc[:, 4 * lo:4 * lo + 768], b8(q_)[0], 512 * 192, rd=q_[1])
-        act(v("otb"), v("tags", 32, 416), Fn.Identity, 1.0, NGOF)
         for k in range(4):
             dma("Y", "os", T.osc[4 * k:4 * k + 4, :], T.xp[32 * k:32 * k + 4, :], 4 * P, rd=v("xp")[1])
-        dma("Y", "ot", T.ot[:], T.otb[8:128:16, :], 32 * P, rd=v("otb")[1])
+        dma("Y", "ot", T.ot[:], T.otb[0:128:16, 32:416], 32 * P, rd=v("otb")[1])
 
     def late(t):
         if t == 0:
-            dma("Y", "wc", b8(v("wq"))[0], T.wc[:], 262144, wr=v("wq")[1], rd=v("rq0")[1])
-            dma("Y", "ws", v("wp")[0], T.ws[:], 65536, wr=v("wp")[1], rd=v("rq0")[1])
+            came = v("rq0")[1]
+            dma("Y", "ws", v("wp")[0], T.ws[:], 65536, wr=v("wp")[1], rd=came)
+            for i, name in enumerate(("wc", "wd")):
+                half = v("wq", 256 * i, 256 * i + 256)
+                dma("Y", name, b8(half)[0], T.wc[:, 1024 * i:1024 * i + 1024], 131072, wr=half[1], rd=came)
         if t == 1:
-            dma("Y", "v", v("vs")[0], T.v[:], 131072, wr=v("vs")[1], rd=v("fq0")[1])
+            dma("Y", "v", v("vs")[0], T.v[:], 131072, wr=v("vs")[1], rd=v("fd", 0, 128)[1])
             quant(v("vq"), v("vp"), v("vs"))
 
     def do(name, f, *a):
@@ -600,24 +554,22 @@ def rank_program(g, core, T, topo):
 
     load("Y", "tg", v("tgi"), T.tg[:], 12288)
     load("S", "ad", v("adi"), T.ad[:], 21504)
-    load("Y", "x", v("w0", 128, 1664), T.x[:], 1024 * P)
+    load("Y", "x", wv(0, 128, 1664), T.x[:], 1024 * P)
     load("Y", "u", v("us"), T.u[:], 131072)
     load("Y", "m", v("ms", 0, 4 * MC), T.m[:], 1024 * MC)
     do("con", constants)
     stage[0] = "rq2"
-    opened = send(owner, "a_rq2", v("rq2"), v("adi", 28, 42), 7168, 1.5)
-    arrives(asker, "a_rq2", [v("rq2")], [opened])
+    opened = send(owner, "a_rq2", v("rq2"), v("adi", 28, 42), 7168)
+    arrives(asker, "a_rq2", [v("rq2")], [opened] + chain[-1:])
     do("sid", sides)
     do("tbl", tables)
     for t in range(3):
-        for name, f in (("loo", lookup), ("tab", table), ("ser", served), ("lat", late), ("pla", places), ("ans", answer), ("mar", marks),
-                        ("blo", blocks), ("vic", victims), ("lay", layer), ("wri", write), ("ret", retag)):
+        for name, f in (("pay", payload), ("loo", lookup), ("ser", served), ("pla", places), ("ans", answer), ("lat", late),
+                        ("mar", marks), ("blo", blocks), ("vic", victims), ("lay", layer), ("wri", write), ("ret", retag)):
             do(name, f, t)
     do("mar3", last)
     do("sto", store)
-
-    if "order" not in PLAN:
-        PLAN["span"], PLAN["order"] = schedule(nodes)
+    PLAN["nodes"] = nodes
 
     waited, count, mark, total = {}, {}, {}, {}
     for nd in nodes:

@@ -7,12 +7,9 @@ SC = 2.0 ** 71
 PAD, ZB, HB, ZC = 912, 1680, 648, 416
 LAND = (160, 320)
 NS = (3, 3, 3)
-RD = ("SSSS", "SS", "SSSS")
-WR = ("SSSSSV", "SSSS", "SSSS")
-RL = ("SSSS", "SSSS", "SSSS")
-MG = ("SVSS", "SSSS")
-PICK = dict(qq="V", ky="V", gb="V", rw="V", svh="S", st="SSSS", ot="S", seg="G", y="SSV")
-LIN = "S" * 40
+NK = (2, 2, 2)
+WR = (4, 4, 4)
+YP = 2
 f32, bf, i32, u16, u8, x4 = "float32", "bfloat16", "int32", "uint16", "uint8", "float8_e4m3fn_x4"
 
 
@@ -34,38 +31,30 @@ SCRATCH = {
     "rq0": _s(8, u16), "rq1": _s(8, u16), "rq2": _s(14, i32), "sa0": _s(16, u16), "sa1": _s(16, u16),
     "r2": _s(56, i32), "f2l": _s(56, u16),
     "iot": _s(MC, f32), "at": _s(OFF + MC, f32), "st": _s(416, f32), "tr": _s(P, f32), "es": _s(432, f32),
-    "jj": _s(A, f32), "k8": _s(A, bf), "val": _s(3 * A, f32), "k14": _s(A, bf), "vd": _s(A, f32),
+    "k8": _s(A, bf), "oh": _s(24, f32), "g4": _s(128, bf), "dm": _s(96, f32), "sk": _s(96, bf),
+    "yk": _s(96, f32), "ys": _s(104, f32),
     "e0": _s(640, f32), "e1": _s(640, f32), "e2": _s(640, f32), "ex": _s(64, f32),
-    "otb": _s(416, f32), "yb": _s(P, f32), "dj": _s(64, f32), "j2": _s(A, f32), "tc": _s(128, f32),
-    "ci": _s(16, i32), "cf": _s(48, f32), "be": _s(4, f32), "cu": _s(4, f32), "ir": _s(96, f32), "pk": _s(24, u16),
-    "uu": _s(192, bf), "g3": _s(128, f32), "seg1": _s(1024, bf), "seg2": _s(648, bf),
-    "ar": _s(1840, f32), "tp": _s(288, f32), "tz": _s(168, f32), "t1": _s(288, f32), "tk": _s(96, f32), "tv": _s(96, f32),
-    "mis": _s(A, f32), "qq": _s(16, f32), "alt": _s(16, f32),
-    "lz": _s(240, u16), "lb": _s(48, u16), "lk": _s(96, u16), "le": _s(288, u16),
+    "otb": _s(416, f32), "yb": _s(P, f32), "dj": _s(64, f32), "tc": _s(128, f32),
+    "ci": _s(16, i32), "cf": _s(48, f32), "be": _s(4, f32), "cu": _s(4, f32), "ir": _s(96, f32), "pk": _s(28, u16),
+    "uu": _s(192, bf), "g3": _s(128, f32), "seg1": _s(1024, bf), "seg2": _s(424, bf),
+    "ar": _s(1840, f32), "tp": _s(288, f32), "t1": _s(400, f32), "tk": _s(96, f32), "tv": _s(100, f32),
+    "mis": _s(A, f32), "alt": _s(31, f32),
+    "lz": _s(192, u16), "lb": _s(48, u16), "lk": _s(96, u16), "le": _s(288, u16),
     "kk": _s(P, f32), "sg3": _s(P, bf), "ky": _s(16, f32),
     "c1": _s(648, bf), "s1": _s(648, bf), "cn": _s(8, f32), "lt": _s(8, u16), "rw": _s(8 * 128, bf),
     "jn1": _s(1024, bf), "jn2": _s(1024, bf),
-    "sm": _s(8, f32), "o6": _s(8, u16), "dk": _s(8, f32), "gb": _s(236, f32),
+    "sm": _s(8, f32), "o6": _s(8, u16), "dk": _s(16, f32), "gb": _s(226, f32),
     "cp": _s(96, f32), "rk": _s(8, u16), "sv": _s(96, f32), "sh": _s(32, f32), "mx": _s(32, f32),
     "hs": _s(3 * 128, bf),
     "ps": ("psum", [128, 4096], f32),
 }
-ROWS = {"ta": (0, 496), "src": (496, 256), "mb": (752, 480), "cb": (1232, 264), "t2": (1496, 256), "vb": (1760, 80)}
-DMAS = ["tg", "ad", "x", "u", "m", "wc", "wd", "ws", "v", "oy", "oz", "oc", "os", "ot", "p0", "p1", "p2", "q1",
-        "j1", "j2", "tr", "ec", "r2"]
+ROWS = {"ta": (0, 496), "src": (496, 256), "mb": (752, 480), "cb": (1232, 264), "vb": (1760, 80)}
+DMAS = ["tg", "ad", "x", "u", "m", "wc", "wd", "ws", "v", "oy", "oz", "oc", "os", "ot", "p0", "p1", "p2", "tr", "r2"]
 SEMAPHORES = ["cV", "cS", "cT", "cG", "sent", "a_rq0", "a_rq1", "a_rq2", "a_f0", "a_f1", "a_f2"] + ["d_" + n for n in DMAS]
-CYC, FIX, GAT, SCA = 1.04e-3, 0.06, 1.56, 3.8
 ORDER = (
-    "(f(j(b)g(a(l(k(m(n)l)m(p(o)k)h)p)i)o(g+l*f+f(h)n)j(c(d(e(q(t(r(s(u(w(x)d+m*h+k,c*i,i+q,b(y)z(v(z)c)b)s)a(i,o*g,n*c)q)u*z,p"
-    "*t*q)r*e.g*w)t*u,u,v*b)x)f*a*v,e,s)e,w,x,k+y*j,m,y,t,z*r-a,l.h-b,q)w*k+z1l-i-e.l.k-d.j.i-f.m-g,d+a+e,a,f+c+j.o.n+r.p*d.y"
-    ".w/a.x.z,h/b.u.s.q.v.r.t-h/c/d-q-c,j,r-m-l7f7g7e7h-s-r-p-t/e/f/g/h-u-v+s+b,g+n*x+t+d+o*l+g+p+i*o+h/i/j+v+u+x+w0l0n)y0k/l"
-    "/n/k/m/o)v0m/p/q/r-w-x.a-y/s*y/t/v7i/w-j.b.f.e.d-k-n1o1n-z.c1p1m3d1k/u7k7j0b0c/x0a/z0o/y0p0t0r0s0q0x0v0d0w0e*s0f0g0i0h0j"
-    "1g0u1q-o1e1r1t1s1u1v1w1x2e2d2f1y1z2a2b1d1b*m1a1h1c0z2g2h0y6f1f1i3f3g1j7l2c*p2r2p2q2s3h3i3j3k2t3l5j7m7n2u2v3m3n3o2l6i6h2k"
-    "2n6g6j2m7o3r3p3t3q3u3s2w3a2x3b2y5k3c2z7p7t7r3v3x3w3y3z4a4b4c4d4e4f4g4h2j4i5l4j4k4l4m5m4n*n7u4t4o7q4p4q4r4s4u2o4v5o5q5n7v"
-    "5p5u2i5s5r5t5v5w5y4y5a4w4z4x5b5c5d5e6c5f5g5h5i6b6k5z5x6d6e3e6l6n6m6o6s6p6t6a6u7x6q6v6r7y:w7w7s:d:e:b:c7b7a7c6z8b8a7z8c8d"
-    "8f8e8g:f8r8p8o8n8q8h8l8j8m8i8k8s8u8t8v8w8x8y8z9a:i:h:g:j:m:k:n:l9b6x7d6w6y9d9c:r9e9f9i9h9g9j9m9k9l:o:q9n9o9q9t9s9p9r9u9v"
-    "9w:s:p9x9z9y:a:t;j:u;n;k:z:v;d;a;e;i;b:x;c;l;m;f;r;q;o;g;h:y;s;p")
-PLAN = {"order": [(ord(ORDER[i]) - 40) * 26 + ord(ORDER[i + 1]) - 97 for i in range(0, len(ORDER), 2)]}
+    "(a(b(f(c(l(d(o+r(k(j(e(n(p(m(g(q(h)w(s(r*n(u*q*c)o(t(w+s)b(x(v)e)d)c(y)f)s,q)g*h)a(z)h)i)k)j*y+e,r)p,s)t*u+k,f*i+j)l)r)q*f+g+n.l(i,n*b-a-b+f*v)n*r)m)u+z-d-c*j*s-e*g-f,o,p-g+i.m)x*k,l+l*e,b,a.p-j,c.o.n-i+t*o.q)y*x,m-k,t.r-l+m.s.t,x*d-s6z+v.u-q,y-p6y.v.x/f-m,u7a/d.z-r,z,e7b.w.k,d/c/e/b.i/a,v-x/g,w.j.y+h*w,h-w-u+q,i/i/h-v+x+d/j-h-y,j/k.a0v/l/m+p)z/n,g,k*a/o-t-z/p7c+y/q+u+w0u/r/s/t+a/v/u.b-o*m.c/y/w.f/z-n+o.g/x*z0s.d)v0a+b0e0b0t0c0d.h.e0f0k0h0w0g0i7e0j0l0x0m0z0y1d1b0n1a0o1c0p0q1n1f0r1o1m1e1q1h1i1r1s1t1g1j1u1x1v1k1w7d1l2h2f2g2i2y5j1y1z3a5h2a3b7f2b5k3d3c3f5i7g7h3e3g2c2k2l2m3i3h2n7i3j*p2o3o2p3s3m2q3u3q3t3k3n+c3r3l3v3p2d3x2r3w2v1p3y2s2j2w2t3z4a2e4b2x4c2u7l4d7n5l4e7j4f7k4g4h5m4n4i5o4k5n4j5q5s4l5p4o4m7p5r*t4p5t4w4u4t4q5u4s4x4v4r4z4y5a5b5y5c5d5e5f6c5w5z5g6d6b6e6f2z5v5x6g7m6i6h6a6m*l6n6j7q6o6k7o7r:q6p7s6l9x6u7w7t7u9y6v6w6t7v9z:a7x7z7y:b8a8f8l:d8b:c8d:f8j8i8k:e8g8h8c8m8e:j8o8n:g8p:i8q8r8s:h8t8u6q6r8w6x8v6s8y:n8x9b8z9c9a:k9d:o9f9g9h9l9i9j9n9k9m9o9e:m9q9p9r9s:l9t9u9v:r9w:p:y:t;c:z:s;e:u;d:x:v;h;g;a:w;b;f")
+ENGINES = "VSSSVSSVSVVVVSSVSSSSSSSSSSVSSSVVSVSSSSSSSSVSVVVVVVVSVVSVSVVVSSSSSVVSVSSSSSSSVVSSSVSVSSSSSSSSSVSSSVSSSSVSSSSSSVSSSSSSVSVSSSSVSSSSSSSSVVVSSSSSSSSVSSSSSSVV"
+PLAN = {"order": [(ord(ORDER[i]) - 40) * 26 + ord(ORDER[i + 1]) - 97 for i in range(0, len(ORDER), 2)], "eng": ENGINES}
 
 
 def overlap(a, b):
@@ -90,13 +79,12 @@ def rank_program(g, core, T, topo):
         hi = SCRATCH[name][1][1] if hi is None else hi
         ap = T[name][:, lo:hi] if step == 1 else T[name][:, lo:hi:step]
         cnt = (hi - lo + step - 1) // step
-        wide = 2 if SCRATCH[name][2] in (bf, u16) else 4
         if name == "ps":
-            return (ap, [(name, lo // 512 * 512, (hi + 511) // 512 * 512, 1)], cnt, wide, 0)
-        return (ap, [(name, lo, hi, step)], cnt, wide, 0)
+            return (ap, [(name, lo // 512 * 512, (hi + 511) // 512 * 512, 1)], cnt)
+        return (ap, [(name, lo, hi, step)], cnt)
 
     def ind(win, off):
-        return (win[0].indirect(off[0]), win[1] + off[1], 16 * off[2], win[3], 1)
+        return (win[0].indirect(off[0]), win[1] + off[1], 16 * off[2])
 
     def w32(x):
         return (x[0].bitcast(dt.uint32),) + x[1:]
@@ -104,7 +92,7 @@ def rank_program(g, core, T, topo):
     def b8(x):
         return (x[0].bitcast(dt.uint8),) + x[1:]
 
-    def node(q, kind, run, wr, rd, cost=0.0, by=0, after=(), tag=0, soft=None, free=()):
+    def node(q, kind, run, wr, rd, after=(), tag=0, soft=None, free=()):
         deps = set(after)
         for regs, w in ((wr, True), (rd, False)):
             for r in regs:
@@ -112,7 +100,7 @@ def rank_program(g, core, T, topo):
                     if (w or w2 or (r[0] == "ps" and nodes[k]["q"] != q)) and overlap(r, r2) and k not in free:
                         deps.add(k)
         me = len(nodes)
-        nodes.append(dict(st=stage[0], nm=(wr or rd)[0][0], q=q, kind=kind, run=run, deps=deps, cost=cost, by=by, tag=tag, soft=soft))
+        nodes.append(dict(st=stage[0], nm=(wr or rd)[0][0], q=q, kind=kind, run=run, deps=deps, tag=tag, soft=soft))
         for regs, w in ((wr, True), (rd, False)):
             for r in regs:
                 h = hist.setdefault(r[0], [])
@@ -121,34 +109,30 @@ def rank_program(g, core, T, topo):
                 h.append((r, w, me))
         return me
 
-    def op(q, call, outs, ins, cyc=None, more=()):
+    def op(q, call, outs, ins, more=()):
         views = [i for i in ins if isinstance(i, tuple)]
-        if cyc is None:
-            big = views[0] if views else outs[0]
-            two = q == "V" and all(x[3] == 2 for x in outs + views if x[2] > 1)
-            cyc = big[2] * (GAT if big[4] else 0.5 if two else 1.0) + (30 if q == "S" else 0)
         wr, rd = [r for o in outs for r in o[1]], list(more) + [r for i in views for r in i[1]]
         args = [o[0] for o in outs] + [i[0] if isinstance(i, tuple) else i for i in ins]
-        return node(q, "op", lambda: call(*args), wr, rd, FIX + cyc * CYC)
+        return node(q, "op", lambda: call(*args), wr, rd)
 
-    def dma(q, name, out, in_, size, wr=(), rd=(), free=(), after=(), soft=None):
-        return node(q, "d_" + name, lambda: Q[q].dma_start(out, in_), list(wr), list(rd), 0.1, size, after, 0, soft, free)
+    def dma(q, name, out, in_, wr=(), rd=(), free=(), after=(), soft=None):
+        return node(q, "d_" + name, lambda: Q[q].dma_start(out, in_), list(wr), list(rd), after, 0, soft, free)
 
-    def spread(name, to, rows, size, rd):
+    def spread(name, to, rows, rd):
         mine = [-1]
         for out, in_ in rows:
-            mine.append(dma("Y", name, out, in_, size, wr=to[1], rd=rd, free=list(mine), after=chain[-1:]))
+            mine.append(dma("Y", name, out, in_, wr=to[1], rd=rd, free=list(mine), after=chain[-1:]))
 
-    def load(q, name, dst, src, size):
+    def load(q, name, dst, src):
         prev = chain[-1:] if q == "Y" else []
-        me = dma(q, name, dst[0], src, size, wr=dst[1], after=prev, soft=prev[0] if prev else None)
+        me = dma(q, name, dst[0], src, wr=dst[1], after=prev, soft=prev[0] if prev else None)
         if q == "Y":
             chain.append(me)
 
-    def send(to, sem, dst, src, size, after=None):
+    def send(to, sem, dst, src, after=None):
         rid, pid = topo.addr(to)[:2]
         return node("G", "send", lambda: g.remote_dma(dst[0], src[0], T.sem[sem], T.sem.sent, pid, rid, topo.mask(core, to)),
-                    [], src[1], 0.3, size, [] if after is None else [after], len(topo.engines(core, to)), after)
+                    [], src[1], [] if after is None else [after], len(topo.engines(core, to)), after)
 
     def arrives(frm, sem, views, mine):
         node("R", sem, None, [r for x in views for r in x[1]], [], after=mine, tag=len(views) * len(topo.engines(frm, core)))
@@ -162,60 +146,64 @@ def rank_program(g, core, T, topo):
             op("V", lambda o, x, p, q_: V.tensor_scalar(o, x, p, q_, o0, o1), [out], [a, s1, s2])
 
     def tt(out, a, b, o):
-        op("V", lambda y, x, z: V.tensor_tensor(y, x, z, o), [out], [a, b], a[2] * (1 if a[1][0][0] == "ps" else 2))
+        op("V", lambda y, x, z: V.tensor_tensor(y, x, z, o), [out], [a, b])
 
     def cp(out, a):
         op("V", V.tensor_copy, [out], [a])
 
     def scat(win, off, a):
-        op("V", V.tensor_copy, [(win[0].indirect(off[0]),) + win[1:]], [a], a[2] * SCA, off[1])
+        op("V", V.tensor_copy, [(win[0].indirect(off[0]),) + win[1:]], [a], off[1])
 
     def scan(out, d0, d1, init, o0, o1):
         op("V", lambda o, a, b, i: V.tensor_tensor_scan(o, a, b, i, o0, o1), [out], [d0, d1, init])
 
     def act(out, a, f, scale=1.0, bias=None, acc=None):
         if acc is not None:
-            op("S", lambda o, ac, x, s, b: g.scalar.activation(o, x, f, bias=b, scale=s, accum_out=ac), [out, acc], [a, scale, bias], a[2] + 50)
+            op("S", lambda o, ac, x, s, b: g.scalar.activation(o, x, f, bias=b, scale=s, accum_out=ac), [out, acc], [a, scale, bias])
         elif bias is None:
             op("S", lambda o, x, s: g.scalar.activation(o, x, f, scale=s), [out], [a, scale])
         else:
             op("S", lambda o, x, s, b: g.scalar.activation(o, x, f, bias=b, scale=s), [out], [a, scale, bias])
 
-    def aff(q, out, a, s, b):
-        if q == "V":
-            ts(out, a, s, Op.mult, b, Op.add)
-        else:
-            act(out, a, Fn.Identity, s, b)
-
-    nl = [0]
-
-    def lin(out, a, s, b):
-        nl[0] += 1
-        aff(LIN[nl[0] - 1], out, a, s, b)
-
-    def move(q, out, a):
-        if q == "V":
-            cp(out, a)
-        else:
-            op("S", lambda o, x: g.scalar.activation(o, x, Fn.Copy), [out], [a])
-
-    def quant(c, s, a):
-        op("V", V.quantize_mx, [c, s], [a], a[2] * 0.265)
-
-    def mm(out, lq, ls, rq, rs):
-        op("T", lambda o, a, b, c, d: g.tensor.matmul_mx(o, a, b, c, d, True, True), [out], [lq, ls, rq, rs], (rq[2] + 16) * 1.2)
-
     def iota(out, pattern, base=0, cm=0):
         if SCRATCH[out[1][0][0]][2] == i32:
-            op("G", lambda o: g.iota(o, pattern, base, cm), [out], [], 100 + 2 * out[2])
+            op("G", lambda o: g.iota(o, pattern, base, cm), [out], [])
         else:
-            op("G", lambda o: g.iota(o, pattern, base, cm, allow_small_or_imprecise_dtypes=True), [out], [], 100 + 2 * out[2])
+            op("G", lambda o: g.iota(o, pattern, base, cm, allow_small_or_imprecise_dtypes=True), [out], [])
 
-    def fill(out, c, q="G"):
-        if q == "G":
-            iota(out, [[0, out[2]]], c)
-        else:
-            op("V", lambda o: V.memset(o, float(c)), [out], [])
+    picked = [0]
+
+    def either(other, scalar):
+        picked[0] += 1
+        (scalar if PLAN["eng"][picked[0] - 1] == "S" else other)()
+        nodes[-1]["flex"] = 1
+
+    def aff(out, a, s, b):
+        either(lambda: ts(out, a, s, Op.mult, b, Op.add), lambda: act(out, a, Fn.Identity, s, b))
+
+    def relu(out, a, s=1.0):
+        either(lambda: ts(out, a, 0.0, Op.max, s, Op.mult), lambda: act(out, a, Fn.Relu, s))
+
+    def move(out, a):
+        either(lambda: cp(out, a), lambda: op("S", lambda o, x: g.scalar.activation(o, x, Fn.Copy), [out], [a]))
+
+    def const(out, c):
+        either(lambda: op("V", lambda o: V.memset(o, c), [out], []), lambda: act(out, v("iot", 0, out[2]), Fn.Identity, 0.0, c))
+
+    def ramp(out, step, base):
+        either(lambda: iota(out, [[step, out[2]]], base), lambda: act(out, v("iot", 0, out[2]), Fn.Identity, float(step), float(base)))
+
+    def fill(out, c):
+        ramp(out, 0, c)
+
+    def quant(c, s, a):
+        op("V", V.quantize_mx, [c, s], [a])
+
+    def mm(out, lq, ls, rq, rs):
+        op("T", lambda o, a, b, c, d: g.tensor.matmul_mx(o, a, b, c, d, True, True), [out], [lq, ls, rq, rs])
+
+    def keep(out, a, pattern, o, c, base, cm):
+        op("G", lambda y, x: g.affine_select(y, x, pattern, o, c, base, cm), [out], [a])
 
     def turn(to, name, lo, width, at=0):
         op("V", V.transpose, [v(to, at, at + width)], [v(name, lo, lo + width)])
@@ -224,9 +212,11 @@ def rank_program(g, core, T, topo):
     ci = lambda k: v("ci", k, k + 1)
     cf = lambda k: v("cf", k, k + 1)
     pk = lambda a, b: v("pk", a, b)
-    (M0, M5, M14, TS, T4, ES, RF1, EBS, EBT, EB, M6S, AL, GA, DE, N8S, MS, MB, AAS, B4, VB, B4T, E2S, H0,
-     PAR, RA, RB, RC, P16, HP, K0, K1, R1, A0, V0, I0, DB, PB) = [cf(k) for k in range(37)]
-    PKT, PK8, PK6, PK2, PKU = pk(0, 1), pk(2, 3), pk(4, 5), pk(6, 7), pk(8, 16)
+    (RF, B4, PAR, OD, HF, QF, TAG, S1, NB, B1, B2, EBS, E1, ES, EB, T1, AL, GA, T2, DE, T4, T5, MB, MS, I1, I0, E2S, SH, B4T,
+     R16, HP, K0, K1, R1, DB, PB, D2) = [cf(k) for k in range(37)]
+    oh = lambda k: v("oh", k, k + 1)
+    RAW, CNT, POS, EVI, QA, QZ, QM, QJ = oh(8), oh(9), oh(10), oh(11), oh(16), oh(17), oh(18), oh(19)
+    PK8, PK6, PK2, PKU, PKZ, PKQ, PKC = pk(2, 3), pk(4, 5), pk(6, 7), pk(8, 16), pk(16, 20), pk(20, 21), pk(24, 28)
     W = ["w0", "w1", "w2", "w3"]
     wv = lambda t, lo=0, hi=4 * (HB + A), step=1: v(W[t], PAD + lo, PAD + hi, step)
     E = ["e0", "e1", "e2"]
@@ -235,221 +225,197 @@ def rank_program(g, core, T, topo):
 
     def constants():
         iota(ci(0), [[0, 1]], 0, 1)
+        iota(v("ir", 0, 16), [[1, 16]])
         iota(v("iot", 0, 448), [[1, 448]])
-        fill(v("at", OFF, OFF + MC), 0, "V")
-        act(v("iot", 448, MC), v("iot", 0, 448), Fn.Identity, 1.0, 448.0)
+        ramp(v("iot", 448, MC), 1, 448)
         ts(ci(1), ci(0), 15, Op.bitwise_and)
-        ts(M0, ci(1), 1.0, Op.is_lt)
-        ts(M5, ci(1), 5.0, Op.is_lt)
-        ts(RF1, ci(1), -1.0, Op.add)
-        ts(M6S, ci(1), 6.0, Op.is_equal, SC, Op.mult)
-        ts(N8S, ci(1), 8.0, Op.is_ge, SC, Op.mult)
-        ts(MS, ci(1), 8.0, Op.is_ge, US, Op.max)
-        lin(M14, M0, -1.0, M5)
-        lin(TS, M14, 3 * SC, SC)
-        lin(T4, M14, 12 * SC, 4 * SC)
-        lin(EBT, RF1, M14, -THR)
-        lin(EBS, EBT, SC, 0.0)
-        lin(AL, M6S, -3.0, T4)
-        lin(GA, M6S, 95.0, TS)
-        lin(DE, TS, 32.0, EBS)
-        lin(v("be"), v("iot", 0, 4), GA, DE)
-        for q in range(4):
-            aff(PICK["st"][q], v("st", 32 + q, 416, 4), v("iot", 0, 96), AL, v("be", q, q + 1))
-        lin(MB, N8S, (1.0 - THR) * US, THR)
-        lin(ES, M0, SC / 1024 - SC, TS)
-        lin(EB, M0, THR * SC + (32 - THR) * SC / 1024, EBS)
-        ts(ci(3), ci(0), 4, Op.logical_shift_right)
-        tt(ci(4), ci(0), ci(3), Op.add)
-        ts(ci(5), ci(4), 1, Op.bitwise_and)
-        ts(PAR, ci(5), 0.0, Op.add)
-        ts(ci(6), ci(0), 1, Op.bitwise_and)
-        ts(ci(7), ci(0), 1, Op.logical_shift_right, 7, Op.bitwise_and)
         ts(ci(2), ci(0), 3, Op.bitwise_and)
-        ts(B4, ci(2), 0.0, Op.add)
-        ts(RA, ci(1), 13.0, Op.min, 16.0, Op.mult)
-        ts(RB, ci(1), 7.0, Op.min, 16.0, Op.mult)
-        ts(P16, ci(6), 16.0, Op.mult)
-        ts(HP, ci(7), P16, Op.add)
-        act(RC, RF1, Fn.Abs, 16.0, -112.0)
-        lin(AAS, N8S, 3.0, SC)
-        lin(VB, B4, N8S, (OFF - THR) * SC)
-        lin(B4T, B4, 1.0, THR)
-        lin(E2S, M0, 1023.0, 1.0)
-        lin(H0, M0, 2.0 ** 95, 0.0)
-        lin(K0, RF1, -2.0, 29.5)
-        lin(K1, RF1, -2.0, 28.5)
-        lin(R1, RF1, 1.0, 2.0)
-        ts(PKT, PAR, 240.0, Op.mult, RA, Op.add)
-        ts(PK8, PAR, 144.0, Op.mult, RB, Op.add)
-        ts(PK6, PAR, 112.0, Op.mult, RC, Op.add)
+        iota(ci(7), [[0, 1]], 0, 17)
+        ts(ci(3), ci(7), 4, Op.logical_shift_right, 1, Op.bitwise_and)
+        ts(ci(4), ci(0), 1, Op.bitwise_and)
+        ts(ci(5), ci(0), 1, Op.logical_shift_right, 7, Op.bitwise_and)
+        ts(ci(6), ci(0), 2, Op.logical_shift_right, 3, Op.bitwise_and)
+        cp(v("cf", 0, 6), v("ci", 1, 7))
+        ts(v("oh", 0, 16), v("ir", 0, 16), RF, Op.is_equal, SC, Op.mult)
+        ts(v("oh", 16, 20), v("ir", 0, 4), QF, Op.is_equal, SC, Op.mult)
+        ts(TAG, RAW, EVI, Op.add, QA, Op.add)
+        ts(NB, QF, 2.0, Op.not_equal, B4, Op.mult)
+        ts(B1, NB, OFF - THR, Op.add, TAG, Op.mult)
+        aff(EBS, NB, SC, -THR * SC)
+        aff(S1, QA, 3.0, TAG)
+        aff(B2, S1, 448.0, B1)
+        for i in range(2):
+            aff(v("at", OFF + 448 * i, OFF + 448 * i + 448), v("iot", 0, 448), S1, (B1, B2)[i])
+        aff(T1, QZ, 4.0, CNT)
+        aff(AL, T1, 4.0, POS)
+        aff(GA, POS, 96.0, T1)
+        aff(T2, TAG, THR + 1, EBS)
+        aff(DE, T1, 32.0, T2)
+        aff(v("be"), v("ir", 0, 4), GA, DE)
+        for q in range(4):
+            aff(v("st", 32 + q, 416, 4), v("iot", 0, 96), AL, v("be", q, q + 1))
+        aff(E1, QM, -3.0, 4 * SC)
+        aff(ES, EVI, 1.0 / 1024 - 1, E1)
+        aff(EB, EVI, THR + (32 - THR) / 1024, EBS)
+        aff(T4, QJ, 4.0, CNT)
+        aff(T5, QZ, THR, T4)
+        aff(MB, POS, THR + 32, T5)
+        aff(MS, QJ, -US, 1.0)
+        aff(I1, CNT, THR + 415, EBS)
+        aff(I0, QJ, 4.0 * HB - 4, I1)
+        aff(E2S, EVI, 1023 * US, 1.0)
+        aff(SH, TAG, 4095 * US, 1.0)
+        aff(R16, RF, 16.0, 0.0)
+        aff(HP, OD, 16.0, HF)
+        aff(B4T, B4, 1.0, THR)
+        aff(K0, RF, -2.0, 31.5)
+        aff(K1, RF, -2.0, 30.5)
+        aff(R1, RF, 1.0, 0.5)
+        ts(PK8, PAR, 144.0, Op.mult, R16, Op.add)
+        ts(PK6, HF, -2.0, Op.add, 16.0, Op.mult)
         ts(PK2, PAR, 48.0, Op.mult, HP, Op.add)
         iota(v("ci", 8, 16), [[16, 8]])
         cp(PKU, v("ci", 8, 16))
         iota(v("es", 0, P), [[1, 4], [4, 96]], 32)
-        iota(v("es", P, 432), [[1, 48]])
-        for t in range(2):
-            act(v(E[t], 32, 464), v("es"), Fn.Identity, ES, EB)
-        iota(v("dj"), [[1, 4], [16, 16]], ZB + 1)
-        lin(DB, B4, 223.0, RF1)
-        act(v("dj"), v("dj"), Fn.Identity, 1.0, DB)
-        iota(v("j2"), [[4, A]], 4 * HB)
-        act(v("j2"), v("j2"), Fn.Identity, SC, EBS)
-        lin(PB, PAR, 240.0, RA)
-        ts(v("pk", 16, 20), v("iot", 3, 7), PB, Op.add)
-        ts(v("pk", 20, 24), v("iot", 0, 4), 0.0, Op.mult, PB, Op.add)
-        act(v("k14"), v("iot", 0, A), Fn.Identity, 0.0, M14)
-        lin(A0, M14, -SC, AAS)
-        lin(V0, M14, (4 - OFF + THR) * SC, VB)
-        lin(I0, EBS, 1.0, (4 * HB - 4) * SC)
-        iota(v("jj"), [[4, 4], [16, 56]], 4 * HB)
-        act(v("jj"), v("jj"), Fn.Identity, SC, EBS)
-        act(v("k8"), v("iot", 0, A), Fn.Identity, 0.0, MS)
+        ramp(v("es", P, 432), 1, 0)
+        for t in range(3):
+            aff(v(E[t], 32, 464), v("es"), ES, EB)
+        iota(v("dj"), [[1, 4], [16, 16]], ZB)
+        aff(DB, B4, 223.0, RF)
+        aff(D2, DB, SC, 0.0)
+        aff(v("dj"), v("dj"), SC, D2)
+        aff(PB, PAR, 240.0, R16)
+        ts(PKZ, v("ir", 4, 8), PB, Op.add)
+        ts(PKQ, PAR, 15.0, Op.mult, RF, Op.add)
+        ts(PKC, v("ir", 9, 13), 9.0, Op.min, PB, Op.add)
+        act(v("k8"), v("iot", 0, A), Fn.Sign, 0.0, T4)
         for t in range(3):
             fill(wv(t, 4 * ZC, ZB), 0)
             fill(wv(t, ZB + 4 * A, 4 * HB), 0)
             fill(wv(t, 0, 128), 0)
-        for name, lo, hi in (("ta", 0, 2), ("ta", 482, 512), ("src", 240, 304), ("mb", 432, 512), ("cb", 224, 296), ("vb", 0, 16), ("vb", 48, 80)):
+        for name, lo, hi in (("ta", 480, 512), ("src", 240, 304), ("mb", 432, 512), ("vb", 64, 80), ("t1", 288, 400)):
             fill(v(name, lo, hi), 0)
-        fill(v("seg2"), 1)
-        op("G", lambda o, x: g.affine_select(o, x, [[1, 516]], Op.is_equal, 0.0, -3, -4), [v("ey")], [v("seg2", 0, 516)], 150 + 2 * 516)
-        fill(v("seg2", 0, 648, 108), 0)
-        fill(v("seg2", 6, 648, 107), -1)
+        fill(v("seg1", 0, 320), 1)
+        fill(v("seg1", 320, 640), 1)
+        keep(v("ey"), v("seg1", 0, 516), [[1, 516]], Op.is_equal, 0.0, -3, -4)
+        keep(v("seg2"), v("seg1", 0, 424), [[0, 4], [1, 106]], Op.is_ge, -1.0, -10, 0)
+        keep(v("g4"), v("seg1", 0, 128), [[-1, 128]], Op.is_ge, 0.0, K - 1, 0)
+        fill(v("seg2", 0, 424, 108), 0)
+        fill(v("dk"), 0)
+        fill(v("ys", 0, 1), 0)
+        iota(v("ir", 16, 96), [[0, 5], [1, 16]])
+        ts(v("dm"), v("ir"), RF, Op.is_equal, 2.0 ** 90 + SC, Op.mult)
+        aff(v("dm"), v("dm"), 1.0, -2.0 ** 90)
+        keep(v("sk"), wv(2, 0, 96), [[0, 6], [1, 16]], Op.not_equal, -2.0 ** 96, 0, 0)
         for b in range(4):
             quant(v("eq", 128 * b, 128 * b + 128), v("ep", 128 * b, 128 * b + 128), v("ey", 3 - b, 515 - b))
-        act(v("sg3"), v("iot", 0, P), Fn.Identity, 0.0, 0.0)
-        act(v("sg3", 0, P, 3), v("iot", 0, 128), Fn.Identity, 0.0, 2.0 ** 95)
-        iota(v("g3", 0, 32), [[-1, 32]])
+        const(v("sg3"), 0.0)
+        const(v("sg3", 0, P, 3), 2.0 ** 95)
+        const(v("gb", 225, 226), -2.0 ** 95)
+        ramp(v("g3", 0, 32), -1, 0)
         fill(v("g3", 32, 128), 64)
-        fill(v("seg1", 0, 128 * (8 - min(NS))), 1, PICK["seg"])
         fill(v("seg1", 0, 128 * (8 - min(NS)), 128), 0)
-        lin(v("cu"), v("iot", 0, 4), 2.0 / 3, 128 + 1.0 / 6)
-        iota(v("ir"), [[0, 6], [1, 16]])
+        aff(v("cu"), v("ir", 0, 4), 2.0 / 3, 128 + 1.0 / 6)
         fill(v("uu", 0, 192, 2), 0)
-        ts(v("uu", 1, 192, 2), v("ir"), R1, Op.is_lt, -1.0, Op.mult)
+        iota(v("yk", 0, 80), [[0, 5], [1, 16]])
+        iota(v("yk", 80, 96), [[1, 16]], 1)
+        act(v("yk"), v("yk"), Fn.Sign, -1.0, R1)
+        aff(v("uu", 1, 192, 2), v("yk"), -0.5, -0.5)
 
     def sides():
         quant(v("uq"), v("up"), v("us"))
         op("V", V.tensor_copy, [w32(v("uq2"))], [ind(w32(v("uq")), PKU)])
-        move("S", v("up2"), ind(v("up"), PKU))
+        move(v("up2"), ind(v("up"), PKU))
 
     def tables():
         cp(v("tgu"), v("tgi"))
         cp(v("adu"), v("adi"))
         scat(AT, v("tgu"), v("st", 32, 416))
-        act(v("tr"), ind(v("iot"), v("tgu")), Fn.Identity, SC, (OFF - THR) * SC)
-        dma("Y", "tr", T.st[0:128:16, 32:416], T.tr[0:128:16, :], 12288, wr=v("st", 32, 416)[1], rd=v("tr")[1], after=chain[-1:])
-
-    def payload(t):
-        val = v("val", A * t, A * t + A)
-        if t == 0:
-            act(v("vd"), ind(v("iot"), v("adu", 0, 14)), Fn.Identity, A0, V0)
-            scan(val, v("k14"), v("vd"), I0, Op.mult, Op.add)
-            return
-        if t == 1:
-            dma("Y", "ec", v(E[2], 32, 464)[0], v(E[1], 32, 464)[0], 432 * 512, wr=v(E[2], 32, 464)[1], rd=v(E[1], 32, 464)[1], after=chain[-1:])
-        jj = "jj" if t == 1 else "j2"
-        act(val, ind(v("iot"), v("adu", 14 * t, 14 * t + 14)), Fn.Identity, AAS, VB)
-        spread("j%d" % t, val, [(T.val[b:128:16, A * t:A * t + A], T[jj][b:128:16, :]) for b in range(1, 5)], 7168, v(jj)[1])
+        aff(v("tr"), ind(v("iot"), v("tgu")), S1, B1)
+        spread("tr", v("st", 32, 416), [(T.st[r:128:16, 32:416], T.tr[r:128:16, :]) for r in (11, 8, 0, 1, 2, 3)], v("tr")[1])
 
     def lookup(t):
         act(v("mis"), ind(AT, v("adu", 14 * t, 14 * t + 14)), Fn.Relu, MS, MB)
-        src = v("src", 16, 240)
-        scan(src, v("k8"), v("mis"), 415.0, Op.mult, Op.add)
-        turn("ta", "src", 16, A, 2)
-        move(PICK["qq"], v("qq"), ind(v("ta", 16, 496), PKT))
-        tt(v("alt"), ind(v("ta", 8, 496), PKT), v("qq"), Op.min)
-        cp(v("lb", 16 * t, 16 * t + 16), v("alt"))
-        scat(v(E[t]), v("lb", 16 * t, 16 * t + 14), v("val", A * t, A * t + A))
-        if t == 0:
-            ts(v("lz", 176, 240), ind(v("ta"), pk(16, 20)), float(4 * ZC), Op.min)
+        src, lz = v("src", 16, 240), v("lz", 64 * t, 64 * t + 64)
+        scan(src, v("k8"), v("mis"), I0, Op.mult, Op.add)
+        turn("ta", "src", 16, A)
+        ta = v("ta")
+        tt(v("alt"), v("ta", 9, 496, 16), v("ta", 10, 496, 16), Op.min)
+        ts(v("lb", 16 * t, 16 * t + 16), ind(v("alt"), PKQ), US, Op.mult)
+        scat(v(E[t]), v("lb", 16 * t, 16 * t + 14), src)
+        if t < 2:
+            ts(lz, ind(ta, PKZ), US, Op.mult, float(4 * ZC), Op.min)
             return
-        if t == 2:
-            ts(v("tc", 0, 64), ind(v("ta", 16, 496), pk(20, 24)), 447.5, Op.subtract, 16384.0, Op.mult)
-            tt(v("tc", 0, 64), v("tc", 0, 64), v("dj"), Op.max)
-            tt(v("tc", 64, 128), ind(v("ta"), pk(16, 20)), v("tc", 0, 64), Op.min)
-            cp(v("lz", 112, 176), v("tc", 64, 128))
-            return
-        to, lo, hi = v("tz", 56 * t, 56 * t + 56), src[1][0][1], src[1][0][2]
-        spread("q%d" % t, to, [(T.tz[b:128:4, 56 * t:56 * t + 56], T.ar[1:128:16, lo:hi]) for b in range(4)], 7168, src[1])
-        ts(v("lz", 56 * t, 56 * t + 56), to, float(4 * ZC), Op.min, B4, Op.add)
+        aff(v("tc", 0, 64), ind(ta, PKC), 16384.0, -447.5 * 16384 * SC)
+        tt(v("tc", 0, 64), v("tc", 0, 64), v("dj"), Op.max)
+        tt(v("tc", 64, 128), ind(ta, PKZ), v("tc", 0, 64), Op.min)
+        ts(lz, v("tc", 64, 128), US, Op.mult)
 
     def served(t):
         turn("tk", E[t], 416, 32)
         if t < 2:
-            ts(v("sa%d" % t), ind(v("tk", 8, 96), PK2), US, Op.mult, THR - OFF, Op.add)
-            mine = send(owner, "a_rq%d" % t, v("rq%d" % t), v("sa%d" % t, 0, 8), 2048, opened)
+            ts(v("sa%d" % t), ind(v("tk"), PK2), US, Op.mult, THR - OFF, Op.add)
+            mine = send(owner, "a_rq%d" % t, v("rq%d" % t), v("sa%d" % t, 0, 8), opened)
             arrives(asker, "a_rq%d" % t, [v("rq%d" % t)], [mine] + chain[-1:])
-            act(v("ex", 32 * t, 32 * t + 32), v(E[t], 416, 448), Fn.Identity, E2S)
-        ts(v("lk", 32 * t, 32 * t + 16), ind(v("tk"), PK2), US, Op.mult, THR, Op.add)
+            aff(v("ex", 32 * t, 32 * t + 32), v(E[t], 416, 448), E2S, 0.0)
+        ts(v("lk", 32 * t + 16, 32 * t + 32), ind(v("tk", 8, 96), PK2), US, Op.mult, THR, Op.add)
 
     def places(t):
         to = v("tp", 96 * t, 96 * t + 96)
-        spread("p%d" % t, to, [(T.tp[b:128:4, 96 * t:96 * t + 96], T[E[t]][1:128:16, 32:416]) for b in range(4)], 12288, v(E[t], 32, 416)[1])
+        spread("p%d" % t, to, [(T.tp[b:128:4, 96 * t:96 * t + 96], T[E[t]][12:128:16, 32:416]) for b in range(4)], v(E[t], 32, 416)[1])
         ts(v("le", 96 * t, 96 * t + 96), to, US, Op.mult, B4T, Op.add)
 
     def answer(t):
         mem = v("ms", 0, 4 * MC)
         eb = lambda b: (v("eq", 128 * b, 128 * b + 128), v("ep", 128 * b, 128 * b + 128))
         if t == 2:
-            spread("r2", v("r2"), [(T.r2[b:128:4, :], T.rq2[:, :]) for b in range(4)], 7168, v("rq2")[1])
+            spread("r2", v("r2"), [(T.r2[b:128:4, :], T.rq2[:, :]) for b in range(4)], v("rq2")[1])
             ts(v("f2l"), v("r2"), 4.0, Op.mult, B4, Op.add)
             for i in range(2):
-                move("S", v("ft", 448 * i, 448 * i + 448), ind(mem, v("f2l", 28 * i, 28 * i + 28)))
+                move(v("ft", 448 * i, 448 * i + 448), ind(mem, v("f2l", 28 * i, 28 * i + 28)))
             quant(v("fq2"), v("fp2"), v("ft"))
             lc, lp = v("lc"), v("lp")
-            mine = [send(asker, "a_f2", b8(lc), b8(v("fq2")), 512 * A), send(asker, "a_f2", lp, v("fp2"), 128 * A)]
+            mine = [send(asker, "a_f2", b8(lc), b8(v("fq2"))), send(asker, "a_f2", lp, v("fp2"))]
             arrives(owner, "a_f2", [lc, lp], mine)
             for b in range(4):
                 bank = 512 * (4 + b % 3)
                 mm(v("ps", bank, bank + A), *eb(b), lc, lp)
-                move("S", wv(2, ZB + b, ZB + 4 * A, 4), v("ps", bank, bank + A))
+                move(wv(2, ZB + b, ZB + 4 * A, 4), v("ps", bank, bank + A))
             return
         lo, at = 4 * (MC + K * t), LAND[t]
-        own = 160 if t == 0 else 128
         for b in range(4):
-            move(MG[t][b], v("ms", lo + b, lo + 4 * K, 4), ind(mem, v("rq%d" % t, 2 * b, 2 * b + 2)))
-        quant(v("fq", at - own, at), v("fp", at - own, at), v("ms", lo + 4 * K - 4 * own, lo + 4 * K))
+            move(v("ms", lo + b, lo + 4 * K, 4), ind(mem, v("rq%d" % t, 2 * b, 2 * b + 2)))
+        quant(v("fq", at - 128, at), v("fp", at - 128, at), v("ms", lo + 4 * K - 512, lo + 4 * K))
         lc, lp = v("fq", at, at + K), v("fp", at, at + K)
-        mine = [send(asker, "a_f%d" % t, b8(lc), b8(v("fq", at - K, at)), 512 * K),
-                send(asker, "a_f%d" % t, lp, v("fp", at - K, at), 128 * K)]
+        mine = [send(asker, "a_f%d" % t, b8(lc), b8(v("fq", at - K, at))), send(asker, "a_f%d" % t, lp, v("fp", at - K, at))]
         arrives(owner, "a_f%d" % t, [lc, lp], mine)
         for b in (1, 0, 3, 2):
             w, bank = 128 + K * (b % 2), 2048 + 512 * (b // 2)
             mm(v("ps", bank, bank + w), *eb(b), v("fq", at + K - w, at + K), v("fp", at + K - w, at + K))
             if b % 2 == 0:
-                move("S", v("fd", 128 * t + K * b, 128 * t + K * b + 64), v("ps", bank + 96, bank + 160))
+                move(v("fd", 128 * t + K * b, 128 * t + K * b + 64), v("ps", bank + 96, bank + 160))
 
     def layer(t):
         zv = (lambda lo, hi, st=1: wv(t, ZB + lo, ZB + hi, st)) if t < 2 else (lambda lo, hi, st=1: v("z2", lo, hi, st))
         win = wv(t, 0, ZB if t < 2 else 4 * HB)
-        for i, q in enumerate(RD[t]):
-            if t == 1:
-                w = 56 // len(RD[t])
-                move(q, zv(16 * w * i, 16 * w * (i + 1)), ind(win, v("lz", 56 + w * i, 56 + w * (i + 1))))
-            else:
-                at = 16 * i + (112 if t else 176)
-                move(q, zv(i, 4 * A, 4), ind(win, v("lz", at, at + 14)))
+        for i in range(4):
+            move(zv(i, 4 * A, 4), ind(win, v("lz", 64 * t + 16 * i, 64 * t + 16 * i + 14)))
         zq, zp = v("zq", A * t, A * t + A), v("zp", A * t, A * t + A)
         if t < 2:
-            scat(v(W[t], 0, PAD + ZB + 4 * A), v("lk", 32 * t + 2, 32 * t + 10), v("fd", 128 * t, 128 * t + 128))
+            scat(v(W[t], 0, PAD + ZB + 4 * A), v("lk", 32 * t + 24, 32 * t + 32), v("fd", 128 * t, 128 * t + 128))
         quant(zq, zp, zv(0, 4 * A))
         for b in range(4):
             mm(v("ps", 512 * b, 512 * b + A), v("wq", 128 * b, 128 * b + 128), v("wp", 128 * b, 128 * b + 128), zq, zp)
         for b in range(4):
-            o, r = wv(t, 4 * HB + b, 4 * (HB + A), 4), v("ps", 512 * b, 512 * b + A)
-            if RL[t][b] == "V":
-                ts(o, r, 0.0, Op.max, 0.03125, Op.mult)
-            else:
-                act(o, r, Fn.Relu, 0.03125)
+            relu(wv(t, 4 * HB + b, 4 * (HB + A), 4), v("ps", 512 * b, 512 * b + A), 0.03125)
 
     def write(t):
         hs = v("hs", 128 * t, 128 * t + 128)
-        move("S", hs, ind(wv(t), v("lk", 32 * t + 2, 32 * t + 10)))
-        w = 96 // len(WR[t])
-        for i, q in enumerate(WR[t]):
-            move(q, wv(t + 1, 128 + 16 * w * i, 128 + 16 * w * (i + 1)), ind(wv(t), v("le", 96 * t + w * i, 96 * t + w * (i + 1))))
-        scat(wv(t + 1, 0, 1664), v("lk", 32 * t + 18, 32 * t + 26), hs)
+        move(hs, ind(wv(t), v("lk", 32 * t + 24, 32 * t + 32)))
+        w = 96 // WR[t]
+        for i in range(WR[t]):
+            move(wv(t + 1, 128 + 16 * w * i, 128 + 16 * w * (i + 1)), ind(wv(t), v("le", 96 * t + w * i, 96 * t + w * (i + 1))))
+        scat(wv(t + 1, 0, 1664), v("lk", 32 * t, 32 * t + 8), hs)
 
     def marks(t):
         quant(v("xq"), v("xp"), wv(t, 128, 1664))
@@ -465,7 +431,7 @@ def rank_program(g, core, T, topo):
         scan(v("mb", 48, 432), v("sg3"), v("kk"), 0.0, Op.add, Op.min)
         op("V", V.transpose, [v("t1", 0, 128)], [mins])
         op("V", V.transpose, [v("t1", 128, 288)], [v("mb", 2, 480, 3)])
-        move(PICK["ky"], v("ky"), ind(v("t1"), PK8))
+        move(v("ky"), ind(v("t1"), PK8))
         nv = 8 - NS[t]
         cut = lambda name, c: v(name, 128 * c, 128 * c + 128)
         for c in range(nv, 8):
@@ -475,12 +441,11 @@ def rank_program(g, core, T, topo):
             ts(cut("jn1", c), mins, v("ky", c, c + 1), Op.is_lt)
         scan(v("jn2", 0, 128 * nv), v("seg1", 0, 128 * nv), v("jn1", 0, 128 * nv), 0.0, Op.mult, Op.add)
         ts(v("lt", 0, nv), v("jn2", 127, 128 * nv, 128), 127.0, Op.min)
-        if nv < 8:
-            ts(v("lt", nv, 8), v("cn", nv, 8), 127.0, Op.min)
-        move(PICK["rw"], rw(0), ind(v("g3"), v("lt")))
+        ts(v("lt", nv, 8), v("cn", nv, 8), 127.0, Op.min)
+        move(rw(0), ind(v("g3"), v("lt")))
         low = v("rw", 383, 384)
         scan(rw(2), rw(0), rw(0), 0.0, Op.min, Op.min)
-        ts(rw(3), rw(0), 0.0, Op.is_le)
+        either(lambda: ts(rw(3), rw(0), 0.0, Op.is_le), lambda: act(rw(3), ind(v("g4"), v("lt")), Fn.Copy))
         ts(rw(4), rw(0), low, Op.is_equal)
         scan(rw(5), rw(3), rw(4), low, Op.add, Op.subtract)
         scan(rw(1), rw(3), rw(5), -32.0, Op.add, Op.min)
@@ -492,79 +457,85 @@ def rank_program(g, core, T, topo):
             ts(v("o6", 3 * i, 3 * i + 3), v("cu", 0, 3), sm(2 + i), Op.subtract, 1.5, Op.mult)
         ts(v("cb", 33, 225, 2), ind(v("kk"), v("o6", 0, 6)), SC, Op.min)
         act(v("cb", 32, 224, 2), v("cb", 33, 225, 2), Fn.Abs, 1.25 * 2.0 ** -24, 2.0 ** -124)
-        op("V", V.transpose, [v("t2", 32, 128)], [v("cb", 33, 225, 2)])
-        op("V", V.transpose, [v("t2", 128, 256)], [v("cb", 1, 257, 2)])
-        move(PICK["gb"], v("gb", 203, 235, 2), ind(v("t2"), PK6))
-        keys = v("gb", 223, 235, 2)
-        act(v("dk", 0, 6), keys, Fn.Abs, 1.25 * 2.0 ** -24, 2.0 ** -124)
-        move("S", v("cp"), ind(v("st", 32, 416), v("o6", 0, 6)))
-        scan(v("gb", 12, 204), v("uu"), v("cb", 32, 224), 0.0, Op.mult, Op.add)
-        tt(v("gb", 1, 13, 2), keys, v("dk", 0, 6), Op.subtract)
-        for c in range(6):
-            ts(v("c1", 108 * c, 108 * c + 108), v("gb", 1 + 2 * c, 217 + 2 * c, 2), v("gb", 223 + 2 * c, 224 + 2 * c), Op.is_lt)
-        scan(v("s1"), v("seg2"), v("c1"), 0.0, Op.mult, Op.add)
-        cp(v("rk", 0, 6), v("s1", 107, 648, 106))
+        tt(v("yk"), ind(v("kk"), v("o6", 0, 6)), v("dm"), Op.min)
+        scan(v("ys", 1, 97), v("sk"), v("yk"), 0.0, Op.add, Op.max)
+        act(v("dk", 6, 16, 2), v("ys", 16, 81, 16), Fn.Abs, 1.25 * 2.0 ** -24, 2.0 ** -124)
+        move(v("cp"), ind(v("st", 32, 416), v("o6", 0, 6)))
+        scan(v("gb", 32, 224), v("uu"), v("cb", 32, 224), 0.0, Op.mult, Op.add)
+        tt(v("gb", 1, 33, 2), ind(v("ys", 0, 97), PK6), v("dk"), Op.subtract)
+        nv = 6 - NK[t]
+        for c in range(nv):
+            ts(v("c1", 106 * c, 106 * c + 106), v("gb", 13, 224, 2), v("ys", 16 + 16 * c, 17 + 16 * c), Op.is_lt)
+        for c in range(nv, 6):
+            w, lo = 92 + c, 128 * c
+            act(v("jn1", lo, lo + w), v("gb", 33, 33 + 2 * w - 1, 2), Fn.Sign, -1.0, v("ys", 16 + 16 * c, 17 + 16 * c))
+            act(v("jn2", lo, lo + w), v("jn1", lo, lo + w), Fn.Relu, 1.0, 0.0, sm(c))
+        ts(v("rk", nv, 6), v("sm", nv, 6), -1.0, Op.add)
+        scan(v("s1", 0, 106 * nv), v("seg2", 0, 106 * nv), v("c1", 0, 106 * nv), 0.0, Op.mult, Op.add)
+        cp(v("rk", 0, nv), v("s1", 105, 106 * nv, 106))
         scat(v("sv"), v("rk", 0, 6), v("cp"))
-        tt(v("vb", 16, 48), v("sv", 0, 32), v("ex", 32 * t, 32 * t + 32) if t < 2 else v(E[t], 416, 448), Op.min)
-        turn("tv", "vb", 16, 32)
-        ts(v("lk", 32 * t + 16, 32 * t + 32), ind(v("tv"), PK2), US, Op.mult, THR, Op.add)
+        tt(v("vb", 32, 64), v("sv", 0, 32), v("ex", 32 * t, 32 * t + 32) if t < 2 else v(E[t], 416, 448), Op.min)
+        if t < 2:
+            relu(v("vb", 0, 32), v("sv", 0, 32))
+        turn("tv", "vb", 32, 32, 4)
+        ts(v("lk", 32 * t, 32 * t + 16), ind(v("tv", 8, 100), PK2), US, Op.mult, THR, Op.add)
 
     def retag(t):
+        cols = v("lk", 32 * t + 10, 32 * t + 12)
         if t < 2:
-            scat(v("at"), v("lk", 32 * t + 14, 32 * t + 18), v("vb", 16, 80))
-        aff(PICK["svh"], v("sh"), v("sv", 0, 32), 1.0, H0)
-        tt(v("mx"), v("sh"), v(E[t], 416, 448), Op.min)
-        if t < 2:
-            scat(v("st"), v("lk", 32 * t + 26, 32 * t + 28), v("mx"))
+            scat(v("at"), v("lk", 32 * t + 14, 32 * t + 18), v("vb", 0, 64))
+            aff(v("sh"), v("sv", 0, 32), SH, 0.0)
+            tt(v("mx"), v("sh"), v(E[t], 416, 448), Op.min)
+            scat(v("st"), cols, v("mx"))
             return
-        act(v("otb", 32, 416), v("st", 32, 416), Fn.Identity, US, THR - OFF)
-        aff(PICK["ot"], v("sh"), v("mx"), US, THR - OFF)
-        scat(v("otb"), v("lk", 32 * t + 26, 32 * t + 28), v("sh"))
+        aff(v("otb", 32, 416), v("st", 32, 416), US, THR - OFF)
+        aff(v("sh"), v(E[t], 416, 448), US, THR - OFF)
+        scat(v("otb"), cols, v("sh"))
 
     def last():
-        w = P // len(PICK["y"])
-        for i, q in enumerate(PICK["y"]):
+        w = P // YP
+        for i in range(YP):
             lo = w * i
             q_, p_, bank, yb = v("xq", lo, lo + w), v("xp", lo, lo + w), 3584 - 512 * i, v("yb", lo, lo + w)
             quant(q_, p_, wv(3, 128 + 4 * lo, 128 + 4 * (lo + w)))
             mm(v("ps", bank, bank + w), v("vq"), v("vp"), q_, p_)
-            move(q, yb, v("ps", bank, bank + w))
-            dma("S" if q == "S" else "Y", "oy" if q == "S" else "oz", T.y[:, lo:lo + w], yb[0], 512 * w, rd=yb[1])
-            dma("S" if i else "Y", "oc", T.oc[:, 4 * lo:4 * (lo + w)], b8(q_)[0], 512 * w, rd=q_[1])
+            move(yb, v("ps", bank, bank + w))
+            dma("Y" if i % 2 else "S", "oz" if i % 2 else "oy", T.y[:, lo:lo + w], yb[0], rd=yb[1])
+            dma("S" if i else "Y", "oc", T.oc[:, 4 * lo:4 * (lo + w)], b8(q_)[0], rd=q_[1])
 
     def store():
         for k in range(4):
-            dma("Y", "os", T.osc[4 * k:4 * k + 4, :], T.xp[32 * k:32 * k + 4, :], 4 * P, rd=v("xp")[1])
-        dma("Y", "ot", T.ot[:], T.otb[0:128:16, 32:416], 32 * P, rd=v("otb")[1])
+            dma("Y", "os", T.osc[4 * k:4 * k + 4, :], T.xp[32 * k:32 * k + 4, :], rd=v("xp")[1])
+        dma("Y", "ot", T.ot[:], T.otb[11:128:16, 32:416], rd=v("otb")[1])
 
     def late(t):
         if t == 0:
             came = v("rq0")[1]
-            dma("Y", "ws", v("wp")[0], T.ws[:], 65536, wr=v("wp")[1], rd=came)
+            dma("Y", "ws", v("wp")[0], T.ws[:], wr=v("wp")[1], rd=came)
             for i, name in enumerate(("wc", "wd")):
                 half = v("wq", 256 * i, 256 * i + 256)
-                dma("Y", name, b8(half)[0], T.wc[:, 1024 * i:1024 * i + 1024], 131072, wr=half[1], rd=came)
+                dma("Y", name, b8(half)[0], T.wc[:, 1024 * i:1024 * i + 1024], wr=half[1], rd=came)
         if t == 1:
-            dma("Y", "v", v("vs")[0], T.v[:], 131072, wr=v("vs")[1], rd=v("fd", 0, 128)[1])
+            dma("Y", "v", v("vs")[0], T.v[:], wr=v("vs")[1], rd=v("fd", 0, 128)[1])
             quant(v("vq"), v("vp"), v("vs"))
 
     def do(name, f, *a):
         stage[0] = name + "".join(str(x) for x in a)
         f(*a)
 
-    load("Y", "tg", v("tgi"), T.tg[:], 12288)
-    load("S", "ad", v("adi"), T.ad[:], 21504)
-    load("Y", "x", wv(0, 128, 1664), T.x[:], 1024 * P)
-    load("Y", "u", v("us"), T.u[:], 131072)
-    load("Y", "m", v("ms", 0, 4 * MC), T.m[:], 1024 * MC)
+    load("Y", "tg", v("tgi"), T.tg[:])
+    load("S", "ad", v("adi"), T.ad[:])
+    load("Y", "x", wv(0, 128, 1664), T.x[:])
+    load("Y", "u", v("us"), T.u[:])
+    load("Y", "m", v("ms", 0, 4 * MC), T.m[:])
     do("con", constants)
     stage[0] = "rq2"
-    opened = send(owner, "a_rq2", v("rq2"), v("adi", 28, 42), 7168)
+    opened = send(owner, "a_rq2", v("rq2"), v("adi", 28, 42))
     arrives(asker, "a_rq2", [v("rq2")], [opened] + chain[-1:])
     do("sid", sides)
     do("tbl", tables)
     for t in range(3):
-        for name, f in (("pay", payload), ("loo", lookup), ("ser", served), ("pla", places), ("ans", answer), ("lat", late),
+        for name, f in (("loo", lookup), ("ser", served), ("pla", places), ("ans", answer), ("lat", late),
                         ("mar", marks), ("blo", blocks), ("vic", victims), ("lay", layer), ("wri", write), ("ret", retag)):
             do(name, f, t)
     do("mar3", last)
@@ -581,7 +552,7 @@ def rank_program(g, core, T, topo):
             Q[q].wait_ge(T.sem[sem], val)
             waited[(q, sem)] = val
 
-    for k in PLAN["order"]:
+    for k in PLAN["order"] or range(len(nodes)):
         nd = nodes[k]
         q, kind = nd["q"], nd["kind"]
         if q == "R":

from concourse.mybir import dt, AluOpType as Op, ActivationFunctionType as Fn

MC, P, A, K = 896, 384, 224, 32
OFF = 2592
THR = 2580.0
SC = 2.0 ** 71
PAD, ZB, HB, ZC = 912, 1680, 648, 416
LAND = (160, 320)
NS = (3, 3, 3)
NK = (2, 2, 2)
WR = (4, 4, 4)
YP = 2
f32, bf, i32, u16, u8, x4 = "float32", "bfloat16", "int32", "uint16", "uint8", "float8_e4m3fn_x4"


def _s(n, d):
    return ("sbuf", [128, n], d)


SCRATCH = {
    "tgi": _s(24, i32), "adi": _s(42, i32), "tgu": _s(24, u16), "adu": _s(42, u16),
    "ms": _s(4 * (MC + 2 * K), bf), "us": _s(512, bf), "vs": _s(512, bf),
    "wq": _s(512, x4), "wp": _s(512, u8),
    "w0": _s(4400, bf), "w1": _s(4400, bf), "w2": _s(4400, bf), "w3": _s(2576, bf),
    "uq": _s(128, x4), "up": _s(128, u8), "uq2": _s(128, x4), "up2": _s(128, u8),
    "vq": _s(128, x4), "vp": _s(128, u8),
    "xq": _s(P, x4), "xp": _s(P, u8), "zq": _s(3 * A, x4), "zp": _s(3 * A, u8),
    "z2": _s(4 * A, bf), "fd": _s(256, bf), "ft": _s(4 * A, bf),
    "fq2": _s(A, x4), "fp2": _s(A, u8), "lc": _s(A, x4), "lp": _s(A, u8), "fq": _s(352, x4), "fp": _s(352, u8),
    "eq": _s(512, x4), "ep": _s(512, u8), "ey": _s(516, bf),
    "rq0": _s(8, u16), "rq1": _s(8, u16), "rq2": _s(14, i32), "sa0": _s(16, u16), "sa1": _s(16, u16),
    "r2": _s(56, i32), "f2l": _s(56, u16),
    "iot": _s(MC, f32), "at": _s(OFF + MC, f32), "st": _s(416, f32), "tr": _s(P, f32), "es": _s(432, f32),
    "k8": _s(A, bf), "oh": _s(24, f32), "g4": _s(128, bf), "dm": _s(96, f32), "sk": _s(96, bf),
    "yk": _s(96, f32), "ys": _s(104, f32),
    "e0": _s(640, f32), "e1": _s(640, f32), "e2": _s(640, f32), "ex": _s(64, f32),
    "otb": _s(416, f32), "yb": _s(P, f32), "dj": _s(64, f32), "tc": _s(128, f32),
    "ci": _s(16, i32), "cf": _s(48, f32), "be": _s(4, f32), "cu": _s(4, f32), "ir": _s(96, f32), "pk": _s(28, u16),
    "uu": _s(192, bf), "g3": _s(128, f32), "seg1": _s(1024, bf), "seg2": _s(424, bf),
    "ar": _s(1840, f32), "tp": _s(288, f32), "t1": _s(400, f32), "tk": _s(96, f32), "tv": _s(100, f32),
    "mis": _s(A, f32), "alt": _s(31, f32),
    "lz": _s(192, u16), "lb": _s(48, u16), "lk": _s(96, u16), "le": _s(288, u16),
    "kk": _s(P, f32), "sg3": _s(P, bf), "ky": _s(16, f32),
    "c1": _s(648, bf), "s1": _s(648, bf), "cn": _s(8, f32), "lt": _s(8, u16), "rw": _s(8 * 128, bf),
    "jn1": _s(1024, bf), "jn2": _s(1024, bf),
    "sm": _s(8, f32), "o6": _s(8, u16), "dk": _s(16, f32), "gb": _s(226, f32),
    "cp": _s(96, f32), "rk": _s(8, u16), "sv": _s(96, f32), "sh": _s(32, f32), "mx": _s(32, f32),
    "hs": _s(3 * 128, bf),
    "ps": ("psum", [128, 4096], f32),
}
ROWS = {"ta": (0, 496), "src": (496, 256), "mb": (752, 480), "cb": (1232, 264), "vb": (1760, 80)}
DMAS = ["tg", "ad", "x", "u", "m", "wc", "wd", "ws", "v", "oy", "oz", "oc", "os", "ot", "p0", "p1", "p2", "tr", "r2"]
SEMAPHORES = ["cV", "cS", "cT", "cG", "sent", "a_rq0", "a_rq1", "a_rq2", "a_f0", "a_f1", "a_f2"] + ["d_" + n for n in DMAS]
ORDER = (
    "(a(b(f(c(l(d(o+r(k(j(e(n(p(m(g(q(h)w(s(r*n(u*q*c)o(t(w+s)b(x(v)e)d)c(y)f)s,q)g*h)a(z)h)i)k)j*y+e,r)p,s)t*u+k,f*i+j)l)r)q*f+g+n.l(i,n*b-a-b+f*v)n*r)m)u+z-d-c*j*s-e*g-f,o,p-g+i.m)x*k,l+l*e,b,a.p-j,c.o.n-i+t*o.q)y*x,m-k,t.r-l+m.s.t,x*d-s6z+v.u-q,y-p6y.v.x/f-m,u7a/d.z-r,z,e7b.w.k,d/c/e/b.i/a,v-x/g,w.j.y+h*w,h-w-u+q,i/i/h-v+x+d/j-h-y,j/k.a0v/l/m+p)z/n,g,k*a/o-t-z/p7c+y/q+u+w0u/r/s/t+a/v/u.b-o*m.c/y/w.f/z-n+o.g/x*z0s.d)v0a+b0e0b0t0c0d.h.e0f0k0h0w0g0i7e0j0l0x0m0z0y1d1b0n1a0o1c0p0q1n1f0r1o1m1e1q1h1i1r1s1t1g1j1u1x1v1k1w7d1l2h2f2g2i2y5j1y1z3a5h2a3b7f2b5k3d3c3f5i7g7h3e3g2c2k2l2m3i3h2n7i3j*p2o3o2p3s3m2q3u3q3t3k3n+c3r3l3v3p2d3x2r3w2v1p3y2s2j2w2t3z4a2e4b2x4c2u7l4d7n5l4e7j4f7k4g4h5m4n4i5o4k5n4j5q5s4l5p4o4m7p5r*t4p5t4w4u4t4q5u4s4x4v4r4z4y5a5b5y5c5d5e5f6c5w5z5g6d6b6e6f2z5v5x6g7m6i6h6a6m*l6n6j7q6o6k7o7r:q6p7s6l9x6u7w7t7u9y6v6w6t7v9z:a7x7z7y:b8a8f8l:d8b:c8d:f8j8i8k:e8g8h8c8m8e:j8o8n:g8p:i8q8r8s:h8t8u6q6r8w6x8v6s8y:n8x9b8z9c9a:k9d:o9f9g9h9l9i9j9n9k9m9o9e:m9q9p9r9s:l9t9u9v:r9w:p:y:t;c:z:s;e:u;d:x:v;h;g;a:w;b;f")
ENGINES = "VSSSVSSVSVVVVSSVSSSSSSSSSSVSSSVVSVSSSSSSSSVSVVVVVVVSVVSVSVVVSSSSSVVSVSSSSSSSVVSSSVSVSSSSSSSSSVSSSVSSSSVSSSSSSVSSSSSSVSVSSSSVSSSSSSSSVVVSSSSSSSSVSSSSSSVV"
PLAN = {"order": [(ord(ORDER[i]) - 40) * 26 + ord(ORDER[i + 1]) - 97 for i in range(0, len(ORDER), 2)], "eng": ENGINES}


def overlap(a, b):
    if a[0] != b[0] or a[2] <= b[1] or b[2] <= a[1]:
        return False
    return not (a[3] == b[3] > 1 and (a[1] - b[1]) % a[3])


def rank_program(g, core, T, topo):
    rank = T.rank_of(core)
    if rank is None:
        return
    n = len(T.cores)
    owner, asker = T.cores[(rank + 1) % n], T.cores[(rank - 1) % n]
    Q = {"V": g.vector, "S": g.scalar, "T": g.tensor, "G": g, "Y": g.sync}
    nodes, hist, stage, chain = [], {}, [""], []

    def v(name, lo=0, hi=None, step=1):
        if name in ROWS:
            at, size = ROWS[name]
            name, lo, hi = "ar", at + lo, at + (size if hi is None else hi)
        hi = SCRATCH[name][1][1] if hi is None else hi
        ap = T[name][:, lo:hi] if step == 1 else T[name][:, lo:hi:step]
        cnt = (hi - lo + step - 1) // step
        if name == "ps":
            return (ap, [(name, lo // 512 * 512, (hi + 511) // 512 * 512, 1)], cnt)
        return (ap, [(name, lo, hi, step)], cnt)

    def ind(win, off):
        return (win[0].indirect(off[0]), win[1] + off[1], 16 * off[2])

    def w32(x):
        return (x[0].bitcast(dt.uint32),) + x[1:]

    def b8(x):
        return (x[0].bitcast(dt.uint8),) + x[1:]

    def node(q, kind, run, wr, rd, after=(), tag=0, soft=None, free=()):
        deps = set(after)
        for regs, w in ((wr, True), (rd, False)):
            for r in regs:
                for r2, w2, k in hist.get(r[0], []):
                    if (w or w2 or (r[0] == "ps" and nodes[k]["q"] != q)) and overlap(r, r2) and k not in free:
                        deps.add(k)
        me = len(nodes)
        nodes.append(dict(st=stage[0], nm=(wr or rd)[0][0], q=q, kind=kind, run=run, deps=deps, tag=tag, soft=soft))
        for regs, w in ((wr, True), (rd, False)):
            for r in regs:
                h = hist.setdefault(r[0], [])
                if w and r[3] == 1 and not free:
                    h[:] = [e for e in h if not (r[1] <= e[0][1] and e[0][2] <= r[2])]
                h.append((r, w, me))
        return me

    def op(q, call, outs, ins, more=()):
        views = [i for i in ins if isinstance(i, tuple)]
        wr, rd = [r for o in outs for r in o[1]], list(more) + [r for i in views for r in i[1]]
        args = [o[0] for o in outs] + [i[0] if isinstance(i, tuple) else i for i in ins]
        return node(q, "op", lambda: call(*args), wr, rd)

    def dma(q, name, out, in_, wr=(), rd=(), free=(), after=(), soft=None):
        return node(q, "d_" + name, lambda: Q[q].dma_start(out, in_), list(wr), list(rd), after, 0, soft, free)

    def spread(name, to, rows, rd):
        mine = [-1]
        for out, in_ in rows:
            mine.append(dma("Y", name, out, in_, wr=to[1], rd=rd, free=list(mine), after=chain[-1:]))

    def load(q, name, dst, src):
        prev = chain[-1:] if q == "Y" else []
        me = dma(q, name, dst[0], src, wr=dst[1], after=prev, soft=prev[0] if prev else None)
        if q == "Y":
            chain.append(me)

    def send(to, sem, dst, src, after=None):
        rid, pid = topo.addr(to)[:2]
        return node("G", "send", lambda: g.remote_dma(dst[0], src[0], T.sem[sem], T.sem.sent, pid, rid, topo.mask(core, to)),
                    [], src[1], [] if after is None else [after], len(topo.engines(core, to)), after)

    def arrives(frm, sem, views, mine):
        node("R", sem, None, [r for x in views for r in x[1]], [], after=mine, tag=len(views) * len(topo.engines(frm, core)))

    V = g.vector

    def ts(out, a, s1, o0, s2=None, o1=None):
        if o1 is None:
            op("V", lambda o, x, p: V.tensor_scalar(o, x, p, None, o0), [out], [a, s1])
        else:
            op("V", lambda o, x, p, q_: V.tensor_scalar(o, x, p, q_, o0, o1), [out], [a, s1, s2])

    def tt(out, a, b, o):
        op("V", lambda y, x, z: V.tensor_tensor(y, x, z, o), [out], [a, b])

    def cp(out, a):
        op("V", V.tensor_copy, [out], [a])

    def scat(win, off, a):
        op("V", V.tensor_copy, [(win[0].indirect(off[0]),) + win[1:]], [a], off[1])

    def scan(out, d0, d1, init, o0, o1):
        op("V", lambda o, a, b, i: V.tensor_tensor_scan(o, a, b, i, o0, o1), [out], [d0, d1, init])

    def act(out, a, f, scale=1.0, bias=None, acc=None):
        if acc is not None:
            op("S", lambda o, ac, x, s, b: g.scalar.activation(o, x, f, bias=b, scale=s, accum_out=ac), [out, acc], [a, scale, bias])
        elif bias is None:
            op("S", lambda o, x, s: g.scalar.activation(o, x, f, scale=s), [out], [a, scale])
        else:
            op("S", lambda o, x, s, b: g.scalar.activation(o, x, f, bias=b, scale=s), [out], [a, scale, bias])

    def iota(out, pattern, base=0, cm=0):
        if SCRATCH[out[1][0][0]][2] == i32:
            op("G", lambda o: g.iota(o, pattern, base, cm), [out], [])
        else:
            op("G", lambda o: g.iota(o, pattern, base, cm, allow_small_or_imprecise_dtypes=True), [out], [])

    picked = [0]

    def either(other, scalar):
        picked[0] += 1
        (scalar if PLAN["eng"][picked[0] - 1] == "S" else other)()
        nodes[-1]["flex"] = 1

    def aff(out, a, s, b):
        either(lambda: ts(out, a, s, Op.mult, b, Op.add), lambda: act(out, a, Fn.Identity, s, b))

    def relu(out, a, s=1.0):
        either(lambda: ts(out, a, 0.0, Op.max, s, Op.mult), lambda: act(out, a, Fn.Relu, s))

    def move(out, a):
        either(lambda: cp(out, a), lambda: op("S", lambda o, x: g.scalar.activation(o, x, Fn.Copy), [out], [a]))

    def const(out, c):
        either(lambda: op("V", lambda o: V.memset(o, c), [out], []), lambda: act(out, v("iot", 0, out[2]), Fn.Identity, 0.0, c))

    def ramp(out, step, base):
        either(lambda: iota(out, [[step, out[2]]], base), lambda: act(out, v("iot", 0, out[2]), Fn.Identity, float(step), float(base)))

    def fill(out, c):
        ramp(out, 0, c)

    def quant(c, s, a):
        op("V", V.quantize_mx, [c, s], [a])

    def mm(out, lq, ls, rq, rs):
        op("T", lambda o, a, b, c, d: g.tensor.matmul_mx(o, a, b, c, d, True, True), [out], [lq, ls, rq, rs])

    def keep(out, a, pattern, o, c, base, cm):
        op("G", lambda y, x: g.affine_select(y, x, pattern, o, c, base, cm), [out], [a])

    def turn(to, name, lo, width, at=0):
        op("V", V.transpose, [v(to, at, at + width)], [v(name, lo, lo + width)])
        op("V", V.transpose, [v(to, at + width, at + 2 * width + 32)], [v(name, lo - 16, lo + width + 16)])

    ci = lambda k: v("ci", k, k + 1)
    cf = lambda k: v("cf", k, k + 1)
    pk = lambda a, b: v("pk", a, b)
    (RF, B4, PAR, OD, HF, QF, TAG, S1, NB, B1, B2, EBS, E1, ES, EB, T1, AL, GA, T2, DE, T4, T5, MB, MS, I1, I0, E2S, SH, B4T,
     R16, HP, K0, K1, R1, DB, PB, D2) = [cf(k) for k in range(37)]
    oh = lambda k: v("oh", k, k + 1)
    RAW, CNT, POS, EVI, QA, QZ, QM, QJ = oh(8), oh(9), oh(10), oh(11), oh(16), oh(17), oh(18), oh(19)
    PK8, PK6, PK2, PKU, PKZ, PKQ, PKC = pk(2, 3), pk(4, 5), pk(6, 7), pk(8, 16), pk(16, 20), pk(20, 21), pk(24, 28)
    W = ["w0", "w1", "w2", "w3"]
    wv = lambda t, lo=0, hi=4 * (HB + A), step=1: v(W[t], PAD + lo, PAD + hi, step)
    E = ["e0", "e1", "e2"]
    AT = v("at", OFF, OFF + MC)
    US = 1.0 / SC

    def constants():
        iota(ci(0), [[0, 1]], 0, 1)
        iota(v("ir", 0, 16), [[1, 16]])
        iota(v("iot", 0, 448), [[1, 448]])
        ramp(v("iot", 448, MC), 1, 448)
        ts(ci(1), ci(0), 15, Op.bitwise_and)
        ts(ci(2), ci(0), 3, Op.bitwise_and)
        iota(ci(7), [[0, 1]], 0, 17)
        ts(ci(3), ci(7), 4, Op.logical_shift_right, 1, Op.bitwise_and)
        ts(ci(4), ci(0), 1, Op.bitwise_and)
        ts(ci(5), ci(0), 1, Op.logical_shift_right, 7, Op.bitwise_and)
        ts(ci(6), ci(0), 2, Op.logical_shift_right, 3, Op.bitwise_and)
        cp(v("cf", 0, 6), v("ci", 1, 7))
        ts(v("oh", 0, 16), v("ir", 0, 16), RF, Op.is_equal, SC, Op.mult)
        ts(v("oh", 16, 20), v("ir", 0, 4), QF, Op.is_equal, SC, Op.mult)
        ts(TAG, RAW, EVI, Op.add, QA, Op.add)
        ts(NB, QF, 2.0, Op.not_equal, B4, Op.mult)
        ts(B1, NB, OFF - THR, Op.add, TAG, Op.mult)
        aff(EBS, NB, SC, -THR * SC)
        aff(S1, QA, 3.0, TAG)
        aff(B2, S1, 448.0, B1)
        for i in range(2):
            aff(v("at", OFF + 448 * i, OFF + 448 * i + 448), v("iot", 0, 448), S1, (B1, B2)[i])
        aff(T1, QZ, 4.0, CNT)
        aff(AL, T1, 4.0, POS)
        aff(GA, POS, 96.0, T1)
        aff(T2, TAG, THR + 1, EBS)
        aff(DE, T1, 32.0, T2)
        aff(v("be"), v("ir", 0, 4), GA, DE)
        for q in range(4):
            aff(v("st", 32 + q, 416, 4), v("iot", 0, 96), AL, v("be", q, q + 1))
        aff(E1, QM, -3.0, 4 * SC)
        aff(ES, EVI, 1.0 / 1024 - 1, E1)
        aff(EB, EVI, THR + (32 - THR) / 1024, EBS)
        aff(T4, QJ, 4.0, CNT)
        aff(T5, QZ, THR, T4)
        aff(MB, POS, THR + 32, T5)
        aff(MS, QJ, -US, 1.0)
        aff(I1, CNT, THR + 415, EBS)
        aff(I0, QJ, 4.0 * HB - 4, I1)
        aff(E2S, EVI, 1023 * US, 1.0)
        aff(SH, TAG, 4095 * US, 1.0)
        aff(R16, RF, 16.0, 0.0)
        aff(HP, OD, 16.0, HF)
        aff(B4T, B4, 1.0, THR)
        aff(K0, RF, -2.0, 31.5)
        aff(K1, RF, -2.0, 30.5)
        aff(R1, RF, 1.0, 0.5)
        ts(PK8, PAR, 144.0, Op.mult, R16, Op.add)
        ts(PK6, HF, -2.0, Op.add, 16.0, Op.mult)
        ts(PK2, PAR, 48.0, Op.mult, HP, Op.add)
        iota(v("ci", 8, 16), [[16, 8]])
        cp(PKU, v("ci", 8, 16))
        iota(v("es", 0, P), [[1, 4], [4, 96]], 32)
        ramp(v("es", P, 432), 1, 0)
        for t in range(3):
            aff(v(E[t], 32, 464), v("es"), ES, EB)
        iota(v("dj"), [[1, 4], [16, 16]], ZB)
        aff(DB, B4, 223.0, RF)
        aff(D2, DB, SC, 0.0)
        aff(v("dj"), v("dj"), SC, D2)
        aff(PB, PAR, 240.0, R16)
        ts(PKZ, v("ir", 4, 8), PB, Op.add)
        ts(PKQ, PAR, 15.0, Op.mult, RF, Op.add)
        ts(PKC, v("ir", 9, 13), 9.0, Op.min, PB, Op.add)
        act(v("k8"), v("iot", 0, A), Fn.Sign, 0.0, T4)
        for t in range(3):
            fill(wv(t, 4 * ZC, ZB), 0)
            fill(wv(t, ZB + 4 * A, 4 * HB), 0)
            fill(wv(t, 0, 128), 0)
        for name, lo, hi in (("ta", 480, 512), ("src", 240, 304), ("mb", 432, 512), ("vb", 64, 80), ("t1", 288, 400)):
            fill(v(name, lo, hi), 0)
        fill(v("seg1", 0, 320), 1)
        fill(v("seg1", 320, 640), 1)
        keep(v("ey"), v("seg1", 0, 516), [[1, 516]], Op.is_equal, 0.0, -3, -4)
        keep(v("seg2"), v("seg1", 0, 424), [[0, 4], [1, 106]], Op.is_ge, -1.0, -10, 0)
        keep(v("g4"), v("seg1", 0, 128), [[-1, 128]], Op.is_ge, 0.0, K - 1, 0)
        fill(v("seg2", 0, 424, 108), 0)
        fill(v("dk"), 0)
        fill(v("ys", 0, 1), 0)
        iota(v("ir", 16, 96), [[0, 5], [1, 16]])
        ts(v("dm"), v("ir"), RF, Op.is_equal, 2.0 ** 90 + SC, Op.mult)
        aff(v("dm"), v("dm"), 1.0, -2.0 ** 90)
        keep(v("sk"), wv(2, 0, 96), [[0, 6], [1, 16]], Op.not_equal, -2.0 ** 96, 0, 0)
        for b in range(4):
            quant(v("eq", 128 * b, 128 * b + 128), v("ep", 128 * b, 128 * b + 128), v("ey", 3 - b, 515 - b))
        const(v("sg3"), 0.0)
        const(v("sg3", 0, P, 3), 2.0 ** 95)
        const(v("gb", 225, 226), -2.0 ** 95)
        ramp(v("g3", 0, 32), -1, 0)
        fill(v("g3", 32, 128), 64)
        fill(v("seg1", 0, 128 * (8 - min(NS)), 128), 0)
        aff(v("cu"), v("ir", 0, 4), 2.0 / 3, 128 + 1.0 / 6)
        fill(v("uu", 0, 192, 2), 0)
        iota(v("yk", 0, 80), [[0, 5], [1, 16]])
        iota(v("yk", 80, 96), [[1, 16]], 1)
        act(v("yk"), v("yk"), Fn.Sign, -1.0, R1)
        aff(v("uu", 1, 192, 2), v("yk"), -0.5, -0.5)

    def sides():
        quant(v("uq"), v("up"), v("us"))
        op("V", V.tensor_copy, [w32(v("uq2"))], [ind(w32(v("uq")), PKU)])
        move(v("up2"), ind(v("up"), PKU))

    def tables():
        cp(v("tgu"), v("tgi"))
        cp(v("adu"), v("adi"))
        scat(AT, v("tgu"), v("st", 32, 416))
        aff(v("tr"), ind(v("iot"), v("tgu")), S1, B1)
        spread("tr", v("st", 32, 416), [(T.st[r:128:16, 32:416], T.tr[r:128:16, :]) for r in (11, 8, 0, 1, 2, 3)], v("tr")[1])

    def lookup(t):
        act(v("mis"), ind(AT, v("adu", 14 * t, 14 * t + 14)), Fn.Relu, MS, MB)
        src, lz = v("src", 16, 240), v("lz", 64 * t, 64 * t + 64)
        scan(src, v("k8"), v("mis"), I0, Op.mult, Op.add)
        turn("ta", "src", 16, A)
        ta = v("ta")
        tt(v("alt"), v("ta", 9, 496, 16), v("ta", 10, 496, 16), Op.min)
        ts(v("lb", 16 * t, 16 * t + 16), ind(v("alt"), PKQ), US, Op.mult)
        scat(v(E[t]), v("lb", 16 * t, 16 * t + 14), src)
        if t < 2:
            ts(lz, ind(ta, PKZ), US, Op.mult, float(4 * ZC), Op.min)
            return
        aff(v("tc", 0, 64), ind(ta, PKC), 16384.0, -447.5 * 16384 * SC)
        tt(v("tc", 0, 64), v("tc", 0, 64), v("dj"), Op.max)
        tt(v("tc", 64, 128), ind(ta, PKZ), v("tc", 0, 64), Op.min)
        ts(lz, v("tc", 64, 128), US, Op.mult)

    def served(t):
        turn("tk", E[t], 416, 32)
        if t < 2:
            ts(v("sa%d" % t), ind(v("tk"), PK2), US, Op.mult, THR - OFF, Op.add)
            mine = send(owner, "a_rq%d" % t, v("rq%d" % t), v("sa%d" % t, 0, 8), opened)
            arrives(asker, "a_rq%d" % t, [v("rq%d" % t)], [mine] + chain[-1:])
            aff(v("ex", 32 * t, 32 * t + 32), v(E[t], 416, 448), E2S, 0.0)
        ts(v("lk", 32 * t + 16, 32 * t + 32), ind(v("tk", 8, 96), PK2), US, Op.mult, THR, Op.add)

    def places(t):
        to = v("tp", 96 * t, 96 * t + 96)
        spread("p%d" % t, to, [(T.tp[b:128:4, 96 * t:96 * t + 96], T[E[t]][12:128:16, 32:416]) for b in range(4)], v(E[t], 32, 416)[1])
        ts(v("le", 96 * t, 96 * t + 96), to, US, Op.mult, B4T, Op.add)

    def answer(t):
        mem = v("ms", 0, 4 * MC)
        eb = lambda b: (v("eq", 128 * b, 128 * b + 128), v("ep", 128 * b, 128 * b + 128))
        if t == 2:
            spread("r2", v("r2"), [(T.r2[b:128:4, :], T.rq2[:, :]) for b in range(4)], v("rq2")[1])
            ts(v("f2l"), v("r2"), 4.0, Op.mult, B4, Op.add)
            for i in range(2):
                move(v("ft", 448 * i, 448 * i + 448), ind(mem, v("f2l", 28 * i, 28 * i + 28)))
            quant(v("fq2"), v("fp2"), v("ft"))
            lc, lp = v("lc"), v("lp")
            mine = [send(asker, "a_f2", b8(lc), b8(v("fq2"))), send(asker, "a_f2", lp, v("fp2"))]
            arrives(owner, "a_f2", [lc, lp], mine)
            for b in range(4):
                bank = 512 * (4 + b % 3)
                mm(v("ps", bank, bank + A), *eb(b), lc, lp)
                move(wv(2, ZB + b, ZB + 4 * A, 4), v("ps", bank, bank + A))
            return
        lo, at = 4 * (MC + K * t), LAND[t]
        for b in range(4):
            move(v("ms", lo + b, lo + 4 * K, 4), ind(mem, v("rq%d" % t, 2 * b, 2 * b + 2)))
        quant(v("fq", at - 128, at), v("fp", at - 128, at), v("ms", lo + 4 * K - 512, lo + 4 * K))
        lc, lp = v("fq", at, at + K), v("fp", at, at + K)
        mine = [send(asker, "a_f%d" % t, b8(lc), b8(v("fq", at - K, at))), send(asker, "a_f%d" % t, lp, v("fp", at - K, at))]
        arrives(owner, "a_f%d" % t, [lc, lp], mine)
        for b in (1, 0, 3, 2):
            w, bank = 128 + K * (b % 2), 2048 + 512 * (b // 2)
            mm(v("ps", bank, bank + w), *eb(b), v("fq", at + K - w, at + K), v("fp", at + K - w, at + K))
            if b % 2 == 0:
                move(v("fd", 128 * t + K * b, 128 * t + K * b + 64), v("ps", bank + 96, bank + 160))

    def layer(t):
        zv = (lambda lo, hi, st=1: wv(t, ZB + lo, ZB + hi, st)) if t < 2 else (lambda lo, hi, st=1: v("z2", lo, hi, st))
        win = wv(t, 0, ZB if t < 2 else 4 * HB)
        for i in range(4):
            move(zv(i, 4 * A, 4), ind(win, v("lz", 64 * t + 16 * i, 64 * t + 16 * i + 14)))
        zq, zp = v("zq", A * t, A * t + A), v("zp", A * t, A * t + A)
        if t < 2:
            scat(v(W[t], 0, PAD + ZB + 4 * A), v("lk", 32 * t + 24, 32 * t + 32), v("fd", 128 * t, 128 * t + 128))
        quant(zq, zp, zv(0, 4 * A))
        for b in range(4):
            mm(v("ps", 512 * b, 512 * b + A), v("wq", 128 * b, 128 * b + 128), v("wp", 128 * b, 128 * b + 128), zq, zp)
        for b in range(4):
            relu(wv(t, 4 * HB + b, 4 * (HB + A), 4), v("ps", 512 * b, 512 * b + A), 0.03125)

    def write(t):
        hs = v("hs", 128 * t, 128 * t + 128)
        move(hs, ind(wv(t), v("lk", 32 * t + 24, 32 * t + 32)))
        w = 96 // WR[t]
        for i in range(WR[t]):
            move(wv(t + 1, 128 + 16 * w * i, 128 + 16 * w * (i + 1)), ind(wv(t), v("le", 96 * t + w * i, 96 * t + w * (i + 1))))
        scat(wv(t + 1, 0, 1664), v("lk", 32 * t, 32 * t + 8), hs)

    def marks(t):
        quant(v("xq"), v("xp"), wv(t, 128, 1664))
        mm(v("ps", 3584, 3584 + P), v("uq2"), v("up2"), v("xq"), v("xp"))

    rw = lambda k: v("rw", 128 * k, 128 * k + 128)
    sm = lambda k: v("sm", k, k + 1)

    def blocks(t):
        mins = v("mb", 50, 432, 3)
        for q in range(4):
            tt(v("kk", q, P, 4), v("ps", 3584 + q, 3584 + P, 4), v(E[t], 32 + 96 * q, 128 + 96 * q), Op.max)
        scan(v("mb", 48, 432), v("sg3"), v("kk"), 0.0, Op.add, Op.min)
        op("V", V.transpose, [v("t1", 0, 128)], [mins])
        op("V", V.transpose, [v("t1", 128, 288)], [v("mb", 2, 480, 3)])
        move(v("ky"), ind(v("t1"), PK8))
        nv = 8 - NS[t]
        cut = lambda name, c: v(name, 128 * c, 128 * c + 128)
        for c in range(nv, 8):
            act(cut("jn1", c), mins, Fn.Sign, -1.0, v("ky", c, c + 1))
            act(cut("jn2", c), cut("jn1", c), Fn.Relu, 1.0, 0.0, v("cn", c, c + 1))
        for c in range(nv):
            ts(cut("jn1", c), mins, v("ky", c, c + 1), Op.is_lt)
        scan(v("jn2", 0, 128 * nv), v("seg1", 0, 128 * nv), v("jn1", 0, 128 * nv), 0.0, Op.mult, Op.add)
        ts(v("lt", 0, nv), v("jn2", 127, 128 * nv, 128), 127.0, Op.min)
        ts(v("lt", nv, 8), v("cn", nv, 8), 127.0, Op.min)
        move(rw(0), ind(v("g3"), v("lt")))
        low = v("rw", 383, 384)
        scan(rw(2), rw(0), rw(0), 0.0, Op.min, Op.min)
        either(lambda: ts(rw(3), rw(0), 0.0, Op.is_le), lambda: act(rw(3), ind(v("g4"), v("lt")), Fn.Copy))
        ts(rw(4), rw(0), low, Op.is_equal)
        scan(rw(5), rw(3), rw(4), low, Op.add, Op.subtract)
        scan(rw(1), rw(3), rw(5), -32.0, Op.add, Op.min)
        act(rw(6), rw(1), Fn.Sign, 1.0, K0, sm(2))
        act(rw(7), rw(1), Fn.Sign, 1.0, K1, sm(3))

    def victims(t):
        for i in range(2):
            ts(v("o6", 3 * i, 3 * i + 3), v("cu", 0, 3), sm(2 + i), Op.subtract, 1.5, Op.mult)
        ts(v("cb", 33, 225, 2), ind(v("kk"), v("o6", 0, 6)), SC, Op.min)
        act(v("cb", 32, 224, 2), v("cb", 33, 225, 2), Fn.Abs, 1.25 * 2.0 ** -24, 2.0 ** -124)
        tt(v("yk"), ind(v("kk"), v("o6", 0, 6)), v("dm"), Op.min)
        scan(v("ys", 1, 97), v("sk"), v("yk"), 0.0, Op.add, Op.max)
        act(v("dk", 6, 16, 2), v("ys", 16, 81, 16), Fn.Abs, 1.25 * 2.0 ** -24, 2.0 ** -124)
        move(v("cp"), ind(v("st", 32, 416), v("o6", 0, 6)))
        scan(v("gb", 32, 224), v("uu"), v("cb", 32, 224), 0.0, Op.mult, Op.add)
        tt(v("gb", 1, 33, 2), ind(v("ys", 0, 97), PK6), v("dk"), Op.subtract)
        nv = 6 - NK[t]
        for c in range(nv):
            ts(v("c1", 106 * c, 106 * c + 106), v("gb", 13, 224, 2), v("ys", 16 + 16 * c, 17 + 16 * c), Op.is_lt)
        for c in range(nv, 6):
            w, lo = 92 + c, 128 * c
            act(v("jn1", lo, lo + w), v("gb", 33, 33 + 2 * w - 1, 2), Fn.Sign, -1.0, v("ys", 16 + 16 * c, 17 + 16 * c))
            act(v("jn2", lo, lo + w), v("jn1", lo, lo + w), Fn.Relu, 1.0, 0.0, sm(c))
        ts(v("rk", nv, 6), v("sm", nv, 6), -1.0, Op.add)
        scan(v("s1", 0, 106 * nv), v("seg2", 0, 106 * nv), v("c1", 0, 106 * nv), 0.0, Op.mult, Op.add)
        cp(v("rk", 0, nv), v("s1", 105, 106 * nv, 106))
        scat(v("sv"), v("rk", 0, 6), v("cp"))
        tt(v("vb", 32, 64), v("sv", 0, 32), v("ex", 32 * t, 32 * t + 32) if t < 2 else v(E[t], 416, 448), Op.min)
        if t < 2:
            relu(v("vb", 0, 32), v("sv", 0, 32))
        turn("tv", "vb", 32, 32, 4)
        ts(v("lk", 32 * t, 32 * t + 16), ind(v("tv", 8, 100), PK2), US, Op.mult, THR, Op.add)

    def retag(t):
        cols = v("lk", 32 * t + 10, 32 * t + 12)
        if t < 2:
            scat(v("at"), v("lk", 32 * t + 14, 32 * t + 18), v("vb", 0, 64))
            aff(v("sh"), v("sv", 0, 32), SH, 0.0)
            tt(v("mx"), v("sh"), v(E[t], 416, 448), Op.min)
            scat(v("st"), cols, v("mx"))
            return
        aff(v("otb", 32, 416), v("st", 32, 416), US, THR - OFF)
        aff(v("sh"), v(E[t], 416, 448), US, THR - OFF)
        scat(v("otb"), cols, v("sh"))

    def last():
        w = P // YP
        for i in range(YP):
            lo = w * i
            q_, p_, bank, yb = v("xq", lo, lo + w), v("xp", lo, lo + w), 3584 - 512 * i, v("yb", lo, lo + w)
            quant(q_, p_, wv(3, 128 + 4 * lo, 128 + 4 * (lo + w)))
            mm(v("ps", bank, bank + w), v("vq"), v("vp"), q_, p_)
            move(yb, v("ps", bank, bank + w))
            dma("Y" if i % 2 else "S", "oz" if i % 2 else "oy", T.y[:, lo:lo + w], yb[0], rd=yb[1])
            dma("S" if i else "Y", "oc", T.oc[:, 4 * lo:4 * (lo + w)], b8(q_)[0], rd=q_[1])

    def store():
        for k in range(4):
            dma("Y", "os", T.osc[4 * k:4 * k + 4, :], T.xp[32 * k:32 * k + 4, :], rd=v("xp")[1])
        dma("Y", "ot", T.ot[:], T.otb[11:128:16, 32:416], rd=v("otb")[1])

    def late(t):
        if t == 0:
            came = v("rq0")[1]
            dma("Y", "ws", v("wp")[0], T.ws[:], wr=v("wp")[1], rd=came)
            for i, name in enumerate(("wc", "wd")):
                half = v("wq", 256 * i, 256 * i + 256)
                dma("Y", name, b8(half)[0], T.wc[:, 1024 * i:1024 * i + 1024], wr=half[1], rd=came)
        if t == 1:
            dma("Y", "v", v("vs")[0], T.v[:], wr=v("vs")[1], rd=v("fd", 0, 128)[1])
            quant(v("vq"), v("vp"), v("vs"))

    def do(name, f, *a):
        stage[0] = name + "".join(str(x) for x in a)
        f(*a)

    load("Y", "tg", v("tgi"), T.tg[:])
    load("S", "ad", v("adi"), T.ad[:])
    load("Y", "x", wv(0, 128, 1664), T.x[:])
    load("Y", "u", v("us"), T.u[:])
    load("Y", "m", v("ms", 0, 4 * MC), T.m[:])
    do("con", constants)
    stage[0] = "rq2"
    opened = send(owner, "a_rq2", v("rq2"), v("adi", 28, 42))
    arrives(asker, "a_rq2", [v("rq2")], [opened] + chain[-1:])
    do("sid", sides)
    do("tbl", tables)
    for t in range(3):
        for name, f in (("loo", lookup), ("ser", served), ("pla", places), ("ans", answer), ("lat", late),
                        ("mar", marks), ("blo", blocks), ("vic", victims), ("lay", layer), ("wri", write), ("ret", retag)):
            do(name, f, t)
    do("mar3", last)
    do("sto", store)
    PLAN["nodes"] = nodes

    waited, count, mark, total = {}, {}, {}, {}
    for nd in nodes:
        if nd["kind"].startswith("d_"):
            total[nd["kind"]] = total.get(nd["kind"], 0) + 16

    def wait(q, sem, val):
        if waited.get((q, sem), 0) < val:
            Q[q].wait_ge(T.sem[sem], val)
            waited[(q, sem)] = val

    for k in PLAN["order"] or range(len(nodes)):
        nd = nodes[k]
        q, kind = nd["q"], nd["kind"]
        if q == "R":
            count[kind] = nd["tag"]
            mark[k] = (kind, nd["tag"])
            continue
        need = {}
        for d in nd["deps"]:
            if d != nd["soft"]:
                sem, val = mark[d]
                need[sem] = max(need.get(sem, 0), val)
        for sem in sorted(need):
            wait(q, sem, need[sem])
        call = nd["run"]()
        if kind == "send":
            count["sent"] = count.get("sent", 0) + nd["tag"]
        elif kind == "op":
            count["c" + q] = count.get("c" + q, 0) + 1
            call.then_inc(T.sem["c" + q], 1)
            mark[k] = ("c" + q, count["c" + q])
        else:
            count[kind] = total[kind]
            call.then_inc(T.sem[kind], 16)
            mark[k] = (kind, total[kind])
    for sem in sorted(count):
        wait("G", sem, count[sem])
